import numpy as np
import ml_dtypes


def mxq(x, axis, fmt="e4m3"):
    dtype, down = {"e4m3": (ml_dtypes.float8_e4m3fn, 7), "e5m2": (ml_dtypes.float8_e5m2, 14)}[fmt]
    v = np.moveaxis(np.asarray(x, np.float32).astype(ml_dtypes.bfloat16).astype(np.float64), axis, -1)
    blocks = v.reshape(v.shape[:-1] + (-1, 32))
    amax = np.abs(blocks).max(-1, keepdims=True)
    byte = np.maximum(np.where(amax > 0, np.frexp(amax)[1] - 1 + 127, 0) - down, 1)
    scale = np.exp2(byte - 127.0)
    codes = (blocks / scale).astype(np.float32).astype(dtype).astype(np.float64)
    return np.moveaxis((codes * scale).reshape(v.shape), -1, axis)


WIDE = False


def mx_kscale(k):
    if not WIDE:
        return np.ones(k)
    levels = np.array([10, -10, 5, -5, 0])
    if k % 512:
        return np.exp2(np.random.permutation(np.resize(levels, k // 32))).repeat(32)
    a = np.empty((k // 512, 16))
    for p in range(k // 512):
        a[p, :8] = np.random.permutation(np.resize(levels, 8))
        for g in range(8):
            far = levels[np.abs(levels - a[p, g]) >= 10]
            a[p, g + 8] = far[np.random.randint(len(far))]
    return np.exp2(a.ravel()).repeat(32)


def f64(x):
    return np.asarray(x).astype(np.float64)


def striped(idx):
    return np.tile(idx.reshape(-1, 16).T, (8, 1)).astype(np.uint16)


def unstriped(offs):
    return offs[:16].T.reshape(-1).astype(np.int64)


E2M1 = np.array([0.0, 0.5, 1.0, 1.5, 2.0, 3.0, 4.0, 6.0, -0.0, -0.5, -1.0, -1.5, -2.0, -3.0, -4.0, -6.0])


def pack_weight(w, fmt):
    k, n = w.shape
    w = f64(np.asarray(w, np.float32).astype(ml_dtypes.bfloat16)).reshape(k // 32, 32, n)
    amax = np.abs(w).max(1)
    if fmt == "e4m3":
        byte = np.frexp(amax)[1] - 1 + 127 - 7
    else:
        mant, ex = np.frexp(amax / 6.0)
        byte = np.where(mant > 0.5, ex, ex - 1) + 127
    byte = np.clip(np.where(amax > 0, byte, 1), 1, 254)
    scaled = (w * np.exp2(127.0 - byte)[:, None, :]).reshape(k, n).astype(np.float32)
    by_word = np.ascontiguousarray(scaled.reshape(k // 512, 128, 4, n).transpose(0, 1, 3, 2))
    if fmt == "e4m3":
        words = by_word.astype(ml_dtypes.float8_e4m3fn).view(np.uint8)
    else:
        c = by_word.astype(ml_dtypes.float4_e2m1fn).view(np.uint8) & 0xF
        words = (c[..., 0::2] | (c[..., 1::2] << 4)).reshape(k // 512, 128, 2 * n)
    return np.ascontiguousarray(words), np.ascontiguousarray(byte.astype(np.uint8).reshape(k // 512, 16, n))


def unpack_weight(words, scales, fmt):
    g, _, n = scales.shape
    words = np.ascontiguousarray(words).reshape(g, 128, n, -1)
    if fmt == "e4m3":
        vals = words.view(ml_dtypes.float8_e4m3fn).astype(np.float64)
    else:
        nib = np.empty((g, 128, n, 4), np.uint8)
        nib[..., 0::2] = words & 0xF
        nib[..., 1::2] = words >> 4
        vals = E2M1[nib]
    vals = vals * np.repeat(np.exp2(scales.astype(np.float64) - 127.0), 8, axis=1)[..., None]
    return vals.transpose(0, 1, 3, 2).reshape(g * 512, n)


def silu(v):
    return v / (1.0 + np.exp(-np.maximum(v, -700.0)))


K, T, E, C, H, N = 512, 1024, 4, 128, 1024, 512
R = 4


def by_expert(wq, xq):
    return np.concatenate([wq[e].T @ xq[:, e * C:(e + 1) * C] for e in range(E)], axis=1)


def setup_inputs():
    n = np.random.standard_normal
    s = mx_kscale(K)[:, None]
    u = mx_kscale(H)
    slot_token = np.concatenate([r * (T // R) + np.random.permutation(T // R)[:C // R] for e in range(E) for r in range(R)])
    w1 = [pack_weight(m, "e2m1") for m in n((E, K, H)) / np.sqrt(K) / s[None]]
    w3 = [pack_weight(m, "e2m1") for m in n((E, K, H)) / np.sqrt(K) / s[None] * u[None, None, :]]
    w2 = [pack_weight(m, "e2m1") for m in n((E, H, N)) / np.sqrt(H) / u[None, :, None]]
    return {
        "xT": (n((K, T)) * s).astype(np.float32),
        "w1_words": np.stack([m[0] for m in w1]),
        "w1_scales": np.stack([m[1] for m in w1]),
        "w3_words": np.stack([m[0] for m in w3]),
        "w3_scales": np.stack([m[1] for m in w3]),
        "w2_words": np.stack([m[0] for m in w2]),
        "w2_scales": np.stack([m[1] for m in w2]),
        "offs": striped(slot_token),
    }


def reference(xT, w1_words, w1_scales, w3_words, w3_scales, w2_words, w2_scales, offs):
    idx = unstriped(offs)
    w1 = np.stack([unpack_weight(w1_words[e], w1_scales[e], "e2m1") for e in range(E)])
    w3 = np.stack([unpack_weight(w3_words[e], w3_scales[e], "e2m1") for e in range(E)])
    w2 = np.stack([unpack_weight(w2_words[e], w2_scales[e], "e2m1") for e in range(E)])
    xq = mxq(f64(xT)[:, idx], 0, "e4m3")
    h = silu(by_expert(w1, xq))
    h = h * by_expert(w3, xq)
    y = by_expert(w2, mxq(h, 0, "e4m3"))
    return y.reshape(N, E, R, C // R).transpose(0, 2, 1, 3).reshape(N, E * C)

@@ -1,0 +1,173 @@
+from contextlib import ExitStack
+
+import concourse.mybir as mybir
+from concourse.masks import make_identity
+
+K, T, E, C, H, N, R = 512, 1024, 4, 128, 1024, 512, 4
+FLOPS = 2 * E * C * (2 * K * H + H * N)
+
+F32 = mybir.dt.float32
+BF16 = mybir.dt.bfloat16
+I32 = mybir.dt.int32
+U32 = mybir.dt.uint32
+U16 = mybir.dt.uint16
+U8 = mybir.dt.uint8
+FP8X4 = mybir.dt.float8_e4m3fn_x4
+FP4X4 = mybir.dt.float4_e2m1fn_x4
+ACT = mybir.ActivationFunctionType
+MULT = mybir.AluOpType.mult
+
+P = 128
+PASS = 512
+HP = H // PASS
+NT = N // P
+U = C // R
+X_CHUNKS = ((0, 512, 320), (512, 256, 160), (768, 256, 160))
+
+
+def tile_moe_eps_glu_silu_kernel(tc, xT, w1_words, w1_scales, w3_words, w3_scales, w2_words, w2_scales, offs, out):
+    nc = tc.nc
+    with ExitStack() as ctx:
+        keep = ctx.enter_context(tc.tile_pool(name="keep", bufs=1))
+        ring = ctx.enter_context(tc.tile_pool(name="ring", bufs=2))
+        psum = ctx.enter_context(tc.psum_pool(name="psum", bufs=2))
+
+        offsets = keep.tile([P, E * C // 16], U16, name="offsets")
+        s1 = keep.tile([P, E, H], U8, name="s1", align_bytes=64)
+        s3 = keep.tile([P, E, H], U8, name="s3", align_bytes=64)
+        s2 = keep.tile([P, E * HP, N], U8, name="s2", align_bytes=64)
+        w1 = [keep.tile([P, 2 * H], U8, name="w1_%d" % e, align_bytes=64) for e in range(E)]
+        w3 = [keep.tile([P, 2 * H], U8, name="w3_%d" % e, align_bytes=64) for e in range(E)]
+        w2 = [keep.tile([P, HP, 2 * N], U8, name="w2_%d" % e, align_bytes=64) for e in range(E)]
+        x_raw = [keep.tile([P, 4, w], F32, name="x_raw%d" % t0) for t0, w, v in X_CHUNKS]
+        x_bf = [keep.tile([P, w, 4], BF16, name="x_bf%d" % t0, align_bytes=64) for t0, w, v in X_CHUNKS]
+        tok_codes = keep.tile([P, T], U32, name="tok_codes", align_bytes=64)
+        tok_scales = keep.tile([P, T], U8, name="tok_scales", align_bytes=64)
+        slot_codes = keep.tile([P, E * C], U32, name="slot_codes", align_bytes=64)
+        slot_scales = keep.tile([P, E * C], U8, name="slot_scales", align_bytes=64)
+        ident = keep.tile([P, P], F32, name="ident")
+        warm_in = keep.tile([P, 1], F32, name="warm_in")
+        warm_out = keep.tile([P, 1], F32, name="warm_out")
+        staged = keep.tile([P, NT, R, E, U], F32, name="staged")
+
+        nc.vector.memset(warm_in[:], 0.0)
+        nc.scalar.activation(warm_out[:], warm_in[:], ACT.Silu)
+        for plane in (s1, s3, s2):
+            nc.vector.memset(plane[:].rearrange("p a n -> p (a n)").bitcast(I32), 0)
+        nc.gpsimd.memset(tok_scales[:], 0)
+        make_identity(nc, ident[:])
+
+        def load_scales(plane, scales):
+            rows = scales.rearrange("e s (q r) n -> r q (e s) n", r=4)
+            for r in range(4):
+                nc.sync.dma_start(plane[r:P:32, :, :].bitcast(I32), rows[r].bitcast(I32))
+
+        def load_first(e):
+            nc.sync.dma_start(w1[e][:].bitcast(I32), w1_words[e, 0].bitcast(I32))
+            nc.sync.dma_start(w3[e][:].bitcast(I32), w3_words[e, 0].bitcast(I32))
+
+        def load_second(e):
+            nc.sync.dma_start(w2[e][:].bitcast(I32), w2_words[e].rearrange("s p n -> p s n").bitcast(I32))
+
+        nc.sync.dma_start(offsets[:], offs)
+        x_rows = xT.rearrange("(p j) t -> p j t", j=4)
+        for i, (t0, w, v) in enumerate(X_CHUNKS):
+            nc.sync.dma_start(x_raw[i][:], x_rows[:, :, t0 : t0 + w])
+        nc.sync.dma_start(w1[0][:].bitcast(I32), w1_words[0, 0].bitcast(I32))
+        load_scales(s1, w1_scales)
+        nc.sync.dma_start(w3[0][:].bitcast(I32), w3_words[0, 0].bitcast(I32))
+        load_scales(s3, w3_scales)
+        load_first(1)
+        load_second(0)
+        load_scales(s2, w2_scales)
+        load_first(2)
+        load_second(1)
+        load_first(3)
+        load_second(2)
+        load_second(3)
+
+        for i, (t0, w, v) in enumerate(X_CHUNKS):
+            src = x_raw[i][:].rearrange("p j (c i) -> p c j i", i=4)
+            dst = x_bf[i][:].rearrange("p (c i) j -> p c j i", i=4)
+            nc.vector.tensor_copy(dst[:, : v // 4], src[:, : v // 4])
+            nc.scalar.activation(dst[:, v // 4 :], src[:, v // 4 :], ACT.Copy)
+            nc.vector.quantize_mx(
+                out=tok_codes[:, t0 : t0 + w].bitcast(FP8X4),
+                scales=tok_scales[:, t0 : t0 + w],
+                in_=x_bf[i][:].rearrange("p t j -> p (t j)"),
+            )
+
+        for e in range(E):
+            cols = slice(e * C, (e + 1) * C)
+            picks = offsets[:, e * C // 16 : (e + 1) * C // 16]
+            nc.vector.tensor_copy(slot_codes[:, cols], tok_codes[:].indirect(picks))
+            nc.vector.tensor_copy(slot_scales[:, cols], tok_scales[:].indirect(picks))
+
+        for e in range(E):
+            cols = slice(e * C, (e + 1) * C)
+            last = e == E - 1
+            h_turned = ring.tile([P, HP, C, 2], F32, name="h_turned", align_bytes=64)
+            h_codes = ring.tile([P, HP, C], U32, name="h_codes", align_bytes=64)
+            h_scales = ring.tile([P, HP, C], U8, name="h_scales", align_bytes=64)
+            for s in range(HP):
+                a = psum.tile([P, PASS], F32, name="a")
+                b = psum.tile([P, PASS], F32, name="b")
+                for acc, words, plane in ((a, w1[e], s1), (b, w3[e], s3)):
+                    nc.tensor.matmul_mx(
+                        acc[:],
+                        lhsT=slot_codes[:, cols].bitcast(FP8X4),
+                        lhsT_scale=slot_scales[:, cols],
+                        rhs=words[:, 2 * PASS * s : 2 * PASS * (s + 1)].bitcast(FP4X4),
+                        rhs_scale=plane[:, e, PASS * s : PASS * (s + 1)],
+                        start=True,
+                        stop=True,
+                    )
+                gate = ring.tile([P, 2, P, 2], F32, name="gate")
+                nc.scalar.activation(gate[:], a[:].rearrange("p (q u c) -> p u q c", u=2, c=2), ACT.Silu)
+                h = ring.tile([P, 2, P, 2], BF16, name="h")
+                nc.vector.tensor_tensor(h[:], b[:].rearrange("p (q u c) -> p u q c", u=2, c=2), gate[:], MULT)
+                pairs = h[:].rearrange("p u q c -> p (u q c)").bitcast(F32)
+                turned = psum.tile([P, 2, C], F32, name="turned")
+                for u in range(2):
+                    nc.tensor.transpose(turned[:, u, :], pairs[:, u * P : (u + 1) * P], ident[:])
+                nc.scalar.copy(h_turned[:, s], turned[:].rearrange("p u c -> p c u"))
+                if last:
+                    nc.vector.quantize_mx(
+                        out=h_codes[:, s].bitcast(FP8X4),
+                        scales=h_scales[:, s],
+                        in_=h_turned[:, s].rearrange("p c u -> p (c u)").bitcast(BF16),
+                    )
+            if not last:
+                nc.vector.quantize_mx(
+                    out=h_codes[:].rearrange("p s c -> p (s c)").bitcast(FP8X4),
+                    scales=h_scales[:].rearrange("p s c -> p (s c)"),
+                    in_=h_turned[:].rearrange("p s c u -> p (s c u)").bitcast(BF16),
+                )
+
+            def second(acc, j):
+                for s in range(HP):
+                    nc.tensor.matmul_mx(
+                        acc,
+                        lhsT=w2[e][:, s, 2 * P * j : 2 * P * (j + 1)].bitcast(FP4X4),
+                        lhsT_scale=s2[:, e * HP + s, P * j : P * (j + 1)],
+                        rhs=h_codes[:, s].bitcast(FP8X4),
+                        rhs_scale=h_scales[:, s],
+                        start=(s == 0),
+                        stop=(s == HP - 1),
+                    )
+
+            if not last:
+                y = psum.tile([P, NT, C], F32, name="y")
+                for j in range(NT):
+                    second(y[:, j, :], j)
+                nc.vector.tensor_copy(staged[:, :, :, e, :], y[:].rearrange("p j (m u) -> p j m u", u=U))
+            else:
+                for j in range(NT):
+                    y = psum.tile([P, C], F32, name=("y", "a", "b", "y")[j])
+                    second(y[:], j)
+                    view = y[:].rearrange("p (m u) -> p m u", u=U)
+                    if j % 2 == 0:
+                        nc.vector.tensor_copy(staged[:, j, :, e, :], view)
+                    else:
+                        nc.scalar.copy(staged[:, j, :, e, :], view)
+                    nc.sync.dma_start(out[P * j : P * (j + 1), :], staged[:, j].rearrange("p m e u -> p (m e u)"))

@@ -22,152 +22,204 @@ PASS = 512
 HP = H // PASS
 NT = N // P
 U = C // R
-X_CHUNKS = ((0, 512, 320), (512, 256, 160), (768, 256, 160))
 
 
 def tile_moe_eps_glu_silu_kernel(tc, xT, w1_words, w1_scales, w3_words, w3_scales, w2_words, w2_scales, offs, out):
     nc = tc.nc
     with ExitStack() as ctx:
         keep = ctx.enter_context(tc.tile_pool(name="keep", bufs=1))
-        ring = ctx.enter_context(tc.tile_pool(name="ring", bufs=2))
-        psum = ctx.enter_context(tc.psum_pool(name="psum", bufs=2))
+        psum = ctx.enter_context(tc.psum_pool(name="psum", bufs=1))
 
         offsets = keep.tile([P, E * C // 16], U16, name="offsets")
-        s1 = keep.tile([P, E, H], U8, name="s1", align_bytes=64)
-        s3 = keep.tile([P, E, H], U8, name="s3", align_bytes=64)
+        s1 = [keep.tile([P, 2, H], U8, name="s1_%d" % g, align_bytes=64) for g in range(2)]
+        s3 = [keep.tile([P, 2, H], U8, name="s3_%d" % g, align_bytes=64) for g in range(2)]
         s2 = keep.tile([P, E * HP, N], U8, name="s2", align_bytes=64)
-        w1 = [keep.tile([P, 2 * H], U8, name="w1_%d" % e, align_bytes=64) for e in range(E)]
-        w3 = [keep.tile([P, 2 * H], U8, name="w3_%d" % e, align_bytes=64) for e in range(E)]
-        w2 = [keep.tile([P, HP, 2 * N], U8, name="w2_%d" % e, align_bytes=64) for e in range(E)]
-        x_raw = [keep.tile([P, 4, w], F32, name="x_raw%d" % t0) for t0, w, v in X_CHUNKS]
-        x_bf = [keep.tile([P, w, 4], BF16, name="x_bf%d" % t0, align_bytes=64) for t0, w, v in X_CHUNKS]
-        tok_codes = keep.tile([P, T], U32, name="tok_codes", align_bytes=64)
-        tok_scales = keep.tile([P, T], U8, name="tok_scales", align_bytes=64)
+        w13 = keep.tile([P, 2, E, 2 * H], U8, name="w13", align_bytes=64)
+        w2 = keep.tile([P, E, HP, 2 * N], U8, name="w2", align_bytes=64)
+        x_row = [keep.tile([P, T], F32, name="x_row%d" % j) for j in range(4)]
+        picked = keep.tile([P, 4, E * C], F32, name="picked")
+        slot_bf = keep.tile([P, E * C, 4], BF16, name="slot_bf", align_bytes=64)
         slot_codes = keep.tile([P, E * C], U32, name="slot_codes", align_bytes=64)
         slot_scales = keep.tile([P, E * C], U8, name="slot_scales", align_bytes=64)
+        gate = keep.tile([P, E, HP, 2, P, 2], F32, name="gate")
+        h = keep.tile([P, E, HP, 2, P, 2], BF16, name="h")
+        h_turned = keep.tile([P, E, HP, C, 2], F32, name="h_turned", align_bytes=64)
+        h_codes = keep.tile([P, E, HP, C], U32, name="h_codes", align_bytes=64)
+        h_scales = keep.tile([P, E, HP, C], U8, name="h_scales", align_bytes=64)
         ident = keep.tile([P, P], F32, name="ident")
         warm_in = keep.tile([P, 1], F32, name="warm_in")
         warm_out = keep.tile([P, 1], F32, name="warm_out")
         staged = keep.tile([P, NT, R, E, U], F32, name="staged")
+        bank = [psum.tile([P, PASS], F32, name="bank%d" % i) for i in range(8)]
 
         nc.vector.memset(warm_in[:], 0.0)
         nc.scalar.activation(warm_out[:], warm_in[:], ACT.Silu)
-        for plane in (s1, s3, s2):
-            nc.vector.memset(plane[:].rearrange("p a n -> p (a n)").bitcast(I32), 0)
-        nc.gpsimd.memset(tok_scales[:], 0)
+        nc.vector.memset(s1[0][:].rearrange("p e b -> p (e b)").bitcast(I32), 0)
+        nc.vector.memset(w13[:].rearrange("p m e b -> p (m e) b").bitcast(I32)[:, :, :2], 0)
+        for plane in (s3[0], s1[1], s3[1]):
+            nc.vector.memset(plane[:].rearrange("p e b -> p (e b)").bitcast(I32), 0)
+        nc.vector.memset(s2[:].rearrange("p a b -> p (a b)").bitcast(I32), 0)
+        nc.vector.memset(w2[:].rearrange("p e s b -> p e (s b)").bitcast(I32)[:, :, :2], 0)
         make_identity(nc, ident[:])
 
-        def load_scales(plane, scales):
+        def load_scales(plane, scales, lo, hi):
             rows = scales.rearrange("e s (q r) n -> r q (e s) n", r=4)
             for r in range(4):
-                nc.sync.dma_start(plane[r:P:32, :, :].bitcast(I32), rows[r].bitcast(I32))
+                nc.sync.dma_start(plane[r:P:32].bitcast(I32), rows[r][:, lo:hi, :].bitcast(I32))
 
         def load_first(e):
-            nc.sync.dma_start(w1[e][:].bitcast(I32), w1_words[e, 0].bitcast(I32))
-            nc.sync.dma_start(w3[e][:].bitcast(I32), w3_words[e, 0].bitcast(I32))
+            nc.sync.dma_start(w13[:, 0, e].bitcast(I32), w1_words[e, 0].bitcast(I32))
+            nc.sync.dma_start(w13[:, 1, e].bitcast(I32), w3_words[e, 0].bitcast(I32))
 
         def load_second(e):
-            nc.sync.dma_start(w2[e][:].bitcast(I32), w2_words[e].rearrange("s p n -> p s n").bitcast(I32))
+            nc.sync.dma_start(w2[:, e].bitcast(I32), w2_words[e].rearrange("s p n -> p s n").bitcast(I32))
 
         nc.sync.dma_start(offsets[:], offs)
-        x_rows = xT.rearrange("(p j) t -> p j t", j=4)
-        for i, (t0, w, v) in enumerate(X_CHUNKS):
-            nc.sync.dma_start(x_raw[i][:], x_rows[:, :, t0 : t0 + w])
-        nc.sync.dma_start(w1[0][:].bitcast(I32), w1_words[0, 0].bitcast(I32))
-        load_scales(s1, w1_scales)
-        nc.sync.dma_start(w3[0][:].bitcast(I32), w3_words[0, 0].bitcast(I32))
-        load_scales(s3, w3_scales)
+        x_rows = xT.rearrange("(p j) t -> j p t", j=4)
+        for j in range(4):
+            nc.sync.dma_start(x_row[j][:], x_rows[j])
+        load_scales(s1[0], w1_scales, 0, 2)
+        load_first(0)
+        load_scales(s3[0], w3_scales, 0, 2)
         load_first(1)
-        load_second(0)
-        load_scales(s2, w2_scales)
+        load_scales(s1[1], w1_scales, 2, E)
+        load_scales(s3[1], w3_scales, 2, E)
         load_first(2)
-        load_second(1)
         load_first(3)
+        load_second(0)
+        load_scales(s2, w2_scales, 0, E * HP)
+        load_second(1)
         load_second(2)
         load_second(3)
 
-        for i, (t0, w, v) in enumerate(X_CHUNKS):
-            src = x_raw[i][:].rearrange("p j (c i) -> p c j i", i=4)
-            dst = x_bf[i][:].rearrange("p (c i) j -> p c j i", i=4)
-            nc.vector.tensor_copy(dst[:, : v // 4], src[:, : v // 4])
-            nc.scalar.activation(dst[:, v // 4 :], src[:, v // 4 :], ACT.Copy)
+        def gather(j, lo, hi):
+            nc.vector.tensor_copy(picked[:, j, lo * C : hi * C], x_row[j][:].indirect(offsets[:, lo * C // 16 : hi * C // 16]))
+
+        def interleave(e, on_scalar):
+            src = picked[:, :, e * C : (e + 1) * C].rearrange("p j (c i) -> p c j i", i=4)
+            dst = slot_bf[:, e * C : (e + 1) * C, :].rearrange("p (c i) j -> p c j i", i=4)
+            if on_scalar:
+                nc.scalar.activation(dst, src, ACT.Copy)
+            else:
+                nc.vector.tensor_copy(dst, src)
+
+        def quantize_slots(e):
             nc.vector.quantize_mx(
-                out=tok_codes[:, t0 : t0 + w].bitcast(FP8X4),
-                scales=tok_scales[:, t0 : t0 + w],
-                in_=x_bf[i][:].rearrange("p t j -> p (t j)"),
+                out=slot_codes[:, e * C : (e + 1) * C].bitcast(FP8X4),
+                scales=slot_scales[:, e * C : (e + 1) * C],
+                in_=slot_bf[:, e * C : (e + 1) * C, :].rearrange("p t j -> p (t j)"),
             )
 
-        for e in range(E):
+        def first(e, s, a, b):
             cols = slice(e * C, (e + 1) * C)
-            picks = offsets[:, e * C // 16 : (e + 1) * C // 16]
-            nc.vector.tensor_copy(slot_codes[:, cols], tok_codes[:].indirect(picks))
-            nc.vector.tensor_copy(slot_scales[:, cols], tok_scales[:].indirect(picks))
-
-        for e in range(E):
-            cols = slice(e * C, (e + 1) * C)
-            last = e == E - 1
-            h_turned = ring.tile([P, HP, C, 2], F32, name="h_turned", align_bytes=64)
-            h_codes = ring.tile([P, HP, C], U32, name="h_codes", align_bytes=64)
-            h_scales = ring.tile([P, HP, C], U8, name="h_scales", align_bytes=64)
-            for s in range(HP):
-                a = psum.tile([P, PASS], F32, name="a")
-                b = psum.tile([P, PASS], F32, name="b")
-                for acc, words, plane in ((a, w1[e], s1), (b, w3[e], s3)):
-                    nc.tensor.matmul_mx(
-                        acc[:],
-                        lhsT=slot_codes[:, cols].bitcast(FP8X4),
-                        lhsT_scale=slot_scales[:, cols],
-                        rhs=words[:, 2 * PASS * s : 2 * PASS * (s + 1)].bitcast(FP4X4),
-                        rhs_scale=plane[:, e, PASS * s : PASS * (s + 1)],
-                        start=True,
-                        stop=True,
-                    )
-                gate = ring.tile([P, 2, P, 2], F32, name="gate")
-                nc.scalar.activation(gate[:], a[:].rearrange("p (q u c) -> p u q c", u=2, c=2), ACT.Silu)
-                h = ring.tile([P, 2, P, 2], BF16, name="h")
-                nc.vector.tensor_tensor(h[:], b[:].rearrange("p (q u c) -> p u q c", u=2, c=2), gate[:], MULT)
-                pairs = h[:].rearrange("p u q c -> p (u q c)").bitcast(F32)
-                turned = psum.tile([P, 2, C], F32, name="turned")
-                for u in range(2):
-                    nc.tensor.transpose(turned[:, u, :], pairs[:, u * P : (u + 1) * P], ident[:])
-                nc.scalar.copy(h_turned[:, s], turned[:].rearrange("p u c -> p c u"))
-                if last:
-                    nc.vector.quantize_mx(
-                        out=h_codes[:, s].bitcast(FP8X4),
-                        scales=h_scales[:, s],
-                        in_=h_turned[:, s].rearrange("p c u -> p (c u)").bitcast(BF16),
-                    )
-            if not last:
-                nc.vector.quantize_mx(
-                    out=h_codes[:].rearrange("p s c -> p (s c)").bitcast(FP8X4),
-                    scales=h_scales[:].rearrange("p s c -> p (s c)"),
-                    in_=h_turned[:].rearrange("p s c u -> p (s c u)").bitcast(BF16),
+            for acc, words, plane in ((a, w13[:, 0, e], s1), (b, w13[:, 1, e], s3)):
+                nc.tensor.matmul_mx(
+                    acc[:],
+                    lhsT=slot_codes[:, cols].bitcast(FP8X4),
+                    lhsT_scale=slot_scales[:, cols],
+                    rhs=words[:, 2 * PASS * s : 2 * PASS * (s + 1)].bitcast(FP4X4),
+                    rhs_scale=plane[e // 2][:, e % 2, PASS * s : PASS * (s + 1)],
+                    start=True,
+                    stop=True,
                 )
 
-            def second(acc, j):
-                for s in range(HP):
-                    nc.tensor.matmul_mx(
-                        acc,
-                        lhsT=w2[e][:, s, 2 * P * j : 2 * P * (j + 1)].bitcast(FP4X4),
-                        lhsT_scale=s2[:, e * HP + s, P * j : P * (j + 1)],
-                        rhs=h_codes[:, s].bitcast(FP8X4),
-                        rhs_scale=h_scales[:, s],
-                        start=(s == 0),
-                        stop=(s == HP - 1),
-                    )
+        def glu(e, s, a, b, u0, u1):
+            a_view = a[:].rearrange("p (q u c) -> p u q c", u=2, c=2)
+            b_view = b[:].rearrange("p (q u c) -> p u q c", u=2, c=2)
+            nc.scalar.activation(gate[:, e, s, u0:u1], a_view[:, u0:u1], ACT.Silu)
+            nc.vector.tensor_tensor(h[:, e, s, u0:u1], b_view[:, u0:u1], gate[:, e, s, u0:u1], MULT)
 
-            if not last:
-                y = psum.tile([P, NT, C], F32, name="y")
-                for j in range(NT):
-                    second(y[:, j, :], j)
-                nc.vector.tensor_copy(staged[:, :, :, e, :], y[:].rearrange("p j (m u) -> p j m u", u=U))
+        def turn(e, s, u, into):
+            pairs = h[:, e, s, u].rearrange("p q c -> p (q c)").bitcast(F32)
+            nc.tensor.transpose(into[:, (2 * s + u) * C : (2 * s + u + 1) * C], pairs, ident[:])
+
+        def requantize(e, lo, hi, source):
+            view = source[:].rearrange("p (s u c) -> p s c u", s=HP, u=2)
+            nc.scalar.copy(h_turned[:, e, lo:hi], view[:, lo:hi])
+            nc.vector.quantize_mx(
+                out=h_codes[:, e, lo:hi].rearrange("p s c -> p (s c)").bitcast(FP8X4),
+                scales=h_scales[:, e, lo:hi].rearrange("p s c -> p (s c)"),
+                in_=h_turned[:, e, lo:hi].rearrange("p s c u -> p (s c u)").bitcast(BF16),
+            )
+
+        def second(acc, e, j, s):
+            nc.tensor.matmul_mx(
+                acc,
+                lhsT=w2[:, e, s, 2 * P * j : 2 * P * (j + 1)].bitcast(FP4X4),
+                lhsT_scale=s2[:, e * HP + s, P * j : P * (j + 1)],
+                rhs=h_codes[:, e, s].bitcast(FP8X4),
+                rhs_scale=h_scales[:, e, s],
+                start=(s == 0),
+                stop=(s == HP - 1),
+            )
+
+        def copy_on(on_scalar, dst, src):
+            if on_scalar:
+                nc.scalar.copy(dst, src)
             else:
-                for j in range(NT):
-                    y = psum.tile([P, C], F32, name=("y", "a", "b", "y")[j])
-                    second(y[:], j)
-                    view = y[:].rearrange("p (m u) -> p m u", u=U)
-                    if j % 2 == 0:
-                        nc.vector.tensor_copy(staged[:, j, :, e, :], view)
-                    else:
-                        nc.scalar.copy(staged[:, j, :, e, :], view)
-                    nc.sync.dma_start(out[P * j : P * (j + 1), :], staged[:, j].rearrange("p m e u -> p (m e u)"))
+                nc.vector.tensor_copy(dst, src)
+
+        def unit(n):
+            e, s = divmod(n, HP)
+            a, b = bank[n % 2], bank[2 + n % 3]
+            first(e, s, a, b)
+            glu(e, s, a, b, 0, 2)
+
+        def middle(e, into):
+            for s in range(HP):
+                for u in range(2):
+                    turn(e, s, u, into)
+            requantize(e, 0, HP, into)
+
+        def finish(e, y, on_scalar):
+            for j in range(NT):
+                for s in range(HP):
+                    second(y[:, j * C : (j + 1) * C], e, j, s)
+            copy_on(on_scalar, staged[:, :, :, e, :], y[:].rearrange("p (j m u) -> p j m u", j=NT, u=U))
+
+        for j in range(3):
+            gather(j, 0, E)
+        gather(3, 0, 1)
+        gather(3, 1, 2)
+        interleave(0, False)
+        interleave(1, True)
+        gather(3, 2, 3)
+        quantize_slots(0)
+        interleave(2, True)
+        gather(3, 3, 4)
+        quantize_slots(1)
+
+        unit(0)
+        interleave(3, False)
+        unit(1)
+        quantize_slots(2)
+        unit(2)
+        quantize_slots(3)
+        unit(3)
+        middle(0, bank[5])
+        unit(4)
+        unit(5)
+        middle(1, bank[5])
+        unit(6)
+        middle(2, bank[5])
+        a, b = bank[1], bank[3]
+        first(3, 1, a, b)
+        for u in range(2):
+            glu(3, 1, a, b, u, u + 1)
+        for u in range(2):
+            turn(3, 0, u, bank[4])
+        requantize(3, 0, 1, bank[4])
+        for u in range(2):
+            turn(3, 1, u, bank[0])
+        requantize(3, 1, 2, bank[0])
+
+        finish(0, bank[6], False)
+        finish(1, bank[7], True)
+        finish(2, bank[6], False)
+        ys = [bank[i] for i in (2, 5, 7, 4)]
+        for s in range(HP):
+            for j in range(NT):
+                second(ys[j][:, :C], 3, j, s)
+        for j in range(NT):
+            copy_on(j % 2 == 1, staged[:, j, :, 3, :], ys[j][:, :C].rearrange("p (m u) -> p m u", u=U))
+            nc.sync.dma_start(out[P * j : P * (j + 1), :], staged[:, j].rearrange("p m e u -> p (m e u)"))

@@ -83,8 +83,9 @@ def tile_moe_eps_glu_silu_kernel(tc, xT, w1_words, w1_scales, w3_words, w3_scale
         load_scales(s3[0], w3_scales, 0, 2)
         load_first(1)
         load_scales(s1[1], w1_scales, 2, E)
+        nc.sync.dma_start(w13[:, 0, 2].bitcast(I32), w1_words[2, 0].bitcast(I32))
         load_scales(s3[1], w3_scales, 2, E)
-        load_first(2)
+        nc.sync.dma_start(w13[:, 1, 2].bitcast(I32), w3_words[2, 0].bitcast(I32))
         load_first(3)
         load_second(0)
         load_scales(s2, w2_scales, 0, E * HP)
@@ -161,7 +162,7 @@ def tile_moe_eps_glu_silu_kernel(tc, xT, w1_words, w1_scales, w3_words, w3_scale
 
         def unit(n):
             e, s = divmod(n, HP)
-            a, b = bank[n % 2], bank[2 + n % 3]
+            a, b = bank[(0, 1, 6)[n % 3]], bank[2 + n % 3]
             first(e, s, a, b)
             glu(e, s, a, b, 0, 2)
 
@@ -199,7 +200,7 @@ def tile_moe_eps_glu_silu_kernel(tc, xT, w1_words, w1_scales, w3_words, w3_scale
         middle(0, bank[5])
         unit(4)
         unit(5)
-        middle(1, bank[5])
+        middle(1, bank[7])
         unit(6)
         middle(2, bank[5])
         a, b = bank[1], bank[3]
@@ -207,16 +208,16 @@ def tile_moe_eps_glu_silu_kernel(tc, xT, w1_words, w1_scales, w3_words, w3_scale
         for u in range(2):
             glu(3, 1, a, b, u, u + 1)
         for u in range(2):
-            turn(3, 0, u, bank[4])
-        requantize(3, 0, 1, bank[4])
+            turn(3, 0, u, bank[7])
+        requantize(3, 0, 1, bank[7])
         for u in range(2):
-            turn(3, 1, u, bank[0])
-        requantize(3, 1, 2, bank[0])
+            turn(3, 1, u, bank[6])
+        requantize(3, 1, 2, bank[6])
 
-        finish(0, bank[6], False)
-        finish(1, bank[7], True)
-        finish(2, bank[6], False)
-        ys = [bank[i] for i in (2, 5, 7, 4)]
+        finish(0, bank[4], False)
+        finish(1, bank[0], True)
+        finish(2, bank[2], False)
+        ys = [bank[i] for i in (1, 3, 5, 4)]
         for s in range(HP):
             for j in range(NT):
                 second(ys[j][:, :C], 3, j, s)

@@ -49,17 +49,25 @@ def tile_moe_eps_glu_silu_kernel(tc, xT, w1_words, w1_scales, w3_words, w3_scale
         ident = keep.tile([P, P], F32, name="ident")
         warm_in = keep.tile([P, 1], F32, name="warm_in")
         warm_out = keep.tile([P, 1], F32, name="warm_out")
+        idle_bf = keep.tile([P, 4 * C], BF16, name="idle_bf", align_bytes=64)
+        idle_codes = keep.tile([P, C], U32, name="idle_codes", align_bytes=64)
+        idle_scales = keep.tile([P, C], U8, name="idle_scales", align_bytes=64)
+        idle_w = keep.tile([P, 2 * P], U8, name="idle_w", align_bytes=64)
+        idle_s = keep.tile([P, P], U8, name="idle_s", align_bytes=64)
         staged = keep.tile([P, NT, R, E, U], F32, name="staged")
         bank = [psum.tile([P, PASS], F32, name="bank%d" % i) for i in range(8)]
 
         nc.vector.memset(warm_in[:], 0.0)
         nc.scalar.activation(warm_out[:], warm_in[:], ACT.Silu)
+        nc.vector.memset(idle_s[:].bitcast(I32), 0)
         nc.vector.memset(s1[0][:].rearrange("p e b -> p (e b)").bitcast(I32), 0)
         nc.vector.memset(w13[:].rearrange("p m e b -> p (m e) b").bitcast(I32)[:, :, :2], 0)
         for plane in (s3[0], s1[1], s3[1]):
             nc.vector.memset(plane[:].rearrange("p e b -> p (e b)").bitcast(I32), 0)
         nc.vector.memset(s2[:].rearrange("p a b -> p (a b)").bitcast(I32), 0)
         nc.vector.memset(w2[:].rearrange("p e s b -> p e (s b)").bitcast(I32)[:, :, :2], 0)
+        nc.vector.memset(idle_bf[:].bitcast(I32), 0)
+        nc.vector.quantize_mx(out=idle_codes[:].bitcast(FP8X4), scales=idle_scales[:], in_=idle_bf[:])
         make_identity(nc, ident[:])
 
         def load_scales(plane, scales, lo, hi):
@@ -72,12 +80,16 @@ def tile_moe_eps_glu_silu_kernel(tc, xT, w1_words, w1_scales, w3_words, w3_scale
             nc.sync.dma_start(w13[:, 1, e].bitcast(I32), w3_words[e, 0].bitcast(I32))
 
         def load_second(e):
-            nc.sync.dma_start(w2[:, e].bitcast(I32), w2_words[e].rearrange("s p n -> p s n").bitcast(I32))
+            nc.sync.dma_start(w2[:, e : e + 2].rearrange("p e s n -> p (e s) n").bitcast(I32), w2_words[e : e + 2].rearrange("e s p n -> p (e s) n").bitcast(I32))
 
-        nc.sync.dma_start(offsets[:], offs)
         x_rows = xT.rearrange("(p j) t -> j p t", j=4)
-        for j in range(4):
-            nc.sync.dma_start(x_row[j][:], x_rows[j])
+        nc.sync.dma_start(x_row[0][:], x_rows[0])
+        nc.sync.dma_start(offsets[:], offs)
+        nc.sync.dma_start(x_row[1][:], x_rows[1])
+        nc.sync.dma_start(x_row[2][:], x_rows[2])
+        nc.sync.dma_start(idle_w[:].bitcast(I32), w1_words[0, 0][:, : 2 * P].bitcast(I32))
+        nc.sync.dma_start(x_row[3][:], x_rows[3])
+        nc.scalar.dma_start(idle_s[0:P:32].bitcast(I32), w1_scales[0, 0].rearrange("(q r) n -> r q n", r=4)[0][:, :P].bitcast(I32))
         load_scales(s1[0], w1_scales, 0, 2)
         load_first(0)
         load_scales(s3[0], w3_scales, 0, 2)
@@ -87,14 +99,15 @@ def tile_moe_eps_glu_silu_kernel(tc, xT, w1_words, w1_scales, w3_words, w3_scale
         load_scales(s3[1], w3_scales, 2, E)
         nc.sync.dma_start(w13[:, 1, 2].bitcast(I32), w3_words[2, 0].bitcast(I32))
         load_first(3)
-        load_second(0)
         load_scales(s2, w2_scales, 0, E * HP)
-        load_second(1)
+        load_second(0)
         load_second(2)
-        load_second(3)
 
         def gather(j, lo, hi):
             nc.vector.tensor_copy(picked[:, j, lo * C : hi * C], x_row[j][:].indirect(offsets[:, lo * C // 16 : hi * C // 16]))
+
+        def gather_rounded(j, e):
+            nc.vector.tensor_copy(slot_bf[:, e * C : (e + 1) * C, j], x_row[j][:].indirect(offsets[:, e * C // 16 : (e + 1) * C // 16]))
 
         def interleave(e, on_scalar):
             src = picked[:, :, e * C : (e + 1) * C].rearrange("p j (c i) -> p c j i", i=4)
@@ -113,13 +126,13 @@ def tile_moe_eps_glu_silu_kernel(tc, xT, w1_words, w1_scales, w3_words, w3_scale
 
         def first(e, s, a, b):
             cols = slice(e * C, (e + 1) * C)
-            for acc, words, plane in ((a, w13[:, 0, e], s1), (b, w13[:, 1, e], s3)):
+            for acc, words, plane in ((a, w13[:, 0, e], s1[e // 2][:, e % 2]), (b, w13[:, 1, e], s3[e // 2][:, e % 2])):
                 nc.tensor.matmul_mx(
                     acc[:],
                     lhsT=slot_codes[:, cols].bitcast(FP8X4),
                     lhsT_scale=slot_scales[:, cols],
                     rhs=words[:, 2 * PASS * s : 2 * PASS * (s + 1)].bitcast(FP4X4),
-                    rhs_scale=plane[e // 2][:, e % 2, PASS * s : PASS * (s + 1)],
+                    rhs_scale=plane[:, PASS * s : PASS * (s + 1)],
                     start=True,
                     stop=True,
                 )
@@ -178,14 +191,16 @@ def tile_moe_eps_glu_silu_kernel(tc, xT, w1_words, w1_scales, w3_words, w3_scale
                     second(y[:, j * C : (j + 1) * C], e, j, s)
             copy_on(on_scalar, staged[:, :, :, e, :], y[:].rearrange("p (j m u) -> p j m u", j=NT, u=U))
 
+        for i in range(20):
+            nc.tensor.matmul_mx(bank[7][:, :C], lhsT=idle_w[:].bitcast(FP4X4), lhsT_scale=idle_s[:], rhs=idle_codes[:].bitcast(FP8X4), rhs_scale=idle_scales[:], start=True, stop=True)
         for j in range(3):
-            gather(j, 0, E)
-        gather(3, 0, 1)
+            gather_rounded(j, 0)
+            gather(j, 1, E)
+        gather_rounded(3, 0)
         gather(3, 1, 2)
-        interleave(0, False)
+        quantize_slots(0)
         interleave(1, True)
         gather(3, 2, 3)
-        quantize_slots(0)
         interleave(2, True)
         gather(3, 3, 4)
         quantize_slots(1)
@@ -214,10 +229,10 @@ def tile_moe_eps_glu_silu_kernel(tc, xT, w1_words, w1_scales, w3_words, w3_scale
             turn(3, 1, u, bank[6])
         requantize(3, 1, 2, bank[6])
 
-        finish(0, bank[4], False)
-        finish(1, bank[0], True)
-        finish(2, bank[2], False)
-        ys = [bank[i] for i in (1, 3, 5, 4)]
+        finish(0, bank[2], False)
+        finish(1, bank[1], True)
+        finish(2, bank[3], False)
+        ys = [bank[i] for i in (0, 4, 5, 7)]
         for s in range(HP):
             for j in range(NT):
                 second(ys[j][:, :C], 3, j, s)

@@ -22,6 +22,9 @@ PASS = 512
 HP = H // PASS
 NT = N // P
 U = C // R
+HALF = T // 2
+UNITS = E * HP
+LAST = E - 1
 
 
 def tile_moe_eps_glu_silu_kernel(tc, xT, w1_words, w1_scales, w3_words, w3_scales, w2_words, w2_scales, offs, out):
@@ -30,44 +33,44 @@ def tile_moe_eps_glu_silu_kernel(tc, xT, w1_words, w1_scales, w3_words, w3_scale
         keep = ctx.enter_context(tc.tile_pool(name="keep", bufs=1))
         psum = ctx.enter_context(tc.psum_pool(name="psum", bufs=1))
 
+        def sbuf(name, shape, dtype, tag=None):
+            return keep.tile([P] + shape, dtype, name=name, tag=tag or name, align_bytes=64)
+
         offsets = keep.tile([P, E * C // 16], U16, name="offsets")
-        s1 = [keep.tile([P, 2, H], U8, name="s1_%d" % g, align_bytes=64) for g in range(2)]
-        s3 = [keep.tile([P, 2, H], U8, name="s3_%d" % g, align_bytes=64) for g in range(2)]
-        s2 = keep.tile([P, E * HP, N], U8, name="s2", align_bytes=64)
-        w13 = keep.tile([P, 2, E, 2 * H], U8, name="w13", align_bytes=64)
-        w2 = keep.tile([P, E, HP, 2 * N], U8, name="w2", align_bytes=64)
-        x_row = [keep.tile([P, T], F32, name="x_row%d" % j) for j in range(4)]
-        picked = keep.tile([P, 4, E * C], F32, name="picked")
-        slot_bf = keep.tile([P, E * C, 4], BF16, name="slot_bf", align_bytes=64)
-        slot_codes = keep.tile([P, E * C], U32, name="slot_codes", align_bytes=64)
-        slot_scales = keep.tile([P, E * C], U8, name="slot_scales", align_bytes=64)
-        gate = keep.tile([P, E, HP, 2, P, 2], F32, name="gate")
-        h = keep.tile([P, E, HP, 2, P, 2], BF16, name="h")
-        h_turned = keep.tile([P, E, HP, C, 2], F32, name="h_turned", align_bytes=64)
-        h_codes = keep.tile([P, E, HP, C], U32, name="h_codes", align_bytes=64)
-        h_scales = keep.tile([P, E, HP, C], U8, name="h_scales", align_bytes=64)
-        ident = keep.tile([P, P], F32, name="ident")
-        warm_in = keep.tile([P, 1], F32, name="warm_in")
-        warm_out = keep.tile([P, 1], F32, name="warm_out")
-        idle_bf = keep.tile([P, 4 * C], BF16, name="idle_bf", align_bytes=64)
-        idle_codes = keep.tile([P, C], U32, name="idle_codes", align_bytes=64)
-        idle_scales = keep.tile([P, C], U8, name="idle_scales", align_bytes=64)
-        idle_w = keep.tile([P, 2 * P], U8, name="idle_w", align_bytes=64)
-        idle_s = keep.tile([P, P], U8, name="idle_s", align_bytes=64)
-        staged = keep.tile([P, NT, R, E, U], F32, name="staged")
+        s1 = [sbuf("s1_%d" % g, [2, H], U8) for g in range(2)]
+        s3 = [sbuf("s3_%d" % g, [2, H], U8) for g in range(2)]
+        x_pairs = [sbuf("x_pairs%d" % u, [T, 2], BF16) for u in range(2)]
+        slots = [sbuf("slots%d" % e, [C, 2], U32) for e in range(E)]
+        slot_codes = [sbuf("slot_codes%d" % e, [C], U32) for e in range(E)]
+        slot_scales = [sbuf("slot_scales%d" % e, [C], U8) for e in range(E)]
+        gate = [sbuf("gate%d" % n, [2, P, 2], F32) for n in range(UNITS)]
+        h = [sbuf("h%d" % n, [2, P, 2], BF16) for n in range(UNITS - 1)]
+        h_last = [sbuf("h_last%d" % u, [P, 2], BF16) for u in range(2)]
+        h_turned = [sbuf("h_turned%d" % e, [HP, C, 2], F32) for e in range(LAST)]
+        h_codes = [sbuf("h_codes%d" % e, [HP, C], U32) for e in range(LAST)]
+        h_scales = [sbuf("h_scales%d" % e, [HP, C], U8) for e in range(LAST)]
+        last_turned = [sbuf("last_turned%d" % s, [1, C, 2], F32) for s in range(HP)]
+        last_codes = [sbuf("last_codes%d" % s, [1, C], U32) for s in range(HP)]
+        last_scales = [sbuf("last_scales%d" % s, [1, C], U8) for s in range(HP)]
+        ident = sbuf("ident", [P], F32)
+        warm_in = sbuf("warm_in", [1], F32, "early_words")
+        warm_out = sbuf("warm_out", [1], F32)
+        idle_bf = sbuf("idle_bf", [4 * C], BF16, "x_second")
+        idle_codes = sbuf("idle_codes", [C], U32)
+        idle_scales = sbuf("idle_scales", [C], U8)
+        staged = sbuf("staged", [NT, R, E, U], F32)
         bank = [psum.tile([P, PASS], F32, name="bank%d" % i) for i in range(8)]
+
+        def clear(engine, plane):
+            engine.memset(plane[:].rearrange("p e b -> p (e b)").bitcast(I32), 0)
 
         nc.vector.memset(warm_in[:], 0.0)
         nc.scalar.activation(warm_out[:], warm_in[:], ACT.Silu)
-        nc.vector.memset(idle_s[:].bitcast(I32), 0)
-        nc.vector.memset(s1[0][:].rearrange("p e b -> p (e b)").bitcast(I32), 0)
-        nc.vector.memset(w13[:].rearrange("p m e b -> p (m e) b").bitcast(I32)[:, :, :2], 0)
-        for plane in (s3[0], s1[1], s3[1]):
-            nc.vector.memset(plane[:].rearrange("p e b -> p (e b)").bitcast(I32), 0)
-        nc.vector.memset(s2[:].rearrange("p a b -> p (a b)").bitcast(I32), 0)
-        nc.vector.memset(w2[:].rearrange("p e s b -> p e (s b)").bitcast(I32)[:, :, :2], 0)
         nc.vector.memset(idle_bf[:].bitcast(I32), 0)
+        clear(nc.vector, s1[0])
         nc.vector.quantize_mx(out=idle_codes[:].bitcast(FP8X4), scales=idle_scales[:], in_=idle_bf[:])
+        for plane in (s3[0], s1[1], s3[1]):
+            clear(nc.vector, plane)
         make_identity(nc, ident[:])
 
         def load_scales(plane, scales, lo, hi):
@@ -75,94 +78,91 @@ def tile_moe_eps_glu_silu_kernel(tc, xT, w1_words, w1_scales, w3_words, w3_scale
             for r in range(4):
                 nc.sync.dma_start(plane[r:P:32].bitcast(I32), rows[r][:, lo:hi, :].bitcast(I32))
 
-        def load_first(e):
-            nc.sync.dma_start(w13[:, 0, e].bitcast(I32), w1_words[e, 0].bitcast(I32))
-            nc.sync.dma_start(w13[:, 1, e].bitcast(I32), w3_words[e, 0].bitcast(I32))
+        def load_words(view, words):
+            nc.sync.dma_start(view.bitcast(I32), words.bitcast(I32))
 
-        def load_second(e):
-            nc.sync.dma_start(w2[:, e : e + 2].rearrange("p e s n -> p (e s) n").bitcast(I32), w2_words[e : e + 2].rearrange("e s p n -> p (e s) n").bitcast(I32))
+        def load_x(view, u, half):
+            rows = xT.rearrange("(p u c) t -> u p c t", u=2, c=2)
+            nc.sync.dma_start(view, rows[u][:, :, HALF * half : HALF * (half + 1)])
 
-        x_rows = xT.rearrange("(p j) t -> j p t", j=4)
-        nc.sync.dma_start(x_row[0][:], x_rows[0])
+        def round_pairs(raw, u, half):
+            nc.scalar.activation(x_pairs[u][:, HALF * half : HALF * (half + 1), :], raw.rearrange("p c t -> p t c"), ACT.Copy)
+
+        x_a = sbuf("x_a", [2, HALF], F32, "late_words")
+        x_b = sbuf("x_b", [2, HALF], F32, "second_scales")
+        x_cd = sbuf("x_cd", [2, T], F32, "x_second")
+        early = sbuf("early", [2, 2, 2 * H], U8, "early_words")
+        load_x(x_a[:], 0, 0)
         nc.sync.dma_start(offsets[:], offs)
-        nc.sync.dma_start(x_row[1][:], x_rows[1])
-        nc.sync.dma_start(x_row[2][:], x_rows[2])
-        nc.sync.dma_start(idle_w[:].bitcast(I32), w1_words[0, 0][:, : 2 * P].bitcast(I32))
-        nc.sync.dma_start(x_row[3][:], x_rows[3])
-        nc.scalar.dma_start(idle_s[0:P:32].bitcast(I32), w1_scales[0, 0].rearrange("(q r) n -> r q n", r=4)[0][:, :P].bitcast(I32))
+        load_x(x_b[:], 0, 1)
         load_scales(s1[0], w1_scales, 0, 2)
-        load_first(0)
+        load_x(x_cd[:, :, :HALF], 1, 0)
+        load_x(x_cd[:, :, HALF:], 1, 1)
         load_scales(s3[0], w3_scales, 0, 2)
-        load_first(1)
+        for e in range(2):
+            load_words(early[:, e, 0], w1_words[e, 0])
+            load_words(early[:, e, 1], w3_words[e, 0])
         load_scales(s1[1], w1_scales, 2, E)
-        nc.sync.dma_start(w13[:, 0, 2].bitcast(I32), w1_words[2, 0].bitcast(I32))
         load_scales(s3[1], w3_scales, 2, E)
-        nc.sync.dma_start(w13[:, 1, 2].bitcast(I32), w3_words[2, 0].bitcast(I32))
-        load_first(3)
+        round_pairs(x_a[:], 0, 0)
+        late = sbuf("late", [2, 2, 2 * H], U8, "late_words")
+        for e in range(2):
+            load_words(late[:, e, 0], w1_words[2 + e, 0])
+            load_words(late[:, e, 1], w3_words[2 + e, 0])
+        round_pairs(x_b[:], 0, 1)
+        s2 = sbuf("s2", [E * HP, N], U8, "second_scales")
+        clear(nc.gpsimd, s2)
         load_scales(s2, w2_scales, 0, E * HP)
-        load_second(0)
-        load_second(2)
+        w1 = [(early, late)[e // 2][:, e % 2, 0] for e in range(E)]
+        w3 = [(early, late)[e // 2][:, e % 2, 1] for e in range(E)]
 
-        def gather(j, lo, hi):
-            nc.vector.tensor_copy(picked[:, j, lo * C : hi * C], x_row[j][:].indirect(offsets[:, lo * C // 16 : hi * C // 16]))
+        def listed(e):
+            return offsets[:, e * C // 16 : (e + 1) * C // 16]
 
-        def gather_rounded(j, e):
-            nc.vector.tensor_copy(slot_bf[:, e * C : (e + 1) * C, j], x_row[j][:].indirect(offsets[:, e * C // 16 : (e + 1) * C // 16]))
+        def gather_pairs(u, e):
+            window = x_pairs[u][:].rearrange("p t c -> p (t c)").bitcast(U32)
+            nc.vector.tensor_copy(slots[e][:, :, u], window.indirect(listed(e)))
 
-        def interleave(e, on_scalar):
-            src = picked[:, :, e * C : (e + 1) * C].rearrange("p j (c i) -> p c j i", i=4)
-            dst = slot_bf[:, e * C : (e + 1) * C, :].rearrange("p (c i) j -> p c j i", i=4)
-            if on_scalar:
-                nc.scalar.activation(dst, src, ACT.Copy)
-            else:
-                nc.vector.tensor_copy(dst, src)
+        def slot_values(e):
+            return slots[e][:].rearrange("p c u -> p (c u)").bitcast(BF16)
+
+        def gather_rounded(c, e):
+            nc.vector.tensor_copy(slot_values(e).rearrange("p (c j) -> p c j", j=4)[:, :, 2 + c], x_cd[:, c].indirect(listed(e)))
 
         def quantize_slots(e):
-            nc.vector.quantize_mx(
-                out=slot_codes[:, e * C : (e + 1) * C].bitcast(FP8X4),
-                scales=slot_scales[:, e * C : (e + 1) * C],
-                in_=slot_bf[:, e * C : (e + 1) * C, :].rearrange("p t j -> p (t j)"),
+            nc.vector.quantize_mx(out=slot_codes[e][:].bitcast(FP8X4), scales=slot_scales[e][:], in_=slot_values(e))
+
+        def product(acc, e, s, words, plane):
+            nc.tensor.matmul_mx(
+                acc[:],
+                lhsT=slot_codes[e][:].bitcast(FP8X4),
+                lhsT_scale=slot_scales[e][:],
+                rhs=words[e][:, 2 * PASS * s : 2 * PASS * (s + 1)].bitcast(FP4X4),
+                rhs_scale=plane[e // 2][:, e % 2, PASS * s : PASS * (s + 1)],
+                start=True,
+                stop=True,
             )
 
-        def first(e, s, a, b):
-            cols = slice(e * C, (e + 1) * C)
-            for acc, words, plane in ((a, w13[:, 0, e], s1[e // 2][:, e % 2]), (b, w13[:, 1, e], s3[e // 2][:, e % 2])):
-                nc.tensor.matmul_mx(
-                    acc[:],
-                    lhsT=slot_codes[:, cols].bitcast(FP8X4),
-                    lhsT_scale=slot_scales[:, cols],
-                    rhs=words[:, 2 * PASS * s : 2 * PASS * (s + 1)].bitcast(FP4X4),
-                    rhs_scale=plane[:, PASS * s : PASS * (s + 1)],
-                    start=True,
-                    stop=True,
-                )
+        def by_pairs(acc):
+            return acc[:].rearrange("p (q u c) -> p u q c", u=2, c=2)
 
-        def glu(e, s, a, b, u0, u1):
-            a_view = a[:].rearrange("p (q u c) -> p u q c", u=2, c=2)
-            b_view = b[:].rearrange("p (q u c) -> p u q c", u=2, c=2)
-            nc.scalar.activation(gate[:, e, s, u0:u1], a_view[:, u0:u1], ACT.Silu)
-            nc.vector.tensor_tensor(h[:, e, s, u0:u1], b_view[:, u0:u1], gate[:, e, s, u0:u1], MULT)
+        def turn(pairs, into, s, u):
+            nc.tensor.transpose(into[:, (2 * s + u) * C : (2 * s + u + 1) * C], pairs.rearrange("p q c -> p (q c)").bitcast(F32), ident[:])
 
-        def turn(e, s, u, into):
-            pairs = h[:, e, s, u].rearrange("p q c -> p (q c)").bitcast(F32)
-            nc.tensor.transpose(into[:, (2 * s + u) * C : (2 * s + u + 1) * C], pairs, ident[:])
-
-        def requantize(e, lo, hi, source):
-            view = source[:].rearrange("p (s u c) -> p s c u", s=HP, u=2)
-            nc.scalar.copy(h_turned[:, e, lo:hi], view[:, lo:hi])
+        def quantize_hidden(turned, codes, scales):
             nc.vector.quantize_mx(
-                out=h_codes[:, e, lo:hi].rearrange("p s c -> p (s c)").bitcast(FP8X4),
-                scales=h_scales[:, e, lo:hi].rearrange("p s c -> p (s c)"),
-                in_=h_turned[:, e, lo:hi].rearrange("p s c u -> p (s c u)").bitcast(BF16),
+                out=codes[:].rearrange("p s c -> p (s c)").bitcast(FP8X4),
+                scales=scales[:].rearrange("p s c -> p (s c)"),
+                in_=turned[:].rearrange("p s c u -> p (s c u)").bitcast(BF16),
             )
 
-        def second(acc, e, j, s):
+        def second(acc, e, j, s, codes, scales):
             nc.tensor.matmul_mx(
                 acc,
                 lhsT=w2[:, e, s, 2 * P * j : 2 * P * (j + 1)].bitcast(FP4X4),
                 lhsT_scale=s2[:, e * HP + s, P * j : P * (j + 1)],
-                rhs=h_codes[:, e, s].bitcast(FP8X4),
-                rhs_scale=h_scales[:, e, s],
+                rhs=codes.bitcast(FP8X4),
+                rhs_scale=scales,
                 start=(s == 0),
                 stop=(s == HP - 1),
             )
@@ -173,69 +173,99 @@ def tile_moe_eps_glu_silu_kernel(tc, xT, w1_words, w1_scales, w3_words, w3_scale
             else:
                 nc.vector.tensor_copy(dst, src)
 
-        def unit(n):
-            e, s = divmod(n, HP)
-            a, b = bank[(0, 1, 6)[n % 3]], bank[2 + n % 3]
-            first(e, s, a, b)
-            glu(e, s, a, b, 0, 2)
+        a_bank = [bank[i] for i in (0, 1, 4, 5, 0, 1, 5, 0)]
+        b_bank = [bank[i] for i in (2, 3, 6, 7, 2, 3, 6, 7)]
+        turn_bank = [bank[i] for i in (4, 1, 2)]
+        last_turn_bank = [bank[i] for i in (5, 3)]
+        y_bank = [bank[i] for i in (4, 6, 7)]
+        last_y_bank = [bank[i] for i in (0, 1, 2, 5)]
 
-        def middle(e, into):
+        def products(e):
+            for s in range(HP):
+                product(a_bank[HP * e + s], e, s, w1, s1)
+            for s in range(HP):
+                product(b_bank[HP * e + s], e, s, w3, s3)
+
+        def silu(n):
+            nc.scalar.activation(gate[n][:], by_pairs(a_bank[n]), ACT.Silu)
+
+        def gated(n):
+            nc.vector.tensor_tensor(h[n][:], by_pairs(b_bank[n]), gate[n][:], MULT)
+
+        def turn_expert(e):
             for s in range(HP):
                 for u in range(2):
-                    turn(e, s, u, into)
-            requantize(e, 0, HP, into)
+                    turn(h[HP * e + s][:, u], turn_bank[e], s, u)
 
-        def finish(e, y, on_scalar):
+        def unload_turned(on_scalar, source, lo, hi, turned):
+            copy_on(on_scalar, turned[:], source[:].rearrange("p (s u c) -> p s c u", s=HP, u=2)[:, lo:hi])
+
+        def second_layer(e):
             for j in range(NT):
                 for s in range(HP):
-                    second(y[:, j * C : (j + 1) * C], e, j, s)
-            copy_on(on_scalar, staged[:, :, :, e, :], y[:].rearrange("p (j m u) -> p j m u", j=NT, u=U))
+                    second(y_bank[e][:, j * C : (j + 1) * C], e, j, s, h_codes[e][:, s], h_scales[e][:, s])
+
+        def unload_y(e, on_scalar):
+            copy_on(on_scalar, staged[:, :, :, e, :], y_bank[e][:].rearrange("p (j m u) -> p j m u", j=NT, u=U))
 
         for i in range(20):
-            nc.tensor.matmul_mx(bank[7][:, :C], lhsT=idle_w[:].bitcast(FP4X4), lhsT_scale=idle_s[:], rhs=idle_codes[:].bitcast(FP8X4), rhs_scale=idle_scales[:], start=True, stop=True)
-        for j in range(3):
-            gather_rounded(j, 0)
-            gather(j, 1, E)
-        gather_rounded(3, 0)
-        gather(3, 1, 2)
+            nc.tensor.matmul_mx(bank[7][:, :C], lhsT=s1[0][:, 0, : 2 * P].bitcast(FP4X4), lhsT_scale=s1[0][:, 0, :P], rhs=idle_codes[:].bitcast(FP8X4), rhs_scale=idle_scales[:], start=True, stop=True)
+        for e in range(E):
+            gather_pairs(0, e)
+        round_pairs(x_cd[:, :, :HALF], 1, 0)
+        round_pairs(x_cd[:, :, HALF:], 1, 1)
+        for c in range(2):
+            gather_rounded(c, 0)
+        w2 = sbuf("w2", [E, HP, 2 * N], U8, "x_second")
+        for e in range(E):
+            load_words(w2[:, e], w2_words[e].rearrange("s p n -> p s n"))
         quantize_slots(0)
-        interleave(1, True)
-        gather(3, 2, 3)
-        interleave(2, True)
-        gather(3, 3, 4)
+        gather_pairs(1, 1)
+        gather_pairs(1, 2)
         quantize_slots(1)
-
-        unit(0)
-        interleave(3, False)
-        unit(1)
+        gather_pairs(1, 3)
         quantize_slots(2)
-        unit(2)
         quantize_slots(3)
-        unit(3)
-        middle(0, bank[5])
-        unit(4)
-        unit(5)
-        middle(1, bank[7])
-        unit(6)
-        middle(2, bank[5])
-        a, b = bank[1], bank[3]
-        first(3, 1, a, b)
-        for u in range(2):
-            glu(3, 1, a, b, u, u + 1)
-        for u in range(2):
-            turn(3, 0, u, bank[7])
-        requantize(3, 0, 1, bank[7])
-        for u in range(2):
-            turn(3, 1, u, bank[6])
-        requantize(3, 1, 2, bank[6])
 
-        finish(0, bank[2], False)
-        finish(1, bank[1], True)
-        finish(2, bank[3], False)
-        ys = [bank[i] for i in (0, 4, 5, 7)]
+        for e in range(LAST):
+            products(e)
+            for s in range(HP):
+                silu(HP * e + s)
+                gated(HP * e + s)
+        turn_expert(0)
+        products(LAST)
+        unload_turned(True, turn_bank[0], 0, HP, h_turned[0])
+        n = UNITS - 1
+        silu(n - 1)
+        quantize_hidden(h_turned[0], h_codes[0], h_scales[0])
+        gated(n - 1)
+        for u in range(2):
+            nc.scalar.activation(gate[n][:, u], by_pairs(a_bank[n])[:, u], ACT.Silu)
+        turn_expert(1)
+        turn_expert(2)
+        for u in range(2):
+            nc.vector.tensor_tensor(h_last[u][:], by_pairs(b_bank[n])[:, u], gate[n][:, u], MULT)
+        for e in (1, 2):
+            unload_turned(True, turn_bank[e], 0, HP, h_turned[e])
+        second_layer(0)
+        for u in range(2):
+            turn(h[n - 1][:, u], last_turn_bank[0], 0, u)
+        for u in range(2):
+            turn(h_last[u][:], last_turn_bank[1], 1, u)
+        for e in (1, 2):
+            quantize_hidden(h_turned[e], h_codes[e], h_scales[e])
+        unload_y(0, True)
+        for s in range(HP):
+            unload_turned(s == 1, last_turn_bank[s], s, s + 1, last_turned[s])
+        for s in range(HP):
+            quantize_hidden(last_turned[s], last_codes[s], last_scales[s])
+        second_layer(1)
+        second_layer(2)
+        unload_y(1, False)
+        unload_y(2, True)
         for s in range(HP):
             for j in range(NT):
-                second(ys[j][:, :C], 3, j, s)
+                second(last_y_bank[j][:, :C], LAST, j, s, last_codes[s][:, 0], last_scales[s][:, 0])
         for j in range(NT):
-            copy_on(j % 2 == 1, staged[:, j, :, 3, :], ys[j][:, :C].rearrange("p (m u) -> p m u", u=U))
+            copy_on(j % 2 == 1, staged[:, j, :, LAST, :], last_y_bank[j][:, :C].rearrange("p (m u) -> p m u", u=U))
             nc.sync.dma_start(out[P * j : P * (j + 1), :], staged[:, j].rearrange("p m e u -> p (m e u)"))

@@ -37,8 +37,8 @@ def tile_moe_eps_glu_silu_kernel(tc, xT, w1_words, w1_scales, w3_words, w3_scale
             return keep.tile([P] + shape, dtype, name=name, tag=tag or name, align_bytes=64)
 
         offsets = keep.tile([P, E * C // 16], U16, name="offsets")
-        s1 = [sbuf("s1_%d" % g, [2, H], U8) for g in range(2)]
-        s3 = [sbuf("s3_%d" % g, [2, H], U8) for g in range(2)]
+        s1 = sbuf("s1", [E, H], U8)
+        s3 = sbuf("s3", [E, H], U8)
         x_pairs = [sbuf("x_pairs%d" % u, [T, 2], BF16) for u in range(2)]
         slots = [sbuf("slots%d" % e, [C, 2], U32) for e in range(E)]
         slot_codes = [sbuf("slot_codes%d" % e, [C], U32) for e in range(E)]
@@ -53,9 +53,9 @@ def tile_moe_eps_glu_silu_kernel(tc, xT, w1_words, w1_scales, w3_words, w3_scale
         last_codes = [sbuf("last_codes%d" % s, [1, C], U32) for s in range(HP)]
         last_scales = [sbuf("last_scales%d" % s, [1, C], U8) for s in range(HP)]
         ident = sbuf("ident", [P], F32)
-        warm_in = sbuf("warm_in", [1], F32, "early_words")
+        warm_in = sbuf("warm_in", [1], F32)
         warm_out = sbuf("warm_out", [1], F32)
-        idle_bf = sbuf("idle_bf", [4 * C], BF16, "x_second")
+        idle_bf = sbuf("idle_bf", [4 * C], BF16)
         idle_codes = sbuf("idle_codes", [C], U32)
         idle_scales = sbuf("idle_scales", [C], U8)
         staged = sbuf("staged", [NT, R, E, U], F32)
@@ -64,19 +64,18 @@ def tile_moe_eps_glu_silu_kernel(tc, xT, w1_words, w1_scales, w3_words, w3_scale
         def clear(engine, plane):
             engine.memset(plane[:].rearrange("p e b -> p (e b)").bitcast(I32), 0)
 
-        nc.vector.memset(warm_in[:], 0.0)
-        nc.scalar.activation(warm_out[:], warm_in[:], ACT.Silu)
-        nc.vector.memset(idle_bf[:].bitcast(I32), 0)
-        clear(nc.vector, s1[0])
-        nc.vector.quantize_mx(out=idle_codes[:].bitcast(FP8X4), scales=idle_scales[:], in_=idle_bf[:])
-        for plane in (s3[0], s1[1], s3[1]):
-            clear(nc.vector, plane)
-        make_identity(nc, ident[:])
-
-        def load_scales(plane, scales, lo, hi):
+        def load_scales(queue, plane, scales, lo, hi):
             rows = scales.rearrange("e s (q r) n -> r q (e s) n", r=4)
             for r in range(4):
-                nc.sync.dma_start(plane[r:P:32].bitcast(I32), rows[r][:, lo:hi, :].bitcast(I32))
+                queue.dma_start(plane[r:P:32].bitcast(I32), rows[r][:, lo:hi, :].bitcast(I32))
+
+        nc.vector.memset(warm_in[:], 0.0)
+        nc.scalar.activation(warm_out[:], warm_in[:], ACT.Silu)
+        clear(nc.vector, s1)
+        clear(nc.vector, s3)
+        nc.vector.memset(idle_bf[:].bitcast(I32), 0)
+        nc.vector.quantize_mx(out=idle_codes[:].bitcast(FP8X4), scales=idle_scales[:], in_=idle_bf[:])
+        make_identity(nc, ident[:])
 
         def load_words(view, words):
             nc.sync.dma_start(view.bitcast(I32), words.bitcast(I32))
@@ -88,33 +87,34 @@ def tile_moe_eps_glu_silu_kernel(tc, xT, w1_words, w1_scales, w3_words, w3_scale
         def round_pairs(raw, u, half):
             nc.scalar.activation(x_pairs[u][:, HALF * half : HALF * (half + 1), :], raw.rearrange("p c t -> p t c"), ACT.Copy)
 
-        x_a = sbuf("x_a", [2, HALF], F32, "late_words")
+        x_a = sbuf("x_a", [2, HALF], F32, "first_words")
         x_b = sbuf("x_b", [2, HALF], F32, "second_scales")
-        x_cd = sbuf("x_cd", [2, T], F32, "x_second")
-        early = sbuf("early", [2, 2, 2 * H], U8, "early_words")
+        x_cd = sbuf("x_cd", [2, 2, HALF], F32, "second_words")
         load_x(x_a[:], 0, 0)
         nc.sync.dma_start(offsets[:], offs)
         load_x(x_b[:], 0, 1)
-        load_scales(s1[0], w1_scales, 0, 2)
-        load_x(x_cd[:, :, :HALF], 1, 0)
-        load_x(x_cd[:, :, HALF:], 1, 1)
-        load_scales(s3[0], w3_scales, 0, 2)
-        for e in range(2):
-            load_words(early[:, e, 0], w1_words[e, 0])
-            load_words(early[:, e, 1], w3_words[e, 0])
-        load_scales(s1[1], w1_scales, 2, E)
-        load_scales(s3[1], w3_scales, 2, E)
+        load_x(x_cd[:, 0], 1, 0)
+        load_x(x_cd[:, 1], 1, 1)
+        load_scales(nc.sync, s1, w1_scales, 0, E)
+        load_scales(nc.sync, s3, w3_scales, 0, E)
         round_pairs(x_a[:], 0, 0)
-        late = sbuf("late", [2, 2, 2 * H], U8, "late_words")
-        for e in range(2):
-            load_words(late[:, e, 0], w1_words[2 + e, 0])
-            load_words(late[:, e, 1], w3_words[2 + e, 0])
+        w13 = sbuf("w13", [E, 2, 2 * H], U8, "first_words")
+        for e in range(E):
+            load_words(w13[:, e, 0], w1_words[e, 0])
+            load_words(w13[:, e, 1], w3_words[e, 0])
         round_pairs(x_b[:], 0, 1)
         s2 = sbuf("s2", [E * HP, N], U8, "second_scales")
-        clear(nc.gpsimd, s2)
-        load_scales(s2, w2_scales, 0, E * HP)
-        w1 = [(early, late)[e // 2][:, e % 2, 0] for e in range(E)]
-        w3 = [(early, late)[e // 2][:, e % 2, 1] for e in range(E)]
+        clear(nc.vector, s2)
+        load_scales(nc.sync, s2, w2_scales, 0, E * HP)
+        round_pairs(x_cd[:, 0], 1, 0)
+        round_pairs(x_cd[:, 1], 1, 1)
+        w2 = sbuf("w2", [E, HP, 2 * N], U8, "second_words")
+        for e in range(E):
+            load_words(w2[:, e], w2_words[e].rearrange("s p n -> p s n"))
+        w1 = [w13[:, e, 0] for e in range(E)]
+        w3 = [w13[:, e, 1] for e in range(E)]
+        p1 = [s1[:, e] for e in range(E)]
+        p3 = [s3[:, e] for e in range(E)]
 
         def listed(e):
             return offsets[:, e * C // 16 : (e + 1) * C // 16]
@@ -126,9 +126,6 @@ def tile_moe_eps_glu_silu_kernel(tc, xT, w1_words, w1_scales, w3_words, w3_scale
         def slot_values(e):
             return slots[e][:].rearrange("p c u -> p (c u)").bitcast(BF16)
 
-        def gather_rounded(c, e):
-            nc.vector.tensor_copy(slot_values(e).rearrange("p (c j) -> p c j", j=4)[:, :, 2 + c], x_cd[:, c].indirect(listed(e)))
-
         def quantize_slots(e):
             nc.vector.quantize_mx(out=slot_codes[e][:].bitcast(FP8X4), scales=slot_scales[e][:], in_=slot_values(e))
 
@@ -138,7 +135,7 @@ def tile_moe_eps_glu_silu_kernel(tc, xT, w1_words, w1_scales, w3_words, w3_scale
                 lhsT=slot_codes[e][:].bitcast(FP8X4),
                 lhsT_scale=slot_scales[e][:],
                 rhs=words[e][:, 2 * PASS * s : 2 * PASS * (s + 1)].bitcast(FP4X4),
-                rhs_scale=plane[e // 2][:, e % 2, PASS * s : PASS * (s + 1)],
+                rhs_scale=plane[e][:, PASS * s : PASS * (s + 1)],
                 start=True,
                 stop=True,
             )
@@ -182,9 +179,9 @@ def tile_moe_eps_glu_silu_kernel(tc, xT, w1_words, w1_scales, w3_words, w3_scale
 
         def products(e):
             for s in range(HP):
-                product(a_bank[HP * e + s], e, s, w1, s1)
+                product(a_bank[HP * e + s], e, s, w1, p1)
             for s in range(HP):
-                product(b_bank[HP * e + s], e, s, w3, s3)
+                product(b_bank[HP * e + s], e, s, w3, p3)
 
         def silu(n):
             nc.scalar.activation(gate[n][:], by_pairs(a_bank[n]), ACT.Silu)
@@ -208,24 +205,15 @@ def tile_moe_eps_glu_silu_kernel(tc, xT, w1_words, w1_scales, w3_words, w3_scale
         def unload_y(e, on_scalar):
             copy_on(on_scalar, staged[:, :, :, e, :], y_bank[e][:].rearrange("p (j m u) -> p j m u", j=NT, u=U))
 
-        for i in range(20):
-            nc.tensor.matmul_mx(bank[7][:, :C], lhsT=s1[0][:, 0, : 2 * P].bitcast(FP4X4), lhsT_scale=s1[0][:, 0, :P], rhs=idle_codes[:].bitcast(FP8X4), rhs_scale=idle_scales[:], start=True, stop=True)
+        for i in range(12):
+            nc.tensor.matmul_mx(bank[7][:, :C], lhsT=s1[:, 0, : 2 * P].bitcast(FP4X4), lhsT_scale=s1[:, 0, :P], rhs=idle_codes[:].bitcast(FP8X4), rhs_scale=idle_scales[:], start=True, stop=True)
         for e in range(E):
             gather_pairs(0, e)
-        round_pairs(x_cd[:, :, :HALF], 1, 0)
-        round_pairs(x_cd[:, :, HALF:], 1, 1)
-        for c in range(2):
-            gather_rounded(c, 0)
-        w2 = sbuf("w2", [E, HP, 2 * N], U8, "x_second")
-        for e in range(E):
-            load_words(w2[:, e], w2_words[e].rearrange("s p n -> p s n"))
-        quantize_slots(0)
-        gather_pairs(1, 1)
-        gather_pairs(1, 2)
-        quantize_slots(1)
-        gather_pairs(1, 3)
-        quantize_slots(2)
-        quantize_slots(3)
+        gather_pairs(1, 0)
+        for e in range(1, E):
+            gather_pairs(1, e)
+            quantize_slots(e - 1)
+        quantize_slots(LAST)
 
         for e in range(LAST):
             products(e)

@@ -39,11 +39,12 @@ def tile_moe_eps_glu_silu_kernel(tc, xT, w1_words, w1_scales, w3_words, w3_scale
         offsets = keep.tile([P, E * C // 16], U16, name="offsets")
         s1 = sbuf("s1", [E, H], U8)
         s3 = sbuf("s3", [E, H], U8)
+        s2 = sbuf("s2", [E * HP, N], U8)
         x_pairs = [sbuf("x_pairs%d" % u, [T, 2], BF16) for u in range(2)]
         slots = [sbuf("slots%d" % e, [C, 2], U32) for e in range(E)]
         slot_codes = [sbuf("slot_codes%d" % e, [C], U32) for e in range(E)]
         slot_scales = [sbuf("slot_scales%d" % e, [C], U8) for e in range(E)]
-        gate = [sbuf("gate%d" % n, [2, P, 2], F32) for n in range(UNITS)]
+        gate = [sbuf("gate%d" % n, [2, P, 2], F32, "second_words" if n == 0 else None) for n in range(UNITS)]
         h = [sbuf("h%d" % n, [2, P, 2], BF16) for n in range(UNITS - 1)]
         h_last = [sbuf("h_last%d" % u, [P, 2], BF16) for u in range(2)]
         h_turned = [sbuf("h_turned%d" % e, [HP, C, 2], F32) for e in range(LAST)]
@@ -75,6 +76,7 @@ def tile_moe_eps_glu_silu_kernel(tc, xT, w1_words, w1_scales, w3_words, w3_scale
         clear(nc.vector, s3)
         nc.vector.memset(idle_bf[:].bitcast(I32), 0)
         nc.vector.quantize_mx(out=idle_codes[:].bitcast(FP8X4), scales=idle_scales[:], in_=idle_bf[:])
+        clear(nc.vector, s2)
         make_identity(nc, ident[:])
 
         def load_words(view, words):
@@ -88,30 +90,27 @@ def tile_moe_eps_glu_silu_kernel(tc, xT, w1_words, w1_scales, w3_words, w3_scale
             nc.scalar.activation(x_pairs[u][:, HALF * half : HALF * (half + 1), :], raw.rearrange("p c t -> p t c"), ACT.Copy)
 
         x_a = sbuf("x_a", [2, HALF], F32, "first_words")
-        x_b = sbuf("x_b", [2, HALF], F32, "second_scales")
-        x_cd = sbuf("x_cd", [2, 2, HALF], F32, "second_words")
+        x_b = sbuf("x_b", [2, HALF], F32)
+        x_cd = sbuf("x_cd", [2, T], F32)
         load_x(x_a[:], 0, 0)
         nc.sync.dma_start(offsets[:], offs)
         load_x(x_b[:], 0, 1)
-        load_x(x_cd[:, 0], 1, 0)
-        load_x(x_cd[:, 1], 1, 1)
+        load_x(x_cd[:, :, :HALF], 1, 0)
+        load_x(x_cd[:, :, HALF:], 1, 1)
+        w1_first = sbuf("w1_first", [2 * H], U8)
+        load_words(w1_first[:], w1_words[0, 0])
         load_scales(nc.sync, s1, w1_scales, 0, E)
         load_scales(nc.sync, s3, w3_scales, 0, E)
         round_pairs(x_a[:], 0, 0)
         w13 = sbuf("w13", [E, 2, 2 * H], U8, "first_words")
         for e in range(E):
-            load_words(w13[:, e, 0], w1_words[e, 0])
+            if e > 0:
+                load_words(w13[:, e, 0], w1_words[e, 0])
             load_words(w13[:, e, 1], w3_words[e, 0])
         round_pairs(x_b[:], 0, 1)
-        s2 = sbuf("s2", [E * HP, N], U8, "second_scales")
-        clear(nc.vector, s2)
-        load_scales(nc.sync, s2, w2_scales, 0, E * HP)
-        round_pairs(x_cd[:, 0], 1, 0)
-        round_pairs(x_cd[:, 1], 1, 1)
-        w2 = sbuf("w2", [E, HP, 2 * N], U8, "second_words")
-        for e in range(E):
-            load_words(w2[:, e], w2_words[e].rearrange("s p n -> p s n"))
-        w1 = [w13[:, e, 0] for e in range(E)]
+        round_pairs(x_cd[:, :, :HALF], 1, 0)
+        round_pairs(x_cd[:, :, HALF:], 1, 1)
+        w1 = [w1_first[:]] + [w13[:, e, 0] for e in range(1, E)]
         w3 = [w13[:, e, 1] for e in range(E)]
         p1 = [s1[:, e] for e in range(E)]
         p3 = [s3[:, e] for e in range(E)]
@@ -125,6 +124,9 @@ def tile_moe_eps_glu_silu_kernel(tc, xT, w1_words, w1_scales, w3_words, w3_scale
 
         def slot_values(e):
             return slots[e][:].rearrange("p c u -> p (c u)").bitcast(BF16)
+
+        def gather_rounded(c, e):
+            nc.vector.tensor_copy(slot_values(e).rearrange("p (c j) -> p c j", j=4)[:, :, 2 + c], x_cd[:, c].indirect(listed(e)))
 
         def quantize_slots(e):
             nc.vector.quantize_mx(out=slot_codes[e][:].bitcast(FP8X4), scales=slot_scales[e][:], in_=slot_values(e))
@@ -205,21 +207,26 @@ def tile_moe_eps_glu_silu_kernel(tc, xT, w1_words, w1_scales, w3_words, w3_scale
         def unload_y(e, on_scalar):
             copy_on(on_scalar, staged[:, :, :, e, :], y_bank[e][:].rearrange("p (j m u) -> p j m u", j=NT, u=U))
 
-        for i in range(12):
-            nc.tensor.matmul_mx(bank[7][:, :C], lhsT=s1[:, 0, : 2 * P].bitcast(FP4X4), lhsT_scale=s1[:, 0, :P], rhs=idle_codes[:].bitcast(FP8X4), rhs_scale=idle_scales[:], start=True, stop=True)
+        for i in range(8):
+            nc.tensor.matmul_mx(bank[7][:, :C], lhsT=w1_first[:, : 2 * P].bitcast(FP4X4), lhsT_scale=s2[:, 0, :P], rhs=idle_codes[:].bitcast(FP8X4), rhs_scale=idle_scales[:], start=True, stop=True)
         for e in range(E):
             gather_pairs(0, e)
-        gather_pairs(1, 0)
+        for c in range(2):
+            gather_rounded(c, 0)
         for e in range(1, E):
             gather_pairs(1, e)
             quantize_slots(e - 1)
         quantize_slots(LAST)
+        load_scales(nc.sync, s2, w2_scales, 0, E * HP)
 
         for e in range(LAST):
             products(e)
             for s in range(HP):
                 silu(HP * e + s)
                 gated(HP * e + s)
+        w2 = sbuf("w2", [E, HP, 2 * N], U8, "second_words")
+        for e in range(E):
+            load_words(w2[:, e], w2_words[e].rearrange("s p n -> p s n"))
         turn_expert(0)
         products(LAST)
         unload_turned(True, turn_bank[0], 0, HP, h_turned[0])

@@ -25,6 +25,7 @@ U = C // R
 HALF = T // 2
 UNITS = E * HP
 LAST = E - 1
+SPLIT = 336
 
 
 def tile_moe_eps_glu_silu_kernel(tc, xT, w1_words, w1_scales, w3_words, w3_scales, w2_words, w2_scales, offs, out):
@@ -37,7 +38,7 @@ def tile_moe_eps_glu_silu_kernel(tc, xT, w1_words, w1_scales, w3_words, w3_scale
             return keep.tile([P] + shape, dtype, name=name, tag=tag or name, align_bytes=64)
 
         offsets = keep.tile([P, E * C // 16], U16, name="offsets")
-        s1 = sbuf("s1", [E, H], U8)
+        s1 = [sbuf("s1_%d" % g, [2, H], U8) for g in range(2)]
         s3 = sbuf("s3", [E, H], U8)
         s2 = sbuf("s2", [E * HP, N], U8)
         x_pairs = [sbuf("x_pairs%d" % u, [T, 2], BF16) for u in range(2)]
@@ -54,9 +55,9 @@ def tile_moe_eps_glu_silu_kernel(tc, xT, w1_words, w1_scales, w3_words, w3_scale
         last_codes = [sbuf("last_codes%d" % s, [1, C], U32) for s in range(HP)]
         last_scales = [sbuf("last_scales%d" % s, [1, C], U8) for s in range(HP)]
         ident = sbuf("ident", [P], F32)
-        warm_in = sbuf("warm_in", [1], F32)
+        warm_in = sbuf("warm_in", [1], F32, "early_words")
         warm_out = sbuf("warm_out", [1], F32)
-        idle_bf = sbuf("idle_bf", [4 * C], BF16)
+        idle_bf = sbuf("idle_bf", [4 * C], BF16, "x_second")
         idle_codes = sbuf("idle_codes", [C], U32)
         idle_scales = sbuf("idle_scales", [C], U8)
         staged = sbuf("staged", [NT, R, E, U], F32)
@@ -72,11 +73,11 @@ def tile_moe_eps_glu_silu_kernel(tc, xT, w1_words, w1_scales, w3_words, w3_scale
 
         nc.vector.memset(warm_in[:], 0.0)
         nc.scalar.activation(warm_out[:], warm_in[:], ACT.Silu)
-        clear(nc.vector, s1)
-        clear(nc.vector, s3)
         nc.vector.memset(idle_bf[:].bitcast(I32), 0)
+        clear(nc.vector, s1[0])
         nc.vector.quantize_mx(out=idle_codes[:].bitcast(FP8X4), scales=idle_scales[:], in_=idle_bf[:])
-        clear(nc.vector, s2)
+        for plane in (s3, s2, s1[1]):
+            clear(nc.vector, plane)
         make_identity(nc, ident[:])
 
         def load_words(view, words):
@@ -86,33 +87,43 @@ def tile_moe_eps_glu_silu_kernel(tc, xT, w1_words, w1_scales, w3_words, w3_scale
             rows = xT.rearrange("(p u c) t -> u p c t", u=2, c=2)
             nc.sync.dma_start(view, rows[u][:, :, HALF * half : HALF * (half + 1)])
 
-        def round_pairs(raw, u, half):
-            nc.scalar.activation(x_pairs[u][:, HALF * half : HALF * (half + 1), :], raw.rearrange("p c t -> p t c"), ACT.Copy)
+        def round_pairs(raw, u, lo, on_scalar):
+            src = raw.rearrange("p c t -> p t c")
+            dst = x_pairs[u][:, lo : lo + raw.shape[2], :]
+            if on_scalar:
+                nc.scalar.activation(dst, src, ACT.Copy)
+            else:
+                nc.vector.tensor_copy(dst, src)
 
-        x_a = sbuf("x_a", [2, HALF], F32, "first_words")
-        x_b = sbuf("x_b", [2, HALF], F32)
-        x_cd = sbuf("x_cd", [2, T], F32)
+        x_a = sbuf("x_a", [2, HALF], F32, "middle_words")
+        x_b = sbuf("x_b", [2, HALF], F32, "late_words")
+        x_cd = sbuf("x_cd", [2, T], F32, "x_second")
+        early = sbuf("early", [2 * H], U8, "early_words")
         load_x(x_a[:], 0, 0)
         nc.sync.dma_start(offsets[:], offs)
         load_x(x_b[:], 0, 1)
+        load_scales(nc.sync, s1[0], w1_scales, 0, 2)
         load_x(x_cd[:, :, :HALF], 1, 0)
         load_x(x_cd[:, :, HALF:], 1, 1)
-        w1_first = sbuf("w1_first", [2 * H], U8)
-        load_words(w1_first[:], w1_words[0, 0])
-        load_scales(nc.sync, s1, w1_scales, 0, E)
+        load_words(early[:], w1_words[0, 0])
         load_scales(nc.sync, s3, w3_scales, 0, E)
-        round_pairs(x_a[:], 0, 0)
-        w13 = sbuf("w13", [E, 2, 2 * H], U8, "first_words")
-        for e in range(E):
-            if e > 0:
-                load_words(w13[:, e, 0], w1_words[e, 0])
-            load_words(w13[:, e, 1], w3_words[e, 0])
-        round_pairs(x_b[:], 0, 1)
-        round_pairs(x_cd[:, :, :HALF], 1, 0)
-        round_pairs(x_cd[:, :, HALF:], 1, 1)
-        w1 = [w1_first[:]] + [w13[:, e, 0] for e in range(1, E)]
-        w3 = [w13[:, e, 1] for e in range(E)]
-        p1 = [s1[:, e] for e in range(E)]
+        round_pairs(x_a[:], 0, 0, True)
+        middle = sbuf("middle", [3, 2 * H], U8, "middle_words")
+        load_words(middle[:, 0], w3_words[0, 0])
+        load_words(middle[:, 1], w1_words[1, 0])
+        load_words(middle[:, 2], w3_words[1, 0])
+        load_scales(nc.sync, s1[1], w1_scales, 2, E)
+        round_pairs(x_b[:, :, :SPLIT], 0, HALF, False)
+        round_pairs(x_b[:, :, SPLIT:], 0, HALF + SPLIT, True)
+        late = sbuf("late", [2, 2, 2 * H], U8, "late_words")
+        for e in range(2):
+            load_words(late[:, e, 0], w1_words[2 + e, 0])
+            load_words(late[:, e, 1], w3_words[2 + e, 0])
+        round_pairs(x_cd[:, :, :HALF], 1, 0, True)
+        round_pairs(x_cd[:, :, HALF:], 1, HALF, True)
+        w1 = [early[:], middle[:, 1], late[:, 0, 0], late[:, 1, 0]]
+        w3 = [middle[:, 0], middle[:, 2], late[:, 0, 1], late[:, 1, 1]]
+        p1 = [s1[e // 2][:, e % 2] for e in range(E)]
         p3 = [s3[:, e] for e in range(E)]
 
         def listed(e):
@@ -207,8 +218,9 @@ def tile_moe_eps_glu_silu_kernel(tc, xT, w1_words, w1_scales, w3_words, w3_scale
         def unload_y(e, on_scalar):
             copy_on(on_scalar, staged[:, :, :, e, :], y_bank[e][:].rearrange("p (j m u) -> p j m u", j=NT, u=U))
 
-        for i in range(8):
-            nc.tensor.matmul_mx(bank[7][:, :C], lhsT=w1_first[:, : 2 * P].bitcast(FP4X4), lhsT_scale=s2[:, 0, :P], rhs=idle_codes[:].bitcast(FP8X4), rhs_scale=idle_scales[:], start=True, stop=True)
+        for words, plane, passes in ((s1[0][:, 0], idle_scales[:], 18), (w1[0], s2[:, 0, :P], 2)):
+            for i in range(passes):
+                nc.tensor.matmul_mx(bank[7][:, :C], lhsT=words[:, : 2 * P].bitcast(FP4X4), lhsT_scale=plane, rhs=idle_codes[:].bitcast(FP8X4), rhs_scale=idle_scales[:], start=True, stop=True)
         for e in range(E):
             gather_pairs(0, e)
         for c in range(2):
@@ -258,8 +270,8 @@ def tile_moe_eps_glu_silu_kernel(tc, xT, w1_words, w1_scales, w3_words, w3_scale
         second_layer(2)
         unload_y(1, False)
         unload_y(2, True)
-        for s in range(HP):
-            for j in range(NT):
+        for j in range(NT):
+            for s in range(HP):
                 second(last_y_bank[j][:, :C], LAST, j, s, last_codes[s][:, 0], last_scales[s][:, 0])
         for j in range(NT):
             copy_on(j % 2 == 1, staged[:, j, :, LAST, :], last_y_bank[j][:, :C].rearrange("p (m u) -> p m u", u=U))

@@ -22,10 +22,10 @@ PASS = 512
 HP = H // PASS
 NT = N // P
 U = C // R
-HALF = T // 2
 UNITS = E * HP
 LAST = E - 1
-SPLIT = 336
+FIRST_SPLIT = 672
+SECOND_SPLIT = 256
 
 
 def tile_moe_eps_glu_silu_kernel(tc, xT, w1_words, w1_scales, w3_words, w3_scales, w2_words, w2_scales, offs, out):
@@ -38,7 +38,7 @@ def tile_moe_eps_glu_silu_kernel(tc, xT, w1_words, w1_scales, w3_words, w3_scale
             return keep.tile([P] + shape, dtype, name=name, tag=tag or name, align_bytes=64)
 
         offsets = keep.tile([P, E * C // 16], U16, name="offsets")
-        s1 = [sbuf("s1_%d" % g, [2, H], U8) for g in range(2)]
+        s1 = sbuf("s1", [E, H], U8)
         s3 = sbuf("s3", [E, H], U8)
         s2 = sbuf("s2", [E * HP, N], U8)
         x_pairs = [sbuf("x_pairs%d" % u, [T, 2], BF16) for u in range(2)]
@@ -74,18 +74,14 @@ def tile_moe_eps_glu_silu_kernel(tc, xT, w1_words, w1_scales, w3_words, w3_scale
         nc.vector.memset(warm_in[:], 0.0)
         nc.scalar.activation(warm_out[:], warm_in[:], ACT.Silu)
         nc.vector.memset(idle_bf[:].bitcast(I32), 0)
-        clear(nc.vector, s1[0])
+        clear(nc.vector, s1)
         nc.vector.quantize_mx(out=idle_codes[:].bitcast(FP8X4), scales=idle_scales[:], in_=idle_bf[:])
-        for plane in (s3, s2, s1[1]):
+        for plane in (s3, s2):
             clear(nc.vector, plane)
         make_identity(nc, ident[:])
 
         def load_words(view, words):
             nc.sync.dma_start(view.bitcast(I32), words.bitcast(I32))
-
-        def load_x(view, u, half):
-            rows = xT.rearrange("(p u c) t -> u p c t", u=2, c=2)
-            nc.sync.dma_start(view, rows[u][:, :, HALF * half : HALF * (half + 1)])
 
         def round_pairs(raw, u, lo, on_scalar):
             src = raw.rearrange("p c t -> p t c")
@@ -95,35 +91,27 @@ def tile_moe_eps_glu_silu_kernel(tc, xT, w1_words, w1_scales, w3_words, w3_scale
             else:
                 nc.vector.tensor_copy(dst, src)
 
-        x_a = sbuf("x_a", [2, HALF], F32, "middle_words")
-        x_b = sbuf("x_b", [2, HALF], F32, "late_words")
+        x_ab = sbuf("x_ab", [2, T], F32, "later_words")
         x_cd = sbuf("x_cd", [2, T], F32, "x_second")
         early = sbuf("early", [2 * H], U8, "early_words")
-        load_x(x_a[:], 0, 0)
+        row_pairs = xT.rearrange("(p u c) t -> u p c t", u=2, c=2)
+        nc.sync.dma_start(x_ab[:], row_pairs[0])
         nc.sync.dma_start(offsets[:], offs)
-        load_x(x_b[:], 0, 1)
-        load_scales(nc.sync, s1[0], w1_scales, 0, 2)
-        load_x(x_cd[:, :, :HALF], 1, 0)
-        load_x(x_cd[:, :, HALF:], 1, 1)
+        load_scales(nc.sync, s1, w1_scales, 0, E)
+        nc.sync.dma_start(x_cd[:], row_pairs[1])
         load_words(early[:], w1_words[0, 0])
         load_scales(nc.sync, s3, w3_scales, 0, E)
-        round_pairs(x_a[:], 0, 0, True)
-        middle = sbuf("middle", [3, 2 * H], U8, "middle_words")
-        load_words(middle[:, 0], w3_words[0, 0])
-        load_words(middle[:, 1], w1_words[1, 0])
-        load_words(middle[:, 2], w3_words[1, 0])
-        load_scales(nc.sync, s1[1], w1_scales, 2, E)
-        round_pairs(x_b[:, :, :SPLIT], 0, HALF, False)
-        round_pairs(x_b[:, :, SPLIT:], 0, HALF + SPLIT, True)
-        late = sbuf("late", [2, 2, 2 * H], U8, "late_words")
-        for e in range(2):
-            load_words(late[:, e, 0], w1_words[2 + e, 0])
-            load_words(late[:, e, 1], w3_words[2 + e, 0])
-        round_pairs(x_cd[:, :, :HALF], 1, 0, True)
-        round_pairs(x_cd[:, :, HALF:], 1, HALF, True)
-        w1 = [early[:], middle[:, 1], late[:, 0, 0], late[:, 1, 0]]
-        w3 = [middle[:, 0], middle[:, 2], late[:, 0, 1], late[:, 1, 1]]
-        p1 = [s1[e // 2][:, e % 2] for e in range(E)]
+        round_pairs(x_ab[:, :, :FIRST_SPLIT], 0, 0, False)
+        round_pairs(x_ab[:, :, FIRST_SPLIT:], 0, FIRST_SPLIT, True)
+        later = sbuf("later", [2 * E - 1, 2 * H], U8, "later_words")
+        load_words(later[:, 0], w3_words[0, 0])
+        for e in range(1, E):
+            load_words(later[:, 2 * e - 1], w1_words[e, 0])
+            load_words(later[:, 2 * e], w3_words[e, 0])
+        round_pairs(x_cd[:, :, SECOND_SPLIT:], 1, SECOND_SPLIT, True)
+        w1 = [early[:]] + [later[:, 2 * e - 1] for e in range(1, E)]
+        w3 = [later[:, 2 * e] for e in range(E)]
+        p1 = [s1[:, e] for e in range(E)]
         p3 = [s3[:, e] for e in range(E)]
 
         def listed(e):
@@ -218,13 +206,14 @@ def tile_moe_eps_glu_silu_kernel(tc, xT, w1_words, w1_scales, w3_words, w3_scale
         def unload_y(e, on_scalar):
             copy_on(on_scalar, staged[:, :, :, e, :], y_bank[e][:].rearrange("p (j m u) -> p j m u", j=NT, u=U))
 
-        for words, plane, passes in ((s1[0][:, 0], idle_scales[:], 18), (w1[0], s2[:, 0, :P], 2)):
+        for words, plane, passes in ((s1[:, 0], idle_scales[:], 18), (w1[0], s2[:, 0, :P], 2)):
             for i in range(passes):
                 nc.tensor.matmul_mx(bank[7][:, :C], lhsT=words[:, : 2 * P].bitcast(FP4X4), lhsT_scale=plane, rhs=idle_codes[:].bitcast(FP8X4), rhs_scale=idle_scales[:], start=True, stop=True)
         for e in range(E):
             gather_pairs(0, e)
         for c in range(2):
             gather_rounded(c, 0)
+        round_pairs(x_cd[:, :, :SECOND_SPLIT], 1, 0, False)
         for e in range(1, E):
             gather_pairs(1, e)
             quantize_slots(e - 1)

@@ -42,7 +42,9 @@ def tile_moe_eps_glu_silu_kernel(tc, xT, w1_words, w1_scales, w3_words, w3_scale
         s3 = sbuf("s3", [E, H], U8)
         s2 = sbuf("s2", [E * HP, N], U8)
         x_pairs = [sbuf("x_pairs%d" % u, [T, 2], BF16) for u in range(2)]
-        slots = [sbuf("slots%d" % e, [C, 2], U32) for e in range(E)]
+        picked_pairs = sbuf("picked_pairs", [2, E * C], U32)
+        slots_first = sbuf("slots_first", [C, 2], U32)
+        slots_rest = sbuf("slots_rest", [LAST * C, 2], U32)
         slot_codes = [sbuf("slot_codes%d" % e, [C], U32) for e in range(E)]
         slot_scales = [sbuf("slot_scales%d" % e, [C], U8) for e in range(E)]
         gate = [sbuf("gate%d" % n, [2, P, 2], F32, "second_words" if n == 0 else None) for n in range(UNITS)]
@@ -55,9 +57,9 @@ def tile_moe_eps_glu_silu_kernel(tc, xT, w1_words, w1_scales, w3_words, w3_scale
         last_codes = [sbuf("last_codes%d" % s, [1, C], U32) for s in range(HP)]
         last_scales = [sbuf("last_scales%d" % s, [1, C], U8) for s in range(HP)]
         ident = sbuf("ident", [P], F32)
-        warm_in = sbuf("warm_in", [1], F32, "early_words")
+        warm_in = sbuf("warm_in", [1], F32)
         warm_out = sbuf("warm_out", [1], F32)
-        idle_bf = sbuf("idle_bf", [4 * C], BF16, "x_second")
+        idle_bf = sbuf("idle_bf", [4 * C], BF16)
         idle_codes = sbuf("idle_codes", [C], U32)
         idle_scales = sbuf("idle_scales", [C], U8)
         staged = sbuf("staged", [NT, R, E, U], F32)
@@ -73,11 +75,11 @@ def tile_moe_eps_glu_silu_kernel(tc, xT, w1_words, w1_scales, w3_words, w3_scale
 
         nc.vector.memset(warm_in[:], 0.0)
         nc.scalar.activation(warm_out[:], warm_in[:], ACT.Silu)
-        nc.vector.memset(idle_bf[:].bitcast(I32), 0)
         clear(nc.vector, s1)
+        clear(nc.vector, s3)
+        nc.vector.memset(idle_bf[:].bitcast(I32), 0)
+        clear(nc.vector, s2)
         nc.vector.quantize_mx(out=idle_codes[:].bitcast(FP8X4), scales=idle_scales[:], in_=idle_bf[:])
-        for plane in (s3, s2):
-            clear(nc.vector, plane)
         make_identity(nc, ident[:])
 
         def load_words(view, words):
@@ -92,14 +94,14 @@ def tile_moe_eps_glu_silu_kernel(tc, xT, w1_words, w1_scales, w3_words, w3_scale
                 nc.vector.tensor_copy(dst, src)
 
         x_ab = sbuf("x_ab", [2, T], F32, "later_words")
-        x_cd = sbuf("x_cd", [2, T], F32, "x_second")
-        early = sbuf("early", [2 * H], U8, "early_words")
+        x_cd = sbuf("x_cd", [2, T], F32)
+        early = sbuf("early", [2 * H], U8)
         row_pairs = xT.rearrange("(p u c) t -> u p c t", u=2, c=2)
         nc.sync.dma_start(x_ab[:], row_pairs[0])
         nc.sync.dma_start(offsets[:], offs)
-        load_scales(nc.sync, s1, w1_scales, 0, E)
         nc.sync.dma_start(x_cd[:], row_pairs[1])
         load_words(early[:], w1_words[0, 0])
+        load_scales(nc.sync, s1, w1_scales, 0, E)
         load_scales(nc.sync, s3, w3_scales, 0, E)
         round_pairs(x_ab[:, :, :FIRST_SPLIT], 0, 0, False)
         round_pairs(x_ab[:, :, FIRST_SPLIT:], 0, FIRST_SPLIT, True)
@@ -114,18 +116,16 @@ def tile_moe_eps_glu_silu_kernel(tc, xT, w1_words, w1_scales, w3_words, w3_scale
         p1 = [s1[:, e] for e in range(E)]
         p3 = [s3[:, e] for e in range(E)]
 
-        def listed(e):
-            return offsets[:, e * C // 16 : (e + 1) * C // 16]
+        def listed(lo, hi):
+            return offsets[:, lo * C // 16 : hi * C // 16]
 
-        def gather_pairs(u, e):
+        def gather_pairs(u, lo):
             window = x_pairs[u][:].rearrange("p t c -> p (t c)").bitcast(U32)
-            nc.vector.tensor_copy(slots[e][:, :, u], window.indirect(listed(e)))
+            nc.vector.tensor_copy(picked_pairs[:, u, lo * C :], window.indirect(listed(lo, E)))
 
         def slot_values(e):
-            return slots[e][:].rearrange("p c u -> p (c u)").bitcast(BF16)
-
-        def gather_rounded(c, e):
-            nc.vector.tensor_copy(slot_values(e).rearrange("p (c j) -> p c j", j=4)[:, :, 2 + c], x_cd[:, c].indirect(listed(e)))
+            words = slots_first[:] if e == 0 else slots_rest[:, (e - 1) * C : e * C]
+            return words.rearrange("p c u -> p (c u)").bitcast(BF16)
 
         def quantize_slots(e):
             nc.vector.quantize_mx(out=slot_codes[e][:].bitcast(FP8X4), scales=slot_scales[e][:], in_=slot_values(e))
@@ -206,18 +206,20 @@ def tile_moe_eps_glu_silu_kernel(tc, xT, w1_words, w1_scales, w3_words, w3_scale
         def unload_y(e, on_scalar):
             copy_on(on_scalar, staged[:, :, :, e, :], y_bank[e][:].rearrange("p (j m u) -> p j m u", j=NT, u=U))
 
-        for words, plane, passes in ((s1[:, 0], idle_scales[:], 18), (w1[0], s2[:, 0, :P], 2)):
-            for i in range(passes):
-                nc.tensor.matmul_mx(bank[7][:, :C], lhsT=words[:, : 2 * P].bitcast(FP4X4), lhsT_scale=plane, rhs=idle_codes[:].bitcast(FP8X4), rhs_scale=idle_scales[:], start=True, stop=True)
-        for e in range(E):
-            gather_pairs(0, e)
+        for i in range(9):
+            nc.tensor.matmul_mx(bank[7][:, :C], lhsT=w1[0][:, : 2 * P].bitcast(FP4X4), lhsT_scale=s2[:, 0, :P], rhs=idle_codes[:].bitcast(FP8X4), rhs_scale=idle_scales[:], start=True, stop=True)
+        gather_pairs(0, 0)
+        nc.vector.tensor_copy(slots_first[:].bitcast(I32)[:, :, 0], picked_pairs[:, 0, :C].bitcast(I32))
+        picked_rows = picked_pairs[:, 1, C : 3 * C].bitcast(F32).rearrange("p (j c) -> p j c", j=2)
         for c in range(2):
-            gather_rounded(c, 0)
+            nc.vector.tensor_copy(picked_rows[:, c], x_cd[:, c].indirect(listed(0, 1)))
+        nc.vector.tensor_copy(slot_values(0).rearrange("p (c j) -> p c j", j=4)[:, :, 2:], picked_rows.rearrange("p j c -> p c j"))
         round_pairs(x_cd[:, :, :SECOND_SPLIT], 1, 0, False)
+        quantize_slots(0)
+        gather_pairs(1, 1)
+        nc.vector.tensor_copy(slots_rest[:].bitcast(I32), picked_pairs[:, :, C:].bitcast(I32).rearrange("p u c -> p c u"))
         for e in range(1, E):
-            gather_pairs(1, e)
-            quantize_slots(e - 1)
-        quantize_slots(LAST)
+            quantize_slots(e)
         load_scales(nc.sync, s2, w2_scales, 0, E * HP)
 
         for e in range(LAST):

@@ -24,8 +24,8 @@ NT = N // P
 U = C // R
 UNITS = E * HP
 LAST = E - 1
-FIRST_SPLIT = 672
-SECOND_SPLIT = 256
+SHARED = 672
+WARM_PASSES = 5
 
 
 def tile_moe_eps_glu_silu_kernel(tc, xT, w1_words, w1_scales, w3_words, w3_scales, w2_words, w2_scales, offs, out):
@@ -38,16 +38,12 @@ def tile_moe_eps_glu_silu_kernel(tc, xT, w1_words, w1_scales, w3_words, w3_scale
             return keep.tile([P] + shape, dtype, name=name, tag=tag or name, align_bytes=64)
 
         offsets = keep.tile([P, E * C // 16], U16, name="offsets")
-        s1 = sbuf("s1", [E, H], U8)
-        s3 = sbuf("s3", [E, H], U8)
-        s2 = sbuf("s2", [E * HP, N], U8)
         x_pairs = [sbuf("x_pairs%d" % u, [T, 2], BF16) for u in range(2)]
-        picked_pairs = sbuf("picked_pairs", [2, E * C], U32)
-        slots_first = sbuf("slots_first", [C, 2], U32)
-        slots_rest = sbuf("slots_rest", [LAST * C, 2], U32)
+        picked = [sbuf("picked_first", [2, C], U32), sbuf("picked_rest", [2, LAST * C], U32)]
+        slots = [sbuf("slots_first", [C, 2], U32), sbuf("slots_rest", [LAST * C, 2], U32)]
         slot_codes = [sbuf("slot_codes%d" % e, [C], U32) for e in range(E)]
         slot_scales = [sbuf("slot_scales%d" % e, [C], U8) for e in range(E)]
-        gate = [sbuf("gate%d" % n, [2, P, 2], F32, "second_words" if n == 0 else None) for n in range(UNITS)]
+        gate = [sbuf("gate%d" % n, [2, P, 2], F32) for n in range(UNITS)]
         h = [sbuf("h%d" % n, [2, P, 2], BF16) for n in range(UNITS - 1)]
         h_last = [sbuf("h_last%d" % u, [P, 2], BF16) for u in range(2)]
         h_turned = [sbuf("h_turned%d" % e, [HP, C, 2], F32) for e in range(LAST)]
@@ -59,76 +55,84 @@ def tile_moe_eps_glu_silu_kernel(tc, xT, w1_words, w1_scales, w3_words, w3_scale
         ident = sbuf("ident", [P], F32)
         warm_in = sbuf("warm_in", [1], F32)
         warm_out = sbuf("warm_out", [1], F32)
-        idle_bf = sbuf("idle_bf", [4 * C], BF16)
-        idle_codes = sbuf("idle_codes", [C], U32)
         idle_scales = sbuf("idle_scales", [C], U8)
         staged = sbuf("staged", [NT, R, E, U], F32)
         bank = [psum.tile([P, PASS], F32, name="bank%d" % i) for i in range(8)]
 
-        def clear(engine, plane):
-            engine.memset(plane[:].rearrange("p e b -> p (e b)").bitcast(I32), 0)
+        def clear(plane):
+            nc.vector.memset(plane[:].rearrange("p e b -> p (e b)").bitcast(I32), 0)
 
-        def load_scales(queue, plane, scales, lo, hi):
+        def load_scales(plane, scales, lo, hi):
             rows = scales.rearrange("e s (q r) n -> r q (e s) n", r=4)
             for r in range(4):
-                queue.dma_start(plane[r:P:32].bitcast(I32), rows[r][:, lo:hi, :].bitcast(I32))
-
-        nc.vector.memset(warm_in[:], 0.0)
-        nc.scalar.activation(warm_out[:], warm_in[:], ACT.Silu)
-        clear(nc.vector, s1)
-        clear(nc.vector, s3)
-        nc.vector.memset(idle_bf[:].bitcast(I32), 0)
-        clear(nc.vector, s2)
-        nc.vector.quantize_mx(out=idle_codes[:].bitcast(FP8X4), scales=idle_scales[:], in_=idle_bf[:])
-        make_identity(nc, ident[:])
+                nc.sync.dma_start(plane[r:P:32].bitcast(I32), rows[r][:, lo:hi, :].bitcast(I32))
 
         def load_words(view, words):
             nc.sync.dma_start(view.bitcast(I32), words.bitcast(I32))
 
-        def round_pairs(raw, u, lo, on_scalar):
-            src = raw.rearrange("p c t -> p t c")
-            dst = x_pairs[u][:, lo : lo + raw.shape[2], :]
-            if on_scalar:
-                nc.scalar.activation(dst, src, ACT.Copy)
-            else:
-                nc.vector.tensor_copy(dst, src)
+        def round_pairs(u):
+            src = raw[u][:].rearrange("p c t -> p t c")
+            nc.vector.tensor_copy(x_pairs[u][:, :SHARED], src[:, :SHARED])
+            nc.scalar.activation(x_pairs[u][:, SHARED:], src[:, SHARED:], ACT.Copy)
 
-        x_ab = sbuf("x_ab", [2, T], F32, "later_words")
-        x_cd = sbuf("x_cd", [2, T], F32)
-        early = sbuf("early", [2 * H], U8)
-        row_pairs = xT.rearrange("(p u c) t -> u p c t", u=2, c=2)
-        nc.sync.dma_start(x_ab[:], row_pairs[0])
-        nc.sync.dma_start(offsets[:], offs)
-        nc.sync.dma_start(x_cd[:], row_pairs[1])
-        load_words(early[:], w1_words[0, 0])
-        load_scales(nc.sync, s1, w1_scales, 0, E)
-        load_scales(nc.sync, s3, w3_scales, 0, E)
-        round_pairs(x_ab[:, :, :FIRST_SPLIT], 0, 0, False)
-        round_pairs(x_ab[:, :, FIRST_SPLIT:], 0, FIRST_SPLIT, True)
-        later = sbuf("later", [2 * E - 1, 2 * H], U8, "later_words")
-        load_words(later[:, 0], w3_words[0, 0])
-        for e in range(1, E):
-            load_words(later[:, 2 * e - 1], w1_words[e, 0])
-            load_words(later[:, 2 * e], w3_words[e, 0])
-        round_pairs(x_cd[:, :, SECOND_SPLIT:], 1, SECOND_SPLIT, True)
-        w1 = [early[:]] + [later[:, 2 * e - 1] for e in range(1, E)]
-        w3 = [later[:, 2 * e] for e in range(E)]
-        p1 = [s1[:, e] for e in range(E)]
-        p3 = [s3[:, e] for e in range(E)]
-
-        def listed(lo, hi):
-            return offsets[:, lo * C // 16 : hi * C // 16]
-
-        def gather_pairs(u, lo):
+        def gather_pairs(g, u):
             window = x_pairs[u][:].rearrange("p t c -> p (t c)").bitcast(U32)
-            nc.vector.tensor_copy(picked_pairs[:, u, lo * C :], window.indirect(listed(lo, E)))
+            lo, hi = ((0, 1), (1, E))[g]
+            nc.vector.tensor_copy(picked[g][:, u], window.indirect(offsets[:, lo * C // 16 : hi * C // 16]))
 
-        def slot_values(e):
-            words = slots_first[:] if e == 0 else slots_rest[:, (e - 1) * C : e * C]
-            return words.rearrange("p c u -> p (c u)").bitcast(BF16)
+        def weave(g):
+            nc.scalar.copy(slots[g][:], picked[g][:].rearrange("p u c -> p c u"))
 
         def quantize_slots(e):
-            nc.vector.quantize_mx(out=slot_codes[e][:].bitcast(FP8X4), scales=slot_scales[e][:], in_=slot_values(e))
+            words = slots[0][:] if e == 0 else slots[1][:, (e - 1) * C : e * C]
+            nc.vector.quantize_mx(out=slot_codes[e][:].bitcast(FP8X4), scales=slot_scales[e][:], in_=words.rearrange("p c u -> p (c u)").bitcast(BF16))
+
+        s1 = sbuf("s1", [E, H], U8)
+        s3 = sbuf("s3", [E, H], U8)
+        s2 = sbuf("s2", [E * HP, N], U8)
+        nc.vector.memset(warm_in[:], 0.0)
+        nc.scalar.activation(warm_out[:], warm_in[:], ACT.Silu)
+        for plane in (s1, s3, s2):
+            clear(plane)
+        make_identity(nc, ident[:])
+
+        raw = [sbuf("raw0", [2, T], F32, "after_raw0"), sbuf("raw1", [2, T], F32)]
+        row_pairs = xT.rearrange("(p u c) t -> u p c t", u=2, c=2)
+        nc.sync.dma_start(raw[0][:], row_pairs[0])
+        nc.sync.dma_start(offsets[:], offs)
+        nc.sync.dma_start(raw[1][:], row_pairs[1])
+        w1 = [sbuf("w1_%d" % e, [2 * H], U8) for e in range(E)]
+        w3 = [sbuf("w3_%d" % e, [2 * H], U8) for e in range(E)]
+        load_words(w1[0][:], w1_words[0, 0])
+        load_scales(s1, w1_scales, 0, E)
+        load_scales(s3, w3_scales, 0, E)
+        load_words(w3[0][:], w3_words[0, 0])
+        for e in range(1, E):
+            load_words(w1[e][:], w1_words[e, 0])
+            load_words(w3[e][:], w3_words[e, 0])
+
+        round_pairs(0)
+        idle_codes = sbuf("idle_codes", [C], U32, "after_raw0")
+        zeros = s2[:, :2].rearrange("p e n -> p (e n)")
+        nc.vector.quantize_mx(out=idle_codes[:].bitcast(FP8X4), scales=idle_scales[:], in_=zeros.bitcast(BF16))
+        for i in range(WARM_PASSES):
+            nc.tensor.matmul_mx(bank[7][:], lhsT=idle_codes[:].bitcast(FP8X4), lhsT_scale=idle_scales[:], rhs=zeros.bitcast(FP4X4), rhs_scale=s2[:, 2], start=True, stop=True)
+        for g in range(2):
+            gather_pairs(g, 0)
+        round_pairs(1)
+        for g in range(2):
+            gather_pairs(g, 1)
+            weave(g)
+        for e in range(E):
+            quantize_slots(e)
+
+        load_scales(s2, w2_scales, 0, E * HP)
+        w2_early = sbuf("w2_early", [2, HP, 2 * N], U8)
+        w2_late = sbuf("w2_late", [2, HP, 2 * N], U8)
+        for e in range(2):
+            load_words(w2_early[:, e], w2_words[e].rearrange("s p n -> p s n"))
+        load_words(w2_late[:].rearrange("p e s n -> p (e s) n"), w2_words[2:].rearrange("e s p n -> p (e s) n"))
+        w2 = [w2_early[:, 0], w2_early[:, 1], w2_late[:, 0], w2_late[:, 1]]
 
         def product(acc, e, s, words, plane):
             nc.tensor.matmul_mx(
@@ -136,7 +140,7 @@ def tile_moe_eps_glu_silu_kernel(tc, xT, w1_words, w1_scales, w3_words, w3_scale
                 lhsT=slot_codes[e][:].bitcast(FP8X4),
                 lhsT_scale=slot_scales[e][:],
                 rhs=words[e][:, 2 * PASS * s : 2 * PASS * (s + 1)].bitcast(FP4X4),
-                rhs_scale=plane[e][:, PASS * s : PASS * (s + 1)],
+                rhs_scale=plane[:, e, PASS * s : PASS * (s + 1)],
                 start=True,
                 stop=True,
             )
@@ -157,7 +161,7 @@ def tile_moe_eps_glu_silu_kernel(tc, xT, w1_words, w1_scales, w3_words, w3_scale
         def second(acc, e, j, s, codes, scales):
             nc.tensor.matmul_mx(
                 acc,
-                lhsT=w2[:, e, s, 2 * P * j : 2 * P * (j + 1)].bitcast(FP4X4),
+                lhsT=w2[e][:, s, 2 * P * j : 2 * P * (j + 1)].bitcast(FP4X4),
                 lhsT_scale=s2[:, e * HP + s, P * j : P * (j + 1)],
                 rhs=codes.bitcast(FP8X4),
                 rhs_scale=scales,
@@ -171,18 +175,20 @@ def tile_moe_eps_glu_silu_kernel(tc, xT, w1_words, w1_scales, w3_words, w3_scale
             else:
                 nc.vector.tensor_copy(dst, src)
 
-        a_bank = [bank[i] for i in (0, 1, 4, 5, 0, 1, 5, 0)]
+        a_bank = [bank[i] for i in (0, 1, 4, 5, 0, 1, 4, 5)]
         b_bank = [bank[i] for i in (2, 3, 6, 7, 2, 3, 6, 7)]
-        turn_bank = [bank[i] for i in (4, 1, 2)]
-        last_turn_bank = [bank[i] for i in (5, 3)]
-        y_bank = [bank[i] for i in (4, 6, 7)]
-        last_y_bank = [bank[i] for i in (0, 1, 2, 5)]
+        turn_bank = [bank[i] for i in (4, 5, 2)]
+        last_turn_bank = [bank[i] for i in (3, 1)]
+        y_bank = [bank[i] for i in (0, 1)]
+        late_bank = [bank[i] for i in (6, 7, 4, 5)]
 
-        def products(e):
+        def firsts(e):
             for s in range(HP):
-                product(a_bank[HP * e + s], e, s, w1, p1)
+                product(a_bank[HP * e + s], e, s, w1, s1)
+
+        def thirds(e):
             for s in range(HP):
-                product(b_bank[HP * e + s], e, s, w3, p3)
+                product(b_bank[HP * e + s], e, s, w3, s3)
 
         def silu(n):
             nc.scalar.activation(gate[n][:], by_pairs(a_bank[n]), ACT.Silu)
@@ -198,6 +204,12 @@ def tile_moe_eps_glu_silu_kernel(tc, xT, w1_words, w1_scales, w3_words, w3_scale
         def unload_turned(on_scalar, source, lo, hi, turned):
             copy_on(on_scalar, turned[:], source[:].rearrange("p (s u c) -> p s c u", s=HP, u=2)[:, lo:hi])
 
+        def unload_expert(e, on_scalar):
+            unload_turned(on_scalar, turn_bank[e], 0, HP, h_turned[e])
+
+        def quantize_expert(e):
+            quantize_hidden(h_turned[e], h_codes[e], h_scales[e])
+
         def second_layer(e):
             for j in range(NT):
                 for s in range(HP):
@@ -206,64 +218,39 @@ def tile_moe_eps_glu_silu_kernel(tc, xT, w1_words, w1_scales, w3_words, w3_scale
         def unload_y(e, on_scalar):
             copy_on(on_scalar, staged[:, :, :, e, :], y_bank[e][:].rearrange("p (j m u) -> p j m u", j=NT, u=U))
 
-        for i in range(9):
-            nc.tensor.matmul_mx(bank[7][:, :C], lhsT=w1[0][:, : 2 * P].bitcast(FP4X4), lhsT_scale=s2[:, 0, :P], rhs=idle_codes[:].bitcast(FP8X4), rhs_scale=idle_scales[:], start=True, stop=True)
-        gather_pairs(0, 0)
-        nc.vector.tensor_copy(slots_first[:].bitcast(I32)[:, :, 0], picked_pairs[:, 0, :C].bitcast(I32))
-        picked_rows = picked_pairs[:, 1, C : 3 * C].bitcast(F32).rearrange("p (j c) -> p j c", j=2)
-        for c in range(2):
-            nc.vector.tensor_copy(picked_rows[:, c], x_cd[:, c].indirect(listed(0, 1)))
-        nc.vector.tensor_copy(slot_values(0).rearrange("p (c j) -> p c j", j=4)[:, :, 2:], picked_rows.rearrange("p j c -> p c j"))
-        round_pairs(x_cd[:, :, :SECOND_SPLIT], 1, 0, False)
-        quantize_slots(0)
-        gather_pairs(1, 1)
-        nc.vector.tensor_copy(slots_rest[:].bitcast(I32), picked_pairs[:, :, C:].bitcast(I32).rearrange("p u c -> p c u"))
-        for e in range(1, E):
-            quantize_slots(e)
-        load_scales(nc.sync, s2, w2_scales, 0, E * HP)
-
-        for e in range(LAST):
-            products(e)
-            for s in range(HP):
-                silu(HP * e + s)
-                gated(HP * e + s)
-        w2 = sbuf("w2", [E, HP, 2 * N], U8, "second_words")
-        for e in range(E):
-            load_words(w2[:, e], w2_words[e].rearrange("s p n -> p s n"))
-        turn_expert(0)
-        products(LAST)
-        unload_turned(True, turn_bank[0], 0, HP, h_turned[0])
         n = UNITS - 1
-        silu(n - 1)
-        quantize_hidden(h_turned[0], h_codes[0], h_scales[0])
-        gated(n - 1)
+        for e in range(E):
+            firsts(e)
+            thirds(e)
+            silu(HP * e)
+            gated(HP * e)
+            if e < LAST:
+                silu(HP * e + 1)
+                gated(HP * e + 1)
         for u in range(2):
             nc.scalar.activation(gate[n][:, u], by_pairs(a_bank[n])[:, u], ACT.Silu)
-        turn_expert(1)
-        turn_expert(2)
-        for u in range(2):
             nc.vector.tensor_tensor(h_last[u][:], by_pairs(b_bank[n])[:, u], gate[n][:, u], MULT)
-        for e in (1, 2):
-            unload_turned(True, turn_bank[e], 0, HP, h_turned[e])
-        second_layer(0)
+        for e in range(LAST):
+            turn_expert(e)
+            unload_expert(e, True)
         for u in range(2):
             turn(h[n - 1][:, u], last_turn_bank[0], 0, u)
         for u in range(2):
-            turn(h_last[u][:], last_turn_bank[1], 1, u)
-        for e in (1, 2):
-            quantize_hidden(h_turned[e], h_codes[e], h_scales[e])
-        unload_y(0, True)
-        for s in range(HP):
-            unload_turned(s == 1, last_turn_bank[s], s, s + 1, last_turned[s])
+            turn(h_last[u][:], last_turn_bank[1], 0, u)
+        quantize_expert(0)
+        unload_turned(False, last_turn_bank[0], 0, 1, last_turned[0])
+        unload_turned(True, last_turn_bank[1], 0, 1, last_turned[1])
+        quantize_expert(1)
+        quantize_expert(2)
         for s in range(HP):
             quantize_hidden(last_turned[s], last_codes[s], last_scales[s])
-        second_layer(1)
-        second_layer(2)
-        unload_y(1, False)
-        unload_y(2, True)
+        for e in range(2):
+            second_layer(e)
+            unload_y(e, e == 0)
         for j in range(NT):
             for s in range(HP):
-                second(last_y_bank[j][:, :C], LAST, j, s, last_codes[s][:, 0], last_scales[s][:, 0])
-        for j in range(NT):
-            copy_on(j % 2 == 1, staged[:, j, :, LAST, :], last_y_bank[j][:, :C].rearrange("p (m u) -> p m u", u=U))
+                second(late_bank[j][:, :C], 2, j, s, h_codes[2][:, s], h_scales[2][:, s])
+            for s in range(HP):
+                second(late_bank[j][:, C : 2 * C], LAST, j, s, last_codes[s][:, 0], last_scales[s][:, 0])
+            copy_on(j % 2 == 0, staged[:, j, :, 2:, :], late_bank[j][:, : 2 * C].rearrange("p (e m u) -> p m e u", e=2, u=U))
             nc.sync.dma_start(out[P * j : P * (j + 1), :], staged[:, j].rearrange("p m e u -> p (m e u)"))

@@ -127,12 +127,16 @@ def tile_moe_eps_glu_silu_kernel(tc, xT, w1_words, w1_scales, w3_words, w3_scale
             quantize_slots(e)
 
         load_scales(s2, w2_scales, 0, E * HP)
-        w2_early = sbuf("w2_early", [2, HP, 2 * N], U8)
-        w2_late = sbuf("w2_late", [2, HP, 2 * N], U8)
-        for e in range(2):
-            load_words(w2_early[:, e], w2_words[e].rearrange("s p n -> p s n"))
-        load_words(w2_late[:].rearrange("p e s n -> p (e s) n"), w2_words[2:].rearrange("e s p n -> p (e s) n"))
-        w2 = [w2_early[:, 0], w2_early[:, 1], w2_late[:, 0], w2_late[:, 1]]
+        w2_first = sbuf("w2_first", [HP, 2 * N], U8)
+        load_words(w2_first[:], w2_words[0].rearrange("s p n -> p s n"))
+        w2_rest = [sbuf("w2_rest%d" % half, [LAST * HP, N], U8) for half in range(2)]
+        for half in range(2):
+            load_words(w2_rest[half][:], w2_words[1:].rearrange("e s p n -> p (e s) n")[:, :, half * N : (half + 1) * N])
+
+        def second_words(e, j, s):
+            if e == 0:
+                return w2_first[:, s, 2 * P * j : 2 * P * (j + 1)]
+            return w2_rest[j // 2][:, (e - 1) * HP + s, 2 * P * (j % 2) : 2 * P * (j % 2 + 1)]
 
         def product(acc, e, s, words, plane):
             nc.tensor.matmul_mx(
@@ -161,7 +165,7 @@ def tile_moe_eps_glu_silu_kernel(tc, xT, w1_words, w1_scales, w3_words, w3_scale
         def second(acc, e, j, s, codes, scales):
             nc.tensor.matmul_mx(
                 acc,
-                lhsT=w2[e][:, s, 2 * P * j : 2 * P * (j + 1)].bitcast(FP4X4),
+                lhsT=second_words(e, j, s).bitcast(FP4X4),
                 lhsT_scale=s2[:, e * HP + s, P * j : P * (j + 1)],
                 rhs=codes.bitcast(FP8X4),
                 rhs_scale=scales,
@@ -179,7 +183,7 @@ def tile_moe_eps_glu_silu_kernel(tc, xT, w1_words, w1_scales, w3_words, w3_scale
         b_bank = [bank[i] for i in (2, 3, 6, 7, 2, 3, 6, 7)]
         turn_bank = [bank[i] for i in (4, 5, 2)]
         last_turn_bank = [bank[i] for i in (3, 1)]
-        y_bank = [bank[i] for i in (0, 1)]
+        y_bank = [bank[0]]
         late_bank = [bank[i] for i in (6, 7, 4, 5)]
 
         def firsts(e):
@@ -244,13 +248,13 @@ def tile_moe_eps_glu_silu_kernel(tc, xT, w1_words, w1_scales, w3_words, w3_scale
         quantize_expert(2)
         for s in range(HP):
             quantize_hidden(last_turned[s], last_codes[s], last_scales[s])
-        for e in range(2):
-            second_layer(e)
-            unload_y(e, e == 0)
+        second_layer(0)
+        unload_y(0, True)
         for j in range(NT):
+            for e in range(1, LAST):
+                for s in range(HP):
+                    second(late_bank[j][:, (e - 1) * C : e * C], e, j, s, h_codes[e][:, s], h_scales[e][:, s])
             for s in range(HP):
-                second(late_bank[j][:, :C], 2, j, s, h_codes[2][:, s], h_scales[2][:, s])
-            for s in range(HP):
-                second(late_bank[j][:, C : 2 * C], LAST, j, s, last_codes[s][:, 0], last_scales[s][:, 0])
-            copy_on(j % 2 == 0, staged[:, j, :, 2:, :], late_bank[j][:, : 2 * C].rearrange("p (e m u) -> p m e u", e=2, u=U))
+                second(late_bank[j][:, 2 * C : 3 * C], LAST, j, s, last_codes[s][:, 0], last_scales[s][:, 0])
+            copy_on(j % 2 == 1, staged[:, j, :, 1:, :], late_bank[j][:, : LAST * C].rearrange("p (e m u) -> p m e u", e=LAST, u=U))
             nc.sync.dma_start(out[P * j : P * (j + 1), :], staged[:, j].rearrange("p m e u -> p (m e u)"))

@@ -25,7 +25,6 @@ U = C // R
 UNITS = E * HP
 LAST = E - 1
 SHARED = 672
-WARM_PASSES = 5
 
 
 def tile_moe_eps_glu_silu_kernel(tc, xT, w1_words, w1_scales, w3_words, w3_scales, w2_words, w2_scales, offs, out):
@@ -55,7 +54,6 @@ def tile_moe_eps_glu_silu_kernel(tc, xT, w1_words, w1_scales, w3_words, w3_scale
         ident = sbuf("ident", [P], F32)
         warm_in = sbuf("warm_in", [1], F32)
         warm_out = sbuf("warm_out", [1], F32)
-        idle_scales = sbuf("idle_scales", [C], U8)
         staged = sbuf("staged", [NT, R, E, U], F32)
         bank = [psum.tile([P, PASS], F32, name="bank%d" % i) for i in range(8)]
 
@@ -96,7 +94,7 @@ def tile_moe_eps_glu_silu_kernel(tc, xT, w1_words, w1_scales, w3_words, w3_scale
             clear(plane)
         make_identity(nc, ident[:])
 
-        raw = [sbuf("raw0", [2, T], F32, "after_raw0"), sbuf("raw1", [2, T], F32)]
+        raw = [sbuf("raw0", [2, T], F32), sbuf("raw1", [2, T], F32)]
         row_pairs = xT.rearrange("(p u c) t -> u p c t", u=2, c=2)
         nc.sync.dma_start(raw[0][:], row_pairs[0])
         nc.sync.dma_start(offsets[:], offs)
@@ -112,11 +110,6 @@ def tile_moe_eps_glu_silu_kernel(tc, xT, w1_words, w1_scales, w3_words, w3_scale
             load_words(w3[e][:], w3_words[e, 0])
 
         round_pairs(0)
-        idle_codes = sbuf("idle_codes", [C], U32, "after_raw0")
-        zeros = s2[:, :2].rearrange("p e n -> p (e n)")
-        nc.vector.quantize_mx(out=idle_codes[:].bitcast(FP8X4), scales=idle_scales[:], in_=zeros.bitcast(BF16))
-        for i in range(WARM_PASSES):
-            nc.tensor.matmul_mx(bank[7][:], lhsT=idle_codes[:].bitcast(FP8X4), lhsT_scale=idle_scales[:], rhs=zeros.bitcast(FP4X4), rhs_scale=s2[:, 2], start=True, stop=True)
         for g in range(2):
             gather_pairs(g, 0)
         round_pairs(1)

@@ -25,6 +25,8 @@ U = C // R
 UNITS = E * HP
 LAST = E - 1
 SHARED = 672
+WARM_PASSES = 6
+WARM_COLUMNS = 256
 
 
 def tile_moe_eps_glu_silu_kernel(tc, xT, w1_words, w1_scales, w3_words, w3_scales, w2_words, w2_scales, offs, out):
@@ -60,10 +62,10 @@ def tile_moe_eps_glu_silu_kernel(tc, xT, w1_words, w1_scales, w3_words, w3_scale
         def clear(plane):
             nc.vector.memset(plane[:].rearrange("p e b -> p (e b)").bitcast(I32), 0)
 
-        def load_scales(plane, scales, lo, hi):
+        def load_scales(plane, scales, lo, hi, queue=nc.sync):
             rows = scales.rearrange("e s (q r) n -> r q (e s) n", r=4)
             for r in range(4):
-                nc.sync.dma_start(plane[r:P:32].bitcast(I32), rows[r][:, lo:hi, :].bitcast(I32))
+                queue.dma_start(plane[r:P:32].bitcast(I32), rows[r][:, lo:hi, :].bitcast(I32))
 
         def load_words(view, words):
             nc.sync.dma_start(view.bitcast(I32), words.bitcast(I32))
@@ -112,6 +114,11 @@ def tile_moe_eps_glu_silu_kernel(tc, xT, w1_words, w1_scales, w3_words, w3_scale
         round_pairs(0)
         for g in range(2):
             gather_pairs(g, 0)
+        warm_codes = sbuf("warm_codes", [WARM_COLUMNS], U32)
+        warm_scales = s2[:, 0, :WARM_COLUMNS]
+        nc.vector.quantize_mx(out=warm_codes[:].bitcast(FP8X4), scales=warm_scales, in_=x_pairs[0][:, : 2 * WARM_COLUMNS].rearrange("p t c -> p (t c)"))
+        for i in range(WARM_PASSES):
+            nc.tensor.matmul_mx(bank[7][:, :WARM_COLUMNS], lhsT=warm_codes[:, :C].bitcast(FP8X4), lhsT_scale=warm_scales[:, :C], rhs=w1[0][:, : 2 * WARM_COLUMNS].bitcast(FP4X4), rhs_scale=warm_scales, start=True, stop=True)
         round_pairs(1)
         for g in range(2):
             gather_pairs(g, 1)
@@ -119,7 +126,7 @@ def tile_moe_eps_glu_silu_kernel(tc, xT, w1_words, w1_scales, w3_words, w3_scale
         for e in range(E):
             quantize_slots(e)
 
-        load_scales(s2, w2_scales, 0, E * HP)
+        load_scales(s2, w2_scales, 0, E * HP, nc.gpsimd)
         w2_first = sbuf("w2_first", [HP, 2 * N], U8)
         load_words(w2_first[:], w2_words[0].rearrange("s p n -> p s n"))
         w2_rest = [sbuf("w2_rest%d" % half, [LAST * HP, N], U8) for half in range(2)]
@@ -178,6 +185,7 @@ def tile_moe_eps_glu_silu_kernel(tc, xT, w1_words, w1_scales, w3_words, w3_scale
         last_turn_bank = [bank[i] for i in (3, 1)]
         y_bank = [bank[0]]
         late_bank = [bank[i] for i in (6, 7, 4, 5)]
+        last_bank = [bank[i] for i in (2, 3, 1, 0)]
 
         def firsts(e):
             for s in range(HP):
@@ -229,13 +237,13 @@ def tile_moe_eps_glu_silu_kernel(tc, xT, w1_words, w1_scales, w3_words, w3_scale
             nc.vector.tensor_tensor(h_last[u][:], by_pairs(b_bank[n])[:, u], gate[n][:, u], MULT)
         for e in range(LAST):
             turn_expert(e)
-            unload_expert(e, True)
+            unload_expert(e, e != 1)
         for u in range(2):
             turn(h[n - 1][:, u], last_turn_bank[0], 0, u)
         for u in range(2):
             turn(h_last[u][:], last_turn_bank[1], 0, u)
         quantize_expert(0)
-        unload_turned(False, last_turn_bank[0], 0, 1, last_turned[0])
+        unload_turned(True, last_turn_bank[0], 0, 1, last_turned[0])
         unload_turned(True, last_turn_bank[1], 0, 1, last_turned[1])
         quantize_expert(1)
         quantize_expert(2)
@@ -243,11 +251,18 @@ def tile_moe_eps_glu_silu_kernel(tc, xT, w1_words, w1_scales, w3_words, w3_scale
             quantize_hidden(last_turned[s], last_codes[s], last_scales[s])
         second_layer(0)
         unload_y(0, True)
-        for j in range(NT):
+        def middle_experts(j):
             for e in range(1, LAST):
                 for s in range(HP):
                     second(late_bank[j][:, (e - 1) * C : e * C], e, j, s, h_codes[e][:, s], h_scales[e][:, s])
+            nc.scalar.copy(staged[:, j, :, 1:LAST, :], late_bank[j][:, : 2 * C].rearrange("p (e m u) -> p m e u", e=2, u=U))
+
+        for j in range(NT // 2):
+            middle_experts(j)
+        for j in range(NT):
+            if j >= NT // 2:
+                middle_experts(j)
             for s in range(HP):
-                second(late_bank[j][:, 2 * C : 3 * C], LAST, j, s, last_codes[s][:, 0], last_scales[s][:, 0])
-            copy_on(j % 2 == 1, staged[:, j, :, 1:, :], late_bank[j][:, : LAST * C].rearrange("p (e m u) -> p m e u", e=LAST, u=U))
+                second(last_bank[j][:, :C], LAST, j, s, last_codes[s][:, 0], last_scales[s][:, 0])
+            nc.vector.tensor_copy(staged[:, j, :, LAST, :], last_bank[j][:, :C].rearrange("p (m u) -> p m u", u=U))
             nc.sync.dma_start(out[P * j : P * (j + 1), :], staged[:, j].rearrange("p m e u -> p (m e u)"))

@@ -24,7 +24,8 @@ NT = N // P
 U = C // R
 UNITS = E * HP
 LAST = E - 1
-SHARED = 672
+FIRST_SHARE = 576
+LAST_SHARE = 352
 WARM_PASSES = 6
 WARM_COLUMNS = 256
 
@@ -62,18 +63,21 @@ def tile_moe_eps_glu_silu_kernel(tc, xT, w1_words, w1_scales, w3_words, w3_scale
         def clear(plane):
             nc.vector.memset(plane[:].rearrange("p e b -> p (e b)").bitcast(I32), 0)
 
-        def load_scales(plane, scales, lo, hi, queue=nc.sync):
+        def load_scales(plane, scales, lo, hi, halved=0):
             rows = scales.rearrange("e s (q r) n -> r q (e s) n", r=4)
+            mid = (lo + hi) // 2
             for r in range(4):
-                queue.dma_start(plane[r:P:32].bitcast(I32), rows[r][:, lo:hi, :].bitcast(I32))
+                for a, b in ((lo, mid), (mid, hi)) if r < halved else ((lo, hi),):
+                    nc.sync.dma_start(plane[r:P:32, a:b].bitcast(I32), rows[r][:, a:b, :].bitcast(I32))
 
         def load_words(view, words):
             nc.sync.dma_start(view.bitcast(I32), words.bitcast(I32))
 
-        def round_pairs(u):
-            src = raw[u][:].rearrange("p c t -> p t c")
-            nc.vector.tensor_copy(x_pairs[u][:, :SHARED], src[:, :SHARED])
-            nc.scalar.activation(x_pairs[u][:, SHARED:], src[:, SHARED:], ACT.Copy)
+        def round_pairs(rows, pairs, on_vector):
+            src = rows[:].rearrange("p c t -> p t c")
+            if on_vector:
+                nc.vector.tensor_copy(pairs[:, :on_vector], src[:, :on_vector])
+            nc.scalar.activation(pairs[:, on_vector:], src[:, on_vector:], ACT.Copy)
 
         def gather_pairs(g, u):
             window = x_pairs[u][:].rearrange("p t c -> p (t c)").bitcast(U32)
@@ -96,11 +100,12 @@ def tile_moe_eps_glu_silu_kernel(tc, xT, w1_words, w1_scales, w3_words, w3_scale
             clear(plane)
         make_identity(nc, ident[:])
 
-        raw = [sbuf("raw0", [2, T], F32), sbuf("raw1", [2, T], F32)]
+        raw = [sbuf("raw0", [2, T], F32), sbuf("raw1a", [2, T // 2], F32), sbuf("raw1b", [2, T // 2], F32)]
         row_pairs = xT.rearrange("(p u c) t -> u p c t", u=2, c=2)
         nc.sync.dma_start(raw[0][:], row_pairs[0])
         nc.sync.dma_start(offsets[:], offs)
-        nc.sync.dma_start(raw[1][:], row_pairs[1])
+        nc.sync.dma_start(raw[1][:], row_pairs[1][:, :, : T // 2])
+        nc.sync.dma_start(raw[2][:], row_pairs[1][:, :, T // 2 :])
         w1 = [sbuf("w1_%d" % e, [2 * H], U8) for e in range(E)]
         w3 = [sbuf("w3_%d" % e, [2 * H], U8) for e in range(E)]
         load_words(w1[0][:], w1_words[0, 0])
@@ -111,22 +116,23 @@ def tile_moe_eps_glu_silu_kernel(tc, xT, w1_words, w1_scales, w3_words, w3_scale
             load_words(w1[e][:], w1_words[e, 0])
             load_words(w3[e][:], w3_words[e, 0])
 
-        round_pairs(0)
+        round_pairs(raw[0], x_pairs[0][:], FIRST_SHARE)
         for g in range(2):
             gather_pairs(g, 0)
         warm_codes = sbuf("warm_codes", [WARM_COLUMNS], U32)
-        warm_scales = s2[:, 0, :WARM_COLUMNS]
+        warm_scales = sbuf("warm_scales", [WARM_COLUMNS], U8)[:]
         nc.vector.quantize_mx(out=warm_codes[:].bitcast(FP8X4), scales=warm_scales, in_=x_pairs[0][:, : 2 * WARM_COLUMNS].rearrange("p t c -> p (t c)"))
         for i in range(WARM_PASSES):
             nc.tensor.matmul_mx(bank[7][:, :WARM_COLUMNS], lhsT=warm_codes[:, :C].bitcast(FP8X4), lhsT_scale=warm_scales[:, :C], rhs=w1[0][:, : 2 * WARM_COLUMNS].bitcast(FP4X4), rhs_scale=warm_scales, start=True, stop=True)
-        round_pairs(1)
+        round_pairs(raw[1], x_pairs[1][:, : T // 2], 0)
+        round_pairs(raw[2], x_pairs[1][:, T // 2 :], LAST_SHARE)
         for g in range(2):
             gather_pairs(g, 1)
             weave(g)
         for e in range(E):
             quantize_slots(e)
 
-        load_scales(s2, w2_scales, 0, E * HP, nc.gpsimd)
+        load_scales(s2, w2_scales, 0, E * HP, 2)
         w2_first = sbuf("w2_first", [HP, 2 * N], U8)
         load_words(w2_first[:], w2_words[0].rearrange("s p n -> p s n"))
         w2_rest = [sbuf("w2_rest%d" % half, [LAST * HP, N], U8) for half in range(2)]

@@ -25,7 +25,7 @@ U = C // R
 UNITS = E * HP
 LAST = E - 1
 FIRST_SHARE = 576
-LAST_SHARE = 352
+LAST_SHARE = 672
 WARM_PASSES = 6
 WARM_COLUMNS = 256
 
@@ -63,20 +63,17 @@ def tile_moe_eps_glu_silu_kernel(tc, xT, w1_words, w1_scales, w3_words, w3_scale
         def clear(plane):
             nc.vector.memset(plane[:].rearrange("p e b -> p (e b)").bitcast(I32), 0)
 
-        def load_scales(plane, scales, lo, hi, halved=0):
+        def load_scales(plane, scales):
             rows = scales.rearrange("e s (q r) n -> r q (e s) n", r=4)
-            mid = (lo + hi) // 2
             for r in range(4):
-                for a, b in ((lo, mid), (mid, hi)) if r < halved else ((lo, hi),):
-                    nc.sync.dma_start(plane[r:P:32, a:b].bitcast(I32), rows[r][:, a:b, :].bitcast(I32))
+                nc.sync.dma_start(plane[r:P:32].bitcast(I32), rows[r].bitcast(I32))
 
         def load_words(view, words):
             nc.sync.dma_start(view.bitcast(I32), words.bitcast(I32))
 
         def round_pairs(rows, pairs, on_vector):
             src = rows[:].rearrange("p c t -> p t c")
-            if on_vector:
-                nc.vector.tensor_copy(pairs[:, :on_vector], src[:, :on_vector])
+            nc.vector.tensor_copy(pairs[:, :on_vector], src[:, :on_vector])
             nc.scalar.activation(pairs[:, on_vector:], src[:, on_vector:], ACT.Copy)
 
         def gather_pairs(g, u):
@@ -93,56 +90,57 @@ def tile_moe_eps_glu_silu_kernel(tc, xT, w1_words, w1_scales, w3_words, w3_scale
 
         s1 = sbuf("s1", [E, H], U8)
         s3 = sbuf("s3", [E, H], U8)
-        s2 = sbuf("s2", [E * HP, N], U8)
+        s2 = [sbuf("s2_%d" % half, [E * HP, N // 2], U8) for half in range(2)]
         nc.vector.memset(warm_in[:], 0.0)
         nc.scalar.activation(warm_out[:], warm_in[:], ACT.Silu)
-        for plane in (s1, s3, s2):
+        for plane in [s1, s3] + s2:
             clear(plane)
         make_identity(nc, ident[:])
 
-        raw = [sbuf("raw0", [2, T], F32), sbuf("raw1a", [2, T // 2], F32), sbuf("raw1b", [2, T // 2], F32)]
+        raw = [sbuf("raw%d" % u, [2, T], F32) for u in range(2)]
         row_pairs = xT.rearrange("(p u c) t -> u p c t", u=2, c=2)
         nc.sync.dma_start(raw[0][:], row_pairs[0])
         nc.sync.dma_start(offsets[:], offs)
-        nc.sync.dma_start(raw[1][:], row_pairs[1][:, :, : T // 2])
-        nc.sync.dma_start(raw[2][:], row_pairs[1][:, :, T // 2 :])
+        nc.sync.dma_start(raw[1][:], row_pairs[1])
         w1 = [sbuf("w1_%d" % e, [2 * H], U8) for e in range(E)]
         w3 = [sbuf("w3_%d" % e, [2 * H], U8) for e in range(E)]
         load_words(w1[0][:], w1_words[0, 0])
-        load_scales(s1, w1_scales, 0, E)
-        load_scales(s3, w3_scales, 0, E)
+        load_scales(s1, w1_scales)
+        load_scales(s3, w3_scales)
         load_words(w3[0][:], w3_words[0, 0])
         for e in range(1, E):
             load_words(w1[e][:], w1_words[e, 0])
             load_words(w3[e][:], w3_words[e, 0])
 
         round_pairs(raw[0], x_pairs[0][:], FIRST_SHARE)
+        warm_codes = sbuf("warm_codes", [WARM_COLUMNS], U32)
+        warm_scales = sbuf("warm_scales", [WARM_COLUMNS], U8)
+        nc.vector.quantize_mx(out=warm_codes[:].bitcast(FP8X4), scales=warm_scales[:], in_=x_pairs[0][:, : 2 * WARM_COLUMNS].rearrange("p t c -> p (t c)"))
+        for i in range(WARM_PASSES):
+            nc.tensor.matmul_mx(bank[7][:, :WARM_COLUMNS], lhsT=warm_codes[:, :C].bitcast(FP8X4), lhsT_scale=warm_scales[:, :C], rhs=w1[0][:, : 2 * WARM_COLUMNS].bitcast(FP4X4), rhs_scale=warm_scales[:], start=True, stop=True)
         for g in range(2):
             gather_pairs(g, 0)
-        warm_codes = sbuf("warm_codes", [WARM_COLUMNS], U32)
-        warm_scales = sbuf("warm_scales", [WARM_COLUMNS], U8)[:]
-        nc.vector.quantize_mx(out=warm_codes[:].bitcast(FP8X4), scales=warm_scales, in_=x_pairs[0][:, : 2 * WARM_COLUMNS].rearrange("p t c -> p (t c)"))
-        for i in range(WARM_PASSES):
-            nc.tensor.matmul_mx(bank[7][:, :WARM_COLUMNS], lhsT=warm_codes[:, :C].bitcast(FP8X4), lhsT_scale=warm_scales[:, :C], rhs=w1[0][:, : 2 * WARM_COLUMNS].bitcast(FP4X4), rhs_scale=warm_scales, start=True, stop=True)
-        round_pairs(raw[1], x_pairs[1][:, : T // 2], 0)
-        round_pairs(raw[2], x_pairs[1][:, T // 2 :], LAST_SHARE)
+        round_pairs(raw[1], x_pairs[1][:], LAST_SHARE)
         for g in range(2):
             gather_pairs(g, 1)
             weave(g)
         for e in range(E):
             quantize_slots(e)
 
-        load_scales(s2, w2_scales, 0, E * HP, 2)
-        w2_first = sbuf("w2_first", [HP, 2 * N], U8)
-        load_words(w2_first[:], w2_words[0].rearrange("s p n -> p s n"))
-        w2_rest = [sbuf("w2_rest%d" % half, [LAST * HP, N], U8) for half in range(2)]
+        load_scales(s2[0], w2_scales[:, :, :, : N // 2])
+        w2_whole = [sbuf("w2_whole%d" % e, [HP, 2 * N], U8) for e in range(2)]
+        for e in range(2):
+            load_words(w2_whole[e][:], w2_words[e].rearrange("s p n -> p s n"))
+        w2_half = [sbuf("w2_half%d" % half, [2 * HP, N], U8) for half in range(2)]
         for half in range(2):
-            load_words(w2_rest[half][:], w2_words[1:].rearrange("e s p n -> p (e s) n")[:, :, half * N : (half + 1) * N])
+            if half:
+                load_scales(s2[1], w2_scales[:, :, :, N // 2 :])
+            load_words(w2_half[half][:], w2_words[2:].rearrange("e s p n -> p (e s) n")[:, :, half * N : (half + 1) * N])
 
         def second_words(e, j, s):
-            if e == 0:
-                return w2_first[:, s, 2 * P * j : 2 * P * (j + 1)]
-            return w2_rest[j // 2][:, (e - 1) * HP + s, 2 * P * (j % 2) : 2 * P * (j % 2 + 1)]
+            if e < 2:
+                return w2_whole[e][:, s, 2 * P * j : 2 * P * (j + 1)]
+            return w2_half[j // 2][:, (e - 2) * HP + s, 2 * P * (j % 2) : 2 * P * (j % 2 + 1)]
 
         def product(acc, e, s, words, plane):
             nc.tensor.matmul_mx(
@@ -172,7 +170,7 @@ def tile_moe_eps_glu_silu_kernel(tc, xT, w1_words, w1_scales, w3_words, w3_scale
             nc.tensor.matmul_mx(
                 acc,
                 lhsT=second_words(e, j, s).bitcast(FP4X4),
-                lhsT_scale=s2[:, e * HP + s, P * j : P * (j + 1)],
+                lhsT_scale=s2[j // 2][:, e * HP + s, P * (j % 2) : P * (j % 2 + 1)],
                 rhs=codes.bitcast(FP8X4),
                 rhs_scale=scales,
                 start=(s == 0),
@@ -189,9 +187,8 @@ def tile_moe_eps_glu_silu_kernel(tc, xT, w1_words, w1_scales, w3_words, w3_scale
         b_bank = [bank[i] for i in (2, 3, 6, 7, 2, 3, 6, 7)]
         turn_bank = [bank[i] for i in (4, 5, 2)]
         last_turn_bank = [bank[i] for i in (3, 1)]
-        y_bank = [bank[0]]
-        late_bank = [bank[i] for i in (6, 7, 4, 5)]
-        last_bank = [bank[i] for i in (2, 3, 1, 0)]
+        early_bank = [bank[i] for i in (0, 6)]
+        late_bank = [bank[i] for i in (7, 4, 5, 2)]
 
         def firsts(e):
             for s in range(HP):
@@ -221,14 +218,6 @@ def tile_moe_eps_glu_silu_kernel(tc, xT, w1_words, w1_scales, w3_words, w3_scale
         def quantize_expert(e):
             quantize_hidden(h_turned[e], h_codes[e], h_scales[e])
 
-        def second_layer(e):
-            for j in range(NT):
-                for s in range(HP):
-                    second(y_bank[e][:, j * C : (j + 1) * C], e, j, s, h_codes[e][:, s], h_scales[e][:, s])
-
-        def unload_y(e, on_scalar):
-            copy_on(on_scalar, staged[:, :, :, e, :], y_bank[e][:].rearrange("p (j m u) -> p j m u", j=NT, u=U))
-
         n = UNITS - 1
         for e in range(E):
             firsts(e)
@@ -255,20 +244,18 @@ def tile_moe_eps_glu_silu_kernel(tc, xT, w1_words, w1_scales, w3_words, w3_scale
         quantize_expert(2)
         for s in range(HP):
             quantize_hidden(last_turned[s], last_codes[s], last_scales[s])
-        second_layer(0)
-        unload_y(0, True)
-        def middle_experts(j):
-            for e in range(1, LAST):
+        for half in range(2):
+            tiles = (2 * half, 2 * half + 1)
+            for e in range(2):
+                for j in tiles:
+                    for s in range(HP):
+                        second(early_bank[half][:, (2 * (j % 2) + e) * C : (2 * (j % 2) + e + 1) * C], e, j, s, h_codes[e][:, s], h_scales[e][:, s])
+            for j in tiles:
+                nc.scalar.copy(staged[:, j, :, :2, :], early_bank[half][:, 2 * (j % 2) * C : 2 * (j % 2 + 1) * C].rearrange("p (e m u) -> p m e u", e=2, u=U))
+            for j in tiles:
                 for s in range(HP):
-                    second(late_bank[j][:, (e - 1) * C : e * C], e, j, s, h_codes[e][:, s], h_scales[e][:, s])
-            nc.scalar.copy(staged[:, j, :, 1:LAST, :], late_bank[j][:, : 2 * C].rearrange("p (e m u) -> p m e u", e=2, u=U))
-
-        for j in range(NT // 2):
-            middle_experts(j)
-        for j in range(NT):
-            if j >= NT // 2:
-                middle_experts(j)
-            for s in range(HP):
-                second(last_bank[j][:, :C], LAST, j, s, last_codes[s][:, 0], last_scales[s][:, 0])
-            nc.vector.tensor_copy(staged[:, j, :, LAST, :], last_bank[j][:, :C].rearrange("p (m u) -> p m u", u=U))
-            nc.sync.dma_start(out[P * j : P * (j + 1), :], staged[:, j].rearrange("p m e u -> p (m e u)"))
+                    second(late_bank[j][:, :C], 2, j, s, h_codes[2][:, s], h_scales[2][:, s])
+                for s in range(HP):
+                    second(late_bank[j][:, C : 2 * C], LAST, j, s, last_codes[s][:, 0], last_scales[s][:, 0])
+                nc.vector.tensor_copy(staged[:, j, :, 2:, :], late_bank[j][:, : 2 * C].rearrange("p (e m u) -> p m e u", e=2, u=U))
+                nc.sync.dma_start(out[P * j : P * (j + 1), :], staged[:, j].rearrange("p m e u -> p (m e u)"))

@@ -26,7 +26,7 @@ UNITS = E * HP
 LAST = E - 1
 FIRST_SHARE = 576
 LAST_SHARE = 672
-WARM_PASSES = 6
+WARM_WIDTHS = (256, 256, 256, 256, 256, 256)
 WARM_COLUMNS = 256
 
 
@@ -116,8 +116,8 @@ def tile_moe_eps_glu_silu_kernel(tc, xT, w1_words, w1_scales, w3_words, w3_scale
         warm_codes = sbuf("warm_codes", [WARM_COLUMNS], U32)
         warm_scales = sbuf("warm_scales", [WARM_COLUMNS], U8)
         nc.vector.quantize_mx(out=warm_codes[:].bitcast(FP8X4), scales=warm_scales[:], in_=x_pairs[0][:, : 2 * WARM_COLUMNS].rearrange("p t c -> p (t c)"))
-        for i in range(WARM_PASSES):
-            nc.tensor.matmul_mx(bank[7][:, :WARM_COLUMNS], lhsT=warm_codes[:, :C].bitcast(FP8X4), lhsT_scale=warm_scales[:, :C], rhs=w1[0][:, : 2 * WARM_COLUMNS].bitcast(FP4X4), rhs_scale=warm_scales[:], start=True, stop=True)
+        for width in WARM_WIDTHS:
+            nc.tensor.matmul_mx(bank[7][:, :width], lhsT=warm_codes[:, :C].bitcast(FP8X4), lhsT_scale=warm_scales[:, :C], rhs=w1[0][:, : 2 * width].bitcast(FP4X4), rhs_scale=warm_scales[:, :width], start=True, stop=True)
         for g in range(2):
             gather_pairs(g, 0)
         round_pairs(raw[1], x_pairs[1][:], LAST_SHARE)
@@ -127,20 +127,12 @@ def tile_moe_eps_glu_silu_kernel(tc, xT, w1_words, w1_scales, w3_words, w3_scale
         for e in range(E):
             quantize_slots(e)
 
-        load_scales(s2[0], w2_scales[:, :, :, : N // 2])
-        w2_whole = [sbuf("w2_whole%d" % e, [HP, 2 * N], U8) for e in range(2)]
-        for e in range(2):
-            load_words(w2_whole[e][:], w2_words[e].rearrange("s p n -> p s n"))
-        w2_half = [sbuf("w2_half%d" % half, [2 * HP, N], U8) for half in range(2)]
-        for half in range(2):
-            if half:
-                load_scales(s2[1], w2_scales[:, :, :, N // 2 :])
-            load_words(w2_half[half][:], w2_words[2:].rearrange("e s p n -> p (e s) n")[:, :, half * N : (half + 1) * N])
-
         def second_words(e, j, s):
             if e < 2:
                 return w2_whole[e][:, s, 2 * P * j : 2 * P * (j + 1)]
-            return w2_half[j // 2][:, (e - 2) * HP + s, 2 * P * (j % 2) : 2 * P * (j % 2 + 1)]
+            if j < 2:
+                return w2_upper[:, (e - 2) * HP + s, 2 * P * j : 2 * P * (j + 1)]
+            return w2_tile[j - 2][:, (e - 2) * HP + s]
 
         def product(acc, e, s, words, plane):
             nc.tensor.matmul_mx(
@@ -230,6 +222,18 @@ def tile_moe_eps_glu_silu_kernel(tc, xT, w1_words, w1_scales, w3_words, w3_scale
         for u in range(2):
             nc.scalar.activation(gate[n][:, u], by_pairs(a_bank[n])[:, u], ACT.Silu)
             nc.vector.tensor_tensor(h_last[u][:], by_pairs(b_bank[n])[:, u], gate[n][:, u], MULT)
+        load_scales(s2[0], w2_scales[:, :, :, : N // 2])
+        w2_whole = [sbuf("w2_whole0", [HP, 2 * N], U8, tag="w1_2"), sbuf("w2_whole1", [HP, 2 * N], U8)]
+        for e in range(2):
+            load_words(w2_whole[e][:], w2_words[e].rearrange("s p n -> p s n"))
+        late_rows = w2_words[2:].rearrange("e s p n -> p (e s) n")
+        w2_upper = sbuf("w2_upper", [2 * HP, N], U8)
+        load_words(w2_upper[:], late_rows[:, :, :N])
+        load_scales(s2[1], w2_scales[:, :, :, N // 2 :])
+        w2_tile = [sbuf("w2_tile2", [2 * HP, 2 * P], U8, tag="gate%d" % (UNITS - 1)), sbuf("w2_tile3", [2 * HP, 2 * P], U8)]
+        for j in range(2, NT):
+            load_words(w2_tile[j - 2][:], late_rows[:, :, 2 * P * j : 2 * P * (j + 1)])
+
         for e in range(LAST):
             turn_expert(e)
             unload_expert(e, e != 1)

@@ -237,6 +237,8 @@ def tile_moe_eps_glu_silu_kernel(tc, xT, w1_words, w1_scales, w3_words, w3_scale
         for e in range(LAST):
             turn_expert(e)
             unload_expert(e, e != 1)
+        for s in range(HP):
+            product(b_bank[n - 1], LAST, s, w1, s1)
         for u in range(2):
             turn(h[n - 1][:, u], last_turn_bank[0], 0, u)
         for u in range(2):

@@ -24,9 +24,10 @@ NT = N // P
 U = C // R
 UNITS = E * HP
 LAST = E - 1
+GROUPS = ((0, 1), (1, 2), (2, 4))
 FIRST_SHARE = 576
 LAST_SHARE = 672
-WARM_WIDTHS = (256, 256, 256, 256, 256, 256)
+WARM_WIDTHS = (256, 256, 256, 256, 128, 64)
 WARM_COLUMNS = 256
 
 
@@ -41,10 +42,12 @@ def tile_moe_eps_glu_silu_kernel(tc, xT, w1_words, w1_scales, w3_words, w3_scale
 
         offsets = keep.tile([P, E * C // 16], U16, name="offsets")
         x_pairs = [sbuf("x_pairs%d" % u, [T, 2], BF16) for u in range(2)]
-        picked = [sbuf("picked_first", [2, C], U32), sbuf("picked_rest", [2, LAST * C], U32)]
-        slots = [sbuf("slots_first", [C, 2], U32), sbuf("slots_rest", [LAST * C, 2], U32)]
-        slot_codes = [sbuf("slot_codes%d" % e, [C], U32) for e in range(E)]
-        slot_scales = [sbuf("slot_scales%d" % e, [C], U8) for e in range(E)]
+        picked = [sbuf("picked%d" % g, [2, (hi - lo) * C], U32) for g, (lo, hi) in enumerate(GROUPS)]
+        slots = [picked[2][:, 1].rearrange("p (c u) -> p c u", u=2), sbuf("slots1", [C, 2], U32)[:], sbuf("slots2", [2 * C, 2], U32)[:]]
+        group_codes = [sbuf("group_codes%d" % g, [(hi - lo) * C], U32) for g, (lo, hi) in enumerate(GROUPS)]
+        group_scales = [sbuf("group_scales%d" % g, [(hi - lo) * C], U8) for g, (lo, hi) in enumerate(GROUPS)]
+        slot_codes = [group_codes[g][:, (e - lo) * C : (e - lo + 1) * C] for g, (lo, hi) in enumerate(GROUPS) for e in range(lo, hi)]
+        slot_scales = [group_scales[g][:, (e - lo) * C : (e - lo + 1) * C] for g, (lo, hi) in enumerate(GROUPS) for e in range(lo, hi)]
         gate = [sbuf("gate%d" % n, [2, P, 2], F32) for n in range(UNITS)]
         h = [sbuf("h%d" % n, [2, P, 2], BF16) for n in range(UNITS - 1)]
         h_last = [sbuf("h_last%d" % u, [P, 2], BF16) for u in range(2)]
@@ -78,15 +81,18 @@ def tile_moe_eps_glu_silu_kernel(tc, xT, w1_words, w1_scales, w3_words, w3_scale
 
         def gather_pairs(g, u):
             window = x_pairs[u][:].rearrange("p t c -> p (t c)").bitcast(U32)
-            lo, hi = ((0, 1), (1, E))[g]
+            lo, hi = GROUPS[g]
             nc.vector.tensor_copy(picked[g][:, u], window.indirect(offsets[:, lo * C // 16 : hi * C // 16]))
 
         def weave(g):
-            nc.scalar.copy(slots[g][:], picked[g][:].rearrange("p u c -> p c u"))
+            woven = picked[g][:].rearrange("p u c -> p c u")
+            if g < 2:
+                nc.scalar.copy(slots[g], woven)
+            else:
+                nc.vector.tensor_copy(slots[g].bitcast(I32), woven.bitcast(I32))
 
-        def quantize_slots(e):
-            words = slots[0][:] if e == 0 else slots[1][:, (e - 1) * C : e * C]
-            nc.vector.quantize_mx(out=slot_codes[e][:].bitcast(FP8X4), scales=slot_scales[e][:], in_=words.rearrange("p c u -> p (c u)").bitcast(BF16))
+        def quantize_slots(g):
+            nc.vector.quantize_mx(out=group_codes[g][:].bitcast(FP8X4), scales=group_scales[g][:], in_=slots[g].rearrange("p c u -> p (c u)").bitcast(BF16))
 
         s1 = sbuf("s1", [E, H], U8)
         s3 = sbuf("s3", [E, H], U8)
@@ -118,27 +124,38 @@ def tile_moe_eps_glu_silu_kernel(tc, xT, w1_words, w1_scales, w3_words, w3_scale
         nc.vector.quantize_mx(out=warm_codes[:].bitcast(FP8X4), scales=warm_scales[:], in_=x_pairs[0][:, : 2 * WARM_COLUMNS].rearrange("p t c -> p (t c)"))
         for width in WARM_WIDTHS:
             nc.tensor.matmul_mx(bank[7][:, :width], lhsT=warm_codes[:, :C].bitcast(FP8X4), lhsT_scale=warm_scales[:, :C], rhs=w1[0][:, : 2 * width].bitcast(FP4X4), rhs_scale=warm_scales[:, :width], start=True, stop=True)
-        for g in range(2):
+        for g in range(len(GROUPS)):
             gather_pairs(g, 0)
         round_pairs(raw[1], x_pairs[1][:], LAST_SHARE)
         for g in range(2):
             gather_pairs(g, 1)
             weave(g)
-        for e in range(E):
-            quantize_slots(e)
+        quantize_slots(0)
+        gather_pairs(2, 1)
+        weave(2)
+        quantize_slots(1)
+        quantize_slots(2)
+
+        load_scales(s2[0], w2_scales[:, :, :, : N // 2])
+        w2_whole = [sbuf("w2_whole%d" % e, [HP, 2 * N], U8) for e in range(2)]
+        for e in range(2):
+            load_words(w2_whole[e][:], w2_words[e].rearrange("s p n -> p s n"))
+        w2_half = [sbuf("w2_half%d" % half, [2 * HP, N], U8) for half in range(2)]
+        for half in range(2):
+            if half:
+                load_scales(s2[1], w2_scales[:, :, :, N // 2 :])
+            load_words(w2_half[half][:], w2_words[2:].rearrange("e s p n -> p (e s) n")[:, :, half * N : (half + 1) * N])
 
         def second_words(e, j, s):
             if e < 2:
                 return w2_whole[e][:, s, 2 * P * j : 2 * P * (j + 1)]
-            if j < 2:
-                return w2_upper[:, (e - 2) * HP + s, 2 * P * j : 2 * P * (j + 1)]
-            return w2_tile[j - 2][:, (e - 2) * HP + s]
+            return w2_half[j // 2][:, (e - 2) * HP + s, 2 * P * (j % 2) : 2 * P * (j % 2 + 1)]
 
         def product(acc, e, s, words, plane):
             nc.tensor.matmul_mx(
                 acc[:],
-                lhsT=slot_codes[e][:].bitcast(FP8X4),
-                lhsT_scale=slot_scales[e][:],
+                lhsT=slot_codes[e].bitcast(FP8X4),
+                lhsT_scale=slot_scales[e],
                 rhs=words[e][:, 2 * PASS * s : 2 * PASS * (s + 1)].bitcast(FP4X4),
                 rhs_scale=plane[:, e, PASS * s : PASS * (s + 1)],
                 start=True,
@@ -177,7 +194,7 @@ def tile_moe_eps_glu_silu_kernel(tc, xT, w1_words, w1_scales, w3_words, w3_scale
 
         a_bank = [bank[i] for i in (0, 1, 4, 5, 0, 1, 4, 5)]
         b_bank = [bank[i] for i in (2, 3, 6, 7, 2, 3, 6, 7)]
-        turn_bank = [bank[i] for i in (4, 5, 2)]
+        turn_bank = [bank[i] for i in (4, 5, 6)]
         last_turn_bank = [bank[i] for i in (3, 1)]
         early_bank = [bank[i] for i in (0, 6)]
         late_bank = [bank[i] for i in (7, 4, 5, 2)]
@@ -222,23 +239,9 @@ def tile_moe_eps_glu_silu_kernel(tc, xT, w1_words, w1_scales, w3_words, w3_scale
         for u in range(2):
             nc.scalar.activation(gate[n][:, u], by_pairs(a_bank[n])[:, u], ACT.Silu)
             nc.vector.tensor_tensor(h_last[u][:], by_pairs(b_bank[n])[:, u], gate[n][:, u], MULT)
-        load_scales(s2[0], w2_scales[:, :, :, : N // 2])
-        w2_whole = [sbuf("w2_whole0", [HP, 2 * N], U8, tag="w1_2"), sbuf("w2_whole1", [HP, 2 * N], U8)]
-        for e in range(2):
-            load_words(w2_whole[e][:], w2_words[e].rearrange("s p n -> p s n"))
-        late_rows = w2_words[2:].rearrange("e s p n -> p (e s) n")
-        w2_upper = sbuf("w2_upper", [2 * HP, N], U8)
-        load_words(w2_upper[:], late_rows[:, :, :N])
-        load_scales(s2[1], w2_scales[:, :, :, N // 2 :])
-        w2_tile = [sbuf("w2_tile2", [2 * HP, 2 * P], U8, tag="gate%d" % (UNITS - 1)), sbuf("w2_tile3", [2 * HP, 2 * P], U8)]
-        for j in range(2, NT):
-            load_words(w2_tile[j - 2][:], late_rows[:, :, 2 * P * j : 2 * P * (j + 1)])
-
         for e in range(LAST):
             turn_expert(e)
             unload_expert(e, e != 1)
-        for s in range(HP):
-            product(b_bank[n - 1], LAST, s, w1, s1)
         for u in range(2):
             turn(h[n - 1][:, u], last_turn_bank[0], 0, u)
         for u in range(2):

@@ -38,7 +38,7 @@ def tile_moe_eps_glu_silu_kernel(tc, xT, w1_words, w1_scales, w3_words, w3_scale
         psum = ctx.enter_context(tc.psum_pool(name="psum", bufs=1))
 
         def sbuf(name, shape, dtype, tag=None):
-            return keep.tile([P] + shape, dtype, name=name, tag=tag or name, align_bytes=64)
+            return keep.tile([P] + shape, dtype, name=name, tag=tag or name, align_bytes=256)
 
         offsets = keep.tile([P, E * C // 16], U16, name="offsets")
         x_pairs = [sbuf("x_pairs%d" % u, [T, 2], BF16) for u in range(2)]

@@ -24,6 +24,7 @@ NT = N // P
 U = C // R
 UNITS = E * HP
 LAST = E - 1
+SHIFT = 128
 GROUPS = ((0, 1), (1, 2), (2, 4))
 FIRST_SHARE = 576
 LAST_SHARE = 672
@@ -40,23 +41,27 @@ def tile_moe_eps_glu_silu_kernel(tc, xT, w1_words, w1_scales, w3_words, w3_scale
         def sbuf(name, shape, dtype, tag=None):
             return keep.tile([P] + shape, dtype, name=name, tag=tag or name, align_bytes=256)
 
+        def shifted(name, passes, columns, dtype, size):
+            lead = SHIFT // size
+            return sbuf(name, [lead + passes * columns], dtype)[:, lead:].rearrange("p (s c) -> p s c", s=passes)
+
         offsets = keep.tile([P, E * C // 16], U16, name="offsets")
         x_pairs = [sbuf("x_pairs%d" % u, [T, 2], BF16) for u in range(2)]
         picked = [sbuf("picked%d" % g, [2, (hi - lo) * C], U32) for g, (lo, hi) in enumerate(GROUPS)]
         slots = [picked[2][:, 1].rearrange("p (c u) -> p c u", u=2), sbuf("slots1", [C, 2], U32)[:], sbuf("slots2", [2 * C, 2], U32)[:]]
-        group_codes = [sbuf("group_codes%d" % g, [(hi - lo) * C], U32) for g, (lo, hi) in enumerate(GROUPS)]
-        group_scales = [sbuf("group_scales%d" % g, [(hi - lo) * C], U8) for g, (lo, hi) in enumerate(GROUPS)]
+        group_codes = [shifted("group_codes%d" % g, 1, (hi - lo) * C, U32, 4)[:, 0] for g, (lo, hi) in enumerate(GROUPS)]
+        group_scales = [shifted("group_scales%d" % g, 1, (hi - lo) * C, U8, 1)[:, 0] for g, (lo, hi) in enumerate(GROUPS)]
         slot_codes = [group_codes[g][:, (e - lo) * C : (e - lo + 1) * C] for g, (lo, hi) in enumerate(GROUPS) for e in range(lo, hi)]
         slot_scales = [group_scales[g][:, (e - lo) * C : (e - lo + 1) * C] for g, (lo, hi) in enumerate(GROUPS) for e in range(lo, hi)]
         gate = [sbuf("gate%d" % n, [2, P, 2], F32) for n in range(UNITS)]
         h = [sbuf("h%d" % n, [2, P, 2], BF16) for n in range(UNITS - 1)]
         h_last = [sbuf("h_last%d" % u, [P, 2], BF16) for u in range(2)]
         h_turned = [sbuf("h_turned%d" % e, [HP, C, 2], F32) for e in range(LAST)]
-        h_codes = [sbuf("h_codes%d" % e, [HP, C], U32) for e in range(LAST)]
-        h_scales = [sbuf("h_scales%d" % e, [HP, C], U8) for e in range(LAST)]
+        h_codes = [shifted("h_codes%d" % e, HP, C, U32, 4) for e in range(LAST)]
+        h_scales = [shifted("h_scales%d" % e, HP, C, U8, 1) for e in range(LAST)]
         last_turned = [sbuf("last_turned%d" % s, [1, C, 2], F32) for s in range(HP)]
-        last_codes = [sbuf("last_codes%d" % s, [1, C], U32) for s in range(HP)]
-        last_scales = [sbuf("last_scales%d" % s, [1, C], U8) for s in range(HP)]
+        last_codes = [shifted("last_codes%d" % s, 1, C, U32, 4) for s in range(HP)]
+        last_scales = [shifted("last_scales%d" % s, 1, C, U8, 1) for s in range(HP)]
         ident = sbuf("ident", [P], F32)
         warm_in = sbuf("warm_in", [1], F32)
         warm_out = sbuf("warm_out", [1], F32)

@@ -71,10 +71,13 @@ def tile_moe_eps_glu_silu_kernel(tc, xT, w1_words, w1_scales, w3_words, w3_scale
         def clear(plane):
             nc.vector.memset(plane[:].rearrange("p e b -> p (e b)").bitcast(I32), 0)
 
-        def load_scales(plane, scales):
+        def load_scales(plane, scales, cut=0):
             rows = scales.rearrange("e s (q r) n -> r q (e s) n", r=4)
+            count = plane.shape[1]
             for r in range(4):
-                nc.sync.dma_start(plane[r:P:32].bitcast(I32), rows[r].bitcast(I32))
+                step = count // 2 if r >= 4 - cut else count
+                for lo in range(0, count, step):
+                    nc.sync.dma_start(plane[r:P:32, lo : lo + step].bitcast(I32), rows[r][:, lo : lo + step].bitcast(I32))
 
         def load_words(view, words):
             nc.sync.dma_start(view.bitcast(I32), words.bitcast(I32))
@@ -117,7 +120,7 @@ def tile_moe_eps_glu_silu_kernel(tc, xT, w1_words, w1_scales, w3_words, w3_scale
         w3 = [sbuf("w3_%d" % e, [2 * H], U8) for e in range(E)]
         load_words(w1[0][:], w1_words[0, 0])
         load_scales(s1, w1_scales)
-        load_scales(s3, w3_scales)
+        load_scales(s3, w3_scales, cut=2)
         load_words(w3[0][:], w3_words[0, 0])
         for e in range(1, E):
             load_words(w1[e][:], w1_words[e, 0])
@@ -141,20 +144,22 @@ def tile_moe_eps_glu_silu_kernel(tc, xT, w1_words, w1_scales, w3_words, w3_scale
         quantize_slots(1)
         quantize_slots(2)
 
-        load_scales(s2[0], w2_scales[:, :, :, : N // 2])
+        load_scales(s2[0], w2_scales[:, :, :, : N // 2], cut=1)
         w2_whole = [sbuf("w2_whole%d" % e, [HP, 2 * N], U8) for e in range(2)]
         for e in range(2):
             load_words(w2_whole[e][:], w2_words[e].rearrange("s p n -> p s n"))
-        w2_half = [sbuf("w2_half%d" % half, [2 * HP, N], U8) for half in range(2)]
-        for half in range(2):
-            if half:
-                load_scales(s2[1], w2_scales[:, :, :, N // 2 :])
-            load_words(w2_half[half][:], w2_words[2:].rearrange("e s p n -> p (e s) n")[:, :, half * N : (half + 1) * N])
+        w2_upper = sbuf("w2_upper", [2 * HP, N], U8)
+        load_words(w2_upper[:], w2_words[2:].rearrange("e s p n -> p (e s) n")[:, :, :N])
+        load_scales(s2[1], w2_scales[:, :, :, N // 2 :], cut=2)
+        w2_lower = sbuf("w2_lower", [2 * HP, N], U8)
+        load_words(w2_lower[:], w2_words[2:].rearrange("e s p n -> p (e s) n")[:, :, N:])
 
         def second_words(e, j, s):
             if e < 2:
                 return w2_whole[e][:, s, 2 * P * j : 2 * P * (j + 1)]
-            return w2_half[j // 2][:, (e - 2) * HP + s, 2 * P * (j % 2) : 2 * P * (j % 2 + 1)]
+            if j < 2:
+                return w2_upper[:, (e - 2) * HP + s, 2 * P * j : 2 * P * (j + 1)]
+            return w2_lower[:, (e - 2) * HP + s, 2 * P * (j - 2) : 2 * P * (j - 1)]
 
         def product(acc, e, s, words, plane):
             nc.tensor.matmul_mx(

@@ -120,7 +120,7 @@ def tile_moe_eps_glu_silu_kernel(tc, xT, w1_words, w1_scales, w3_words, w3_scale
         w3 = [sbuf("w3_%d" % e, [2 * H], U8) for e in range(E)]
         load_words(w1[0][:], w1_words[0, 0])
         load_scales(s1, w1_scales)
-        load_scales(s3, w3_scales, cut=2)
+        load_scales(s3, w3_scales)
         load_words(w3[0][:], w3_words[0, 0])
         for e in range(1, E):
             load_words(w1[e][:], w1_words[e, 0])

@@ -151,15 +151,16 @@ def tile_moe_eps_glu_silu_kernel(tc, xT, w1_words, w1_scales, w3_words, w3_scale
         w2_upper = sbuf("w2_upper", [2 * HP, N], U8)
         load_words(w2_upper[:], w2_words[2:].rearrange("e s p n -> p (e s) n")[:, :, :N])
         load_scales(s2[1], w2_scales[:, :, :, N // 2 :], cut=2)
-        w2_lower = sbuf("w2_lower", [2 * HP, N], U8)
-        load_words(w2_lower[:], w2_words[2:].rearrange("e s p n -> p (e s) n")[:, :, N:])
+        w2_lower = [sbuf("w2_lower%d" % j, [2 * HP, 2 * P], U8) for j in range(2, NT)]
+        for j in range(2, NT):
+            load_words(w2_lower[j - 2][:], w2_words[2:].rearrange("e s p n -> p (e s) n")[:, :, 2 * P * j : 2 * P * (j + 1)])
 
         def second_words(e, j, s):
             if e < 2:
                 return w2_whole[e][:, s, 2 * P * j : 2 * P * (j + 1)]
             if j < 2:
                 return w2_upper[:, (e - 2) * HP + s, 2 * P * j : 2 * P * (j + 1)]
-            return w2_lower[:, (e - 2) * HP + s, 2 * P * (j - 2) : 2 * P * (j - 1)]
+            return w2_lower[j - 2][:, (e - 2) * HP + s]
 
         def product(acc, e, s, words, plane):
             nc.tensor.matmul_mx(

@@ -150,9 +150,15 @@ def tile_moe_eps_glu_silu_kernel(tc, xT, w1_words, w1_scales, w3_words, w3_scale
             load_words(w2_whole[e][:], w2_words[e].rearrange("s p n -> p s n"))
         w2_upper = sbuf("w2_upper", [2 * HP, N], U8)
         load_words(w2_upper[:], w2_words[2:].rearrange("e s p n -> p (e s) n")[:, :, :N])
-        load_scales(s2[1], w2_scales[:, :, :, N // 2 :], cut=2)
+        lower_rows = w2_scales[:, :, :, N // 2 :].rearrange("e s (q r) n -> r q (e s) n", r=4)
+        for r in range(3):
+            for lo in range(0, E * HP, E * HP // 2 if r == 2 else E * HP):
+                hi = lo + (E * HP // 2 if r == 2 else E * HP)
+                nc.sync.dma_start(s2[1][r:P:32, lo:hi].bitcast(I32), lower_rows[r][:, lo:hi].bitcast(I32))
         w2_lower = [sbuf("w2_lower%d" % j, [2 * HP, 2 * P], U8) for j in range(2, NT)]
         for j in range(2, NT):
+            cols = slice(P * (j - 2), P * (j - 1))
+            nc.sync.dma_start(s2[1][3:P:32, :, cols].bitcast(I32), lower_rows[3][:, :, cols].bitcast(I32))
             load_words(w2_lower[j - 2][:], w2_words[2:].rearrange("e s p n -> p (e s) n")[:, :, 2 * P * j : 2 * P * (j + 1)])
 
         def second_words(e, j, s):
@@ -207,7 +213,7 @@ def tile_moe_eps_glu_silu_kernel(tc, xT, w1_words, w1_scales, w3_words, w3_scale
         b_bank = [bank[i] for i in (2, 3, 6, 7, 2, 3, 6, 7)]
         turn_bank = [bank[i] for i in (4, 5, 6)]
         last_turn_bank = [bank[i] for i in (3, 1)]
-        early_bank = [bank[i] for i in (0, 6)]
+        early_bank = [bank[i] for i in (0, 6, 1)]
         late_bank = [bank[i] for i in (7, 4, 5, 2)]
 
         def firsts(e):
@@ -264,18 +270,32 @@ def tile_moe_eps_glu_silu_kernel(tc, xT, w1_words, w1_scales, w3_words, w3_scale
         quantize_expert(2)
         for s in range(HP):
             quantize_hidden(last_turned[s], last_codes[s], last_scales[s])
-        for half in range(2):
-            tiles = (2 * half, 2 * half + 1)
+
+        def early(acc, j):
             for e in range(2):
-                for j in tiles:
-                    for s in range(HP):
-                        second(early_bank[half][:, (2 * (j % 2) + e) * C : (2 * (j % 2) + e + 1) * C], e, j, s, h_codes[e][:, s], h_scales[e][:, s])
-            for j in tiles:
-                nc.scalar.copy(staged[:, j, :, :2, :], early_bank[half][:, 2 * (j % 2) * C : 2 * (j % 2 + 1) * C].rearrange("p (e m u) -> p m e u", e=2, u=U))
-            for j in tiles:
                 for s in range(HP):
-                    second(late_bank[j][:, :C], 2, j, s, h_codes[2][:, s], h_scales[2][:, s])
+                    second(acc[:, e * C : (e + 1) * C], e, j, s, h_codes[e][:, s], h_scales[e][:, s])
+
+        def late(j):
+            for s in range(HP):
+                second(late_bank[j][:, :C], 2, j, s, h_codes[2][:, s], h_scales[2][:, s])
+            for s in range(HP):
+                second(late_bank[j][:, C : 2 * C], LAST, j, s, last_codes[s][:, 0], last_scales[s][:, 0])
+            nc.vector.tensor_copy(staged[:, j, :, 2:, :], late_bank[j][:, : 2 * C].rearrange("p (e m u) -> p m e u", e=2, u=U))
+            nc.sync.dma_start(out[P * j : P * (j + 1), :], staged[:, j].rearrange("p m e u -> p (m e u)"))
+
+        def unload_early(acc, j):
+            nc.scalar.copy(staged[:, j, :, :2, :], acc.rearrange("p (e m u) -> p m e u", e=2, u=U))
+
+        for e in range(2):
+            for j in range(2):
                 for s in range(HP):
-                    second(late_bank[j][:, C : 2 * C], LAST, j, s, last_codes[s][:, 0], last_scales[s][:, 0])
-                nc.vector.tensor_copy(staged[:, j, :, 2:, :], late_bank[j][:, : 2 * C].rearrange("p (e m u) -> p m e u", e=2, u=U))
-                nc.sync.dma_start(out[P * j : P * (j + 1), :], staged[:, j].rearrange("p m e u -> p (m e u)"))
+                    second(early_bank[0][:, (2 * j + e) * C : (2 * j + e + 1) * C], e, j, s, h_codes[e][:, s], h_scales[e][:, s])
+        for j in range(2):
+            unload_early(early_bank[0][:, 2 * j * C : 2 * (j + 1) * C], j)
+        for j in range(2):
+            late(j)
+        for j in range(2, NT):
+            early(early_bank[j - 1][:, : 2 * C], j)
+            unload_early(early_bank[j - 1][:, : 2 * C], j)
+            late(j)

@@ -213,8 +213,6 @@ def tile_moe_eps_glu_silu_kernel(tc, xT, w1_words, w1_scales, w3_words, w3_scale
         b_bank = [bank[i] for i in (2, 3, 6, 7, 2, 3, 6, 7)]
         turn_bank = [bank[i] for i in (4, 5, 6)]
         last_turn_bank = [bank[i] for i in (3, 1)]
-        early_bank = [bank[i] for i in (0, 6, 1)]
-        late_bank = [bank[i] for i in (7, 4, 5, 2)]
 
         def firsts(e):
             for s in range(HP):
@@ -271,31 +269,35 @@ def tile_moe_eps_glu_silu_kernel(tc, xT, w1_words, w1_scales, w3_words, w3_scale
         for s in range(HP):
             quantize_hidden(last_turned[s], last_codes[s], last_scales[s])
 
-        def early(acc, j):
-            for e in range(2):
-                for s in range(HP):
-                    second(acc[:, e * C : (e + 1) * C], e, j, s, h_codes[e][:, s], h_scales[e][:, s])
+        def passes(acc, e, j):
+            for s in range(HP):
+                if e < LAST:
+                    second(acc, e, j, s, h_codes[e][:, s], h_scales[e][:, s])
+                else:
+                    second(acc, e, j, s, last_codes[s][:, 0], last_scales[s][:, 0])
 
-        def late(j):
-            for s in range(HP):
-                second(late_bank[j][:, :C], 2, j, s, h_codes[2][:, s], h_scales[2][:, s])
-            for s in range(HP):
-                second(late_bank[j][:, C : 2 * C], LAST, j, s, last_codes[s][:, 0], last_scales[s][:, 0])
-            nc.vector.tensor_copy(staged[:, j, :, 2:, :], late_bank[j][:, : 2 * C].rearrange("p (e m u) -> p m e u", e=2, u=U))
+        def results(acc, on_scalar, j, lo, hi):
+            for e in range(lo, hi):
+                passes(acc[:, (e - lo) * C : (e - lo + 1) * C], e, j)
+            copy_on(on_scalar, staged[:, j, :, lo:hi, :], acc[:, : (hi - lo) * C].rearrange("p (e m u) -> p m e u", e=hi - lo, u=U))
+
+        def store(j):
             nc.sync.dma_start(out[P * j : P * (j + 1), :], staged[:, j].rearrange("p m e u -> p (m e u)"))
-
-        def unload_early(acc, j):
-            nc.scalar.copy(staged[:, j, :, :2, :], acc.rearrange("p (e m u) -> p m e u", e=2, u=U))
 
         for e in range(2):
             for j in range(2):
-                for s in range(HP):
-                    second(early_bank[0][:, (2 * j + e) * C : (2 * j + e + 1) * C], e, j, s, h_codes[e][:, s], h_scales[e][:, s])
+                passes(bank[0][:, (2 * j + e) * C : (2 * j + e + 1) * C], e, j)
         for j in range(2):
-            unload_early(early_bank[0][:, 2 * j * C : 2 * (j + 1) * C], j)
-        for j in range(2):
-            late(j)
-        for j in range(2, NT):
-            early(early_bank[j - 1][:, : 2 * C], j)
-            unload_early(early_bank[j - 1][:, : 2 * C], j)
-            late(j)
+            nc.scalar.copy(staged[:, j, :, :2, :], bank[0][:, 2 * j * C : 2 * (j + 1) * C].rearrange("p (e m u) -> p m e u", e=2, u=U))
+        results(bank[2], True, 0, 2, LAST)
+        results(bank[7], False, 0, LAST, E)
+        store(0)
+        results(bank[4], False, 1, 2, E)
+        store(1)
+        results(bank[6], True, 2, 0, 2)
+        results(bank[5], False, 2, 2, E)
+        store(2)
+        results(bank[1], True, 3, 0, 2)
+        results(bank[3], True, 3, 2, LAST)
+        results(bank[7], False, 3, LAST, E)
+        store(3)

from contextlib import ExitStack

import concourse.mybir as mybir
from concourse.masks import make_identity

K, T, E, C, H, N, R = 512, 1024, 4, 128, 1024, 512, 4
FLOPS = 2 * E * C * (2 * K * H + H * N)

F32 = mybir.dt.float32
BF16 = mybir.dt.bfloat16
I32 = mybir.dt.int32
U32 = mybir.dt.uint32
U16 = mybir.dt.uint16
U8 = mybir.dt.uint8
FP8X4 = mybir.dt.float8_e4m3fn_x4
FP4X4 = mybir.dt.float4_e2m1fn_x4
ACT = mybir.ActivationFunctionType
MULT = mybir.AluOpType.mult

P = 128
PASS = 512
HP = H // PASS
NT = N // P
U = C // R
UNITS = E * HP
LAST = E - 1
SHIFT = 128
GROUPS = ((0, 1), (1, 2), (2, 4))
FIRST_SHARE = 576
LAST_SHARE = 672
WARM_WIDTHS = (256, 256, 256, 256, 128, 64)
WARM_COLUMNS = 256


def tile_moe_eps_glu_silu_kernel(tc, xT, w1_words, w1_scales, w3_words, w3_scales, w2_words, w2_scales, offs, out):
    nc = tc.nc
    with ExitStack() as ctx:
        keep = ctx.enter_context(tc.tile_pool(name="keep", bufs=1))
        psum = ctx.enter_context(tc.psum_pool(name="psum", bufs=1))

        def sbuf(name, shape, dtype, tag=None):
            return keep.tile([P] + shape, dtype, name=name, tag=tag or name, align_bytes=256)

        def shifted(name, passes, columns, dtype, size):
            lead = SHIFT // size
            return sbuf(name, [lead + passes * columns], dtype)[:, lead:].rearrange("p (s c) -> p s c", s=passes)

        offsets = keep.tile([P, E * C // 16], U16, name="offsets")
        x_pairs = [sbuf("x_pairs%d" % u, [T, 2], BF16) for u in range(2)]
        picked = [sbuf("picked%d" % g, [2, (hi - lo) * C], U32) for g, (lo, hi) in enumerate(GROUPS)]
        slots = [picked[2][:, 1].rearrange("p (c u) -> p c u", u=2), sbuf("slots1", [C, 2], U32)[:], sbuf("slots2", [2 * C, 2], U32)[:]]
        group_codes = [shifted("group_codes%d" % g, 1, (hi - lo) * C, U32, 4)[:, 0] for g, (lo, hi) in enumerate(GROUPS)]
        group_scales = [shifted("group_scales%d" % g, 1, (hi - lo) * C, U8, 1)[:, 0] for g, (lo, hi) in enumerate(GROUPS)]
        slot_codes = [group_codes[g][:, (e - lo) * C : (e - lo + 1) * C] for g, (lo, hi) in enumerate(GROUPS) for e in range(lo, hi)]
        slot_scales = [group_scales[g][:, (e - lo) * C : (e - lo + 1) * C] for g, (lo, hi) in enumerate(GROUPS) for e in range(lo, hi)]
        gate = [sbuf("gate%d" % n, [2, P, 2], F32) for n in range(UNITS)]
        h = [sbuf("h%d" % n, [2, P, 2], BF16) for n in range(UNITS - 1)]
        h_last = [sbuf("h_last%d" % u, [P, 2], BF16) for u in range(2)]
        h_turned = [sbuf("h_turned%d" % e, [HP, C, 2], F32) for e in range(LAST)]
        h_codes = [shifted("h_codes%d" % e, HP, C, U32, 4) for e in range(LAST)]
        h_scales = [shifted("h_scales%d" % e, HP, C, U8, 1) for e in range(LAST)]
        last_turned = [sbuf("last_turned%d" % s, [1, C, 2], F32) for s in range(HP)]
        last_codes = [shifted("last_codes%d" % s, 1, C, U32, 4) for s in range(HP)]
        last_scales = [shifted("last_scales%d" % s, 1, C, U8, 1) for s in range(HP)]
        ident = sbuf("ident", [P], F32)
        warm_in = sbuf("warm_in", [1], F32)
        warm_out = sbuf("warm_out", [1], F32)
        staged = sbuf("staged", [NT, R, E, U], F32)
        bank = [psum.tile([P, PASS], F32, name="bank%d" % i) for i in range(8)]

        def clear(plane):
            nc.vector.memset(plane[:].rearrange("p e b -> p (e b)").bitcast(I32), 0)

        def load_scales(plane, scales, cut=0):
            rows = scales.rearrange("e s (q r) n -> r q (e s) n", r=4)
            count = plane.shape[1]
            for r in range(4):
                step = count // 2 if r >= 4 - cut else count
                for lo in range(0, count, step):
                    nc.sync.dma_start(plane[r:P:32, lo : lo + step].bitcast(I32), rows[r][:, lo : lo + step].bitcast(I32))

        def load_words(view, words):
            nc.sync.dma_start(view.bitcast(I32), words.bitcast(I32))

        def round_pairs(rows, pairs, on_vector):
            src = rows[:].rearrange("p c t -> p t c")
            nc.vector.tensor_copy(pairs[:, :on_vector], src[:, :on_vector])
            nc.scalar.activation(pairs[:, on_vector:], src[:, on_vector:], ACT.Copy)

        def gather_pairs(g, u):
            window = x_pairs[u][:].rearrange("p t c -> p (t c)").bitcast(U32)
            lo, hi = GROUPS[g]
            nc.vector.tensor_copy(picked[g][:, u], window.indirect(offsets[:, lo * C // 16 : hi * C // 16]))

        def weave(g):
            woven = picked[g][:].rearrange("p u c -> p c u")
            if g < 2:
                nc.scalar.copy(slots[g], woven)
            else:
                nc.vector.tensor_copy(slots[g].bitcast(I32), woven.bitcast(I32))

        def quantize_slots(g):
            nc.vector.quantize_mx(out=group_codes[g][:].bitcast(FP8X4), scales=group_scales[g][:], in_=slots[g].rearrange("p c u -> p (c u)").bitcast(BF16))

        s1 = sbuf("s1", [E, H], U8)
        s3 = sbuf("s3", [E, H], U8)
        s2 = [sbuf("s2_%d" % half, [E * HP, N // 2], U8) for half in range(2)]
        nc.vector.memset(warm_in[:], 0.0)
        nc.scalar.activation(warm_out[:], warm_in[:], ACT.Silu)
        for plane in [s1, s3] + s2:
            clear(plane)
        make_identity(nc, ident[:])

        raw = [sbuf("raw%d" % u, [2, T], F32) for u in range(2)]
        row_pairs = xT.rearrange("(p u c) t -> u p c t", u=2, c=2)
        nc.sync.dma_start(raw[0][:], row_pairs[0])
        nc.sync.dma_start(offsets[:], offs)
        nc.sync.dma_start(raw[1][:], row_pairs[1])
        w1 = [sbuf("w1_%d" % e, [2 * H], U8) for e in range(E)]
        w3 = [sbuf("w3_%d" % e, [2 * H], U8) for e in range(E)]
        load_words(w1[0][:], w1_words[0, 0])
        load_scales(s1, w1_scales)
        load_scales(s3, w3_scales)
        load_words(w3[0][:], w3_words[0, 0])
        for e in range(1, E):
            load_words(w1[e][:], w1_words[e, 0])
            load_words(w3[e][:], w3_words[e, 0])

        round_pairs(raw[0], x_pairs[0][:], FIRST_SHARE)
        warm_codes = sbuf("warm_codes", [WARM_COLUMNS], U32)
        warm_scales = sbuf("warm_scales", [WARM_COLUMNS], U8)
        nc.vector.quantize_mx(out=warm_codes[:].bitcast(FP8X4), scales=warm_scales[:], in_=x_pairs[0][:, : 2 * WARM_COLUMNS].rearrange("p t c -> p (t c)"))
        for width in WARM_WIDTHS:
            nc.tensor.matmul_mx(bank[7][:, :width], lhsT=warm_codes[:, :C].bitcast(FP8X4), lhsT_scale=warm_scales[:, :C], rhs=w1[0][:, : 2 * width].bitcast(FP4X4), rhs_scale=warm_scales[:, :width], start=True, stop=True)
        for g in range(len(GROUPS)):
            gather_pairs(g, 0)
        round_pairs(raw[1], x_pairs[1][:], LAST_SHARE)
        for g in range(2):
            gather_pairs(g, 1)
            weave(g)
        quantize_slots(0)
        gather_pairs(2, 1)
        weave(2)
        quantize_slots(1)
        quantize_slots(2)

        load_scales(s2[0], w2_scales[:, :, :, : N // 2], cut=1)
        w2_whole = [sbuf("w2_whole%d" % e, [HP, 2 * N], U8) for e in range(2)]
        for e in range(2):
            load_words(w2_whole[e][:], w2_words[e].rearrange("s p n -> p s n"))
        w2_upper = sbuf("w2_upper", [2 * HP, N], U8)
        load_words(w2_upper[:], w2_words[2:].rearrange("e s p n -> p (e s) n")[:, :, :N])
        lower_rows = w2_scales[:, :, :, N // 2 :].rearrange("e s (q r) n -> r q (e s) n", r=4)
        for r in range(3):
            for lo in range(0, E * HP, E * HP // 2 if r == 2 else E * HP):
                hi = lo + (E * HP // 2 if r == 2 else E * HP)
                nc.sync.dma_start(s2[1][r:P:32, lo:hi].bitcast(I32), lower_rows[r][:, lo:hi].bitcast(I32))
        w2_lower = [sbuf("w2_lower%d" % j, [2 * HP, 2 * P], U8) for j in range(2, NT)]
        for j in range(2, NT):
            cols = slice(P * (j - 2), P * (j - 1))
            nc.sync.dma_start(s2[1][3:P:32, :, cols].bitcast(I32), lower_rows[3][:, :, cols].bitcast(I32))
            load_words(w2_lower[j - 2][:], w2_words[2:].rearrange("e s p n -> p (e s) n")[:, :, 2 * P * j : 2 * P * (j + 1)])

        def second_words(e, j, s):
            if e < 2:
                return w2_whole[e][:, s, 2 * P * j : 2 * P * (j + 1)]
            if j < 2:
                return w2_upper[:, (e - 2) * HP + s, 2 * P * j : 2 * P * (j + 1)]
            return w2_lower[j - 2][:, (e - 2) * HP + s]

        def product(acc, e, s, words, plane):
            nc.tensor.matmul_mx(
                acc[:],
                lhsT=slot_codes[e].bitcast(FP8X4),
                lhsT_scale=slot_scales[e],
                rhs=words[e][:, 2 * PASS * s : 2 * PASS * (s + 1)].bitcast(FP4X4),
                rhs_scale=plane[:, e, PASS * s : PASS * (s + 1)],
                start=True,
                stop=True,
            )

        def by_pairs(acc):
            return acc[:].rearrange("p (q u c) -> p u q c", u=2, c=2)

        def turn(pairs, into, s, u):
            nc.tensor.transpose(into[:, (2 * s + u) * C : (2 * s + u + 1) * C], pairs.rearrange("p q c -> p (q c)").bitcast(F32), ident[:])

        def quantize_hidden(turned, codes, scales):
            nc.vector.quantize_mx(
                out=codes[:].rearrange("p s c -> p (s c)").bitcast(FP8X4),
                scales=scales[:].rearrange("p s c -> p (s c)"),
                in_=turned[:].rearrange("p s c u -> p (s c u)").bitcast(BF16),
            )

        def second(acc, e, j, s, codes, scales):
            nc.tensor.matmul_mx(
                acc,
                lhsT=second_words(e, j, s).bitcast(FP4X4),
                lhsT_scale=s2[j // 2][:, e * HP + s, P * (j % 2) : P * (j % 2 + 1)],
                rhs=codes.bitcast(FP8X4),
                rhs_scale=scales,
                start=(s == 0),
                stop=(s == HP - 1),
            )

        def copy_on(on_scalar, dst, src):
            if on_scalar:
                nc.scalar.copy(dst, src)
            else:
                nc.vector.tensor_copy(dst, src)

        a_bank = [bank[i] for i in (0, 1, 4, 5, 0, 1, 4, 5)]
        b_bank = [bank[i] for i in (2, 3, 6, 7, 2, 3, 6, 7)]
        turn_bank = [bank[i] for i in (4, 5, 6)]
        last_turn_bank = [bank[i] for i in (3, 1)]

        def firsts(e):
            for s in range(HP):
                product(a_bank[HP * e + s], e, s, w1, s1)

        def thirds(e):
            for s in range(HP):
                product(b_bank[HP * e + s], e, s, w3, s3)

        def silu(n):
            nc.scalar.activation(gate[n][:], by_pairs(a_bank[n]), ACT.Silu)

        def gated(n):
            nc.vector.tensor_tensor(h[n][:], by_pairs(b_bank[n]), gate[n][:], MULT)

        def turn_expert(e):
            for s in range(HP):
                for u in range(2):
                    turn(h[HP * e + s][:, u], turn_bank[e], s, u)

        def unload_turned(on_scalar, source, lo, hi, turned):
            copy_on(on_scalar, turned[:], source[:].rearrange("p (s u c) -> p s c u", s=HP, u=2)[:, lo:hi])

        def unload_expert(e, on_scalar):
            unload_turned(on_scalar, turn_bank[e], 0, HP, h_turned[e])

        def quantize_expert(e):
            quantize_hidden(h_turned[e], h_codes[e], h_scales[e])

        n = UNITS - 1
        for e in range(E):
            firsts(e)
            thirds(e)
            silu(HP * e)
            gated(HP * e)
            if e < LAST:
                silu(HP * e + 1)
                gated(HP * e + 1)
        for u in range(2):
            nc.scalar.activation(gate[n][:, u], by_pairs(a_bank[n])[:, u], ACT.Silu)
            nc.vector.tensor_tensor(h_last[u][:], by_pairs(b_bank[n])[:, u], gate[n][:, u], MULT)
        for e in range(LAST):
            turn_expert(e)
            unload_expert(e, e != 1)
        for u in range(2):
            turn(h[n - 1][:, u], last_turn_bank[0], 0, u)
        for u in range(2):
            turn(h_last[u][:], last_turn_bank[1], 0, u)
        quantize_expert(0)
        unload_turned(True, last_turn_bank[0], 0, 1, last_turned[0])
        unload_turned(True, last_turn_bank[1], 0, 1, last_turned[1])
        quantize_expert(1)
        quantize_expert(2)
        for s in range(HP):
            quantize_hidden(last_turned[s], last_codes[s], last_scales[s])

        def passes(acc, e, j):
            for s in range(HP):
                if e < LAST:
                    second(acc, e, j, s, h_codes[e][:, s], h_scales[e][:, s])
                else:
                    second(acc, e, j, s, last_codes[s][:, 0], last_scales[s][:, 0])

        def results(acc, on_scalar, j, lo, hi):
            for e in range(lo, hi):
                passes(acc[:, (e - lo) * C : (e - lo + 1) * C], e, j)
            copy_on(on_scalar, staged[:, j, :, lo:hi, :], acc[:, : (hi - lo) * C].rearrange("p (e m u) -> p m e u", e=hi - lo, u=U))

        def store(j):
            nc.sync.dma_start(out[P * j : P * (j + 1), :], staged[:, j].rearrange("p m e u -> p (m e u)"))

        for e in range(2):
            for j in range(2):
                passes(bank[0][:, (2 * j + e) * C : (2 * j + e + 1) * C], e, j)
        for j in range(2):
            nc.scalar.copy(staged[:, j, :, :2, :], bank[0][:, 2 * j * C : 2 * (j + 1) * C].rearrange("p (e m u) -> p m e u", e=2, u=U))
        results(bank[2], True, 0, 2, LAST)
        results(bank[7], False, 0, LAST, E)
        store(0)
        results(bank[4], False, 1, 2, E)
        store(1)
        results(bank[6], True, 2, 0, 2)
        results(bank[5], False, 2, 2, E)
        store(2)
        results(bank[1], True, 3, 0, 2)
        results(bank[3], True, 3, 2, LAST)
        results(bank[7], False, 3, LAST, E)
        store(3)
